import numpy as np
import ml_dtypes


def mxq(x, axis, fmt="e4m3"):
    dtype, down = {"e4m3": (ml_dtypes.float8_e4m3fn, 7), "e5m2": (ml_dtypes.float8_e5m2, 14)}[fmt]
    v = np.moveaxis(np.asarray(x, np.float32).astype(ml_dtypes.bfloat16).astype(np.float64), axis, -1)
    blocks = v.reshape(v.shape[:-1] + (-1, 32))
    amax = np.abs(blocks).max(-1, keepdims=True)
    byte = np.maximum(np.where(amax > 0, np.frexp(amax)[1] - 1 + 127, 0) - down, 1)
    scale = np.exp2(byte - 127.0)
    codes = (blocks / scale).astype(np.float32).astype(dtype).astype(np.float64)
    return np.moveaxis((codes * scale).reshape(v.shape), -1, axis)


WIDE = False


def mx_kscale(k):
    if not WIDE:
        return np.ones(k)
    levels = np.array([10, -10, 5, -5, 0])
    if k % 512:
        return np.exp2(np.random.permutation(np.resize(levels, k // 32))).repeat(32)
    a = np.empty((k // 512, 16))
    for p in range(k // 512):
        a[p, :8] = np.random.permutation(np.resize(levels, 8))
        for g in range(8):
            far = levels[np.abs(levels - a[p, g]) >= 10]
            a[p, g + 8] = far[np.random.randint(len(far))]
    return np.exp2(a.ravel()).repeat(32)


def f64(x):
    return np.asarray(x).astype(np.float64)


def striped(idx):
    return np.tile(idx.reshape(-1, 16).T, (8, 1)).astype(np.uint16)


def unstriped(offs):
    return offs[:16].T.reshape(-1).astype(np.int64)


def pack_weight(w):
    k, n = w.shape
    w = f64(np.asarray(w, np.float32).astype(ml_dtypes.bfloat16)).reshape(k // 32, 32, n)
    amax = np.abs(w).max(1)
    byte = np.clip(np.where(amax > 0, np.frexp(amax)[1] - 1 + 127 - 7, 1), 1, 254)
    scaled = (w * np.exp2(127.0 - byte)[:, None, :]).reshape(k, n).astype(np.float32)
    words = np.ascontiguousarray(scaled.reshape(k // 512, 128, 4, n).transpose(0, 1, 3, 2)).astype(ml_dtypes.float8_e4m3fn).view(np.uint8)
    return words, np.ascontiguousarray(byte.astype(np.uint8).reshape(k // 512, 16, n))


def unpack_weight(words, scales):
    g, p, n, _ = words.shape
    vals = np.ascontiguousarray(words).view(ml_dtypes.float8_e4m3fn).astype(np.float64) * np.repeat(np.exp2(scales.astype(np.float64) - 127.0), 8, axis=1)[..., None]
    return vals.transpose(0, 1, 3, 2).reshape(g * 512, n)


E2M1 = np.array([0.0, 0.5, 1.0, 1.5, 2.0, 3.0, 4.0, 6.0, -0.0, -0.5, -1.0, -1.5, -2.0, -3.0, -4.0, -6.0])


def pack_fp4(w):
    k, n = w.shape
    w = f64(np.asarray(w, np.float32).astype(ml_dtypes.bfloat16)).reshape(k // 32, 32, n)
    amax = np.abs(w).max(1)
    mant, ex = np.frexp(amax / 6.0)
    byte = np.clip(np.where(amax > 0, np.where(mant > 0.5, ex, ex - 1) + 127, 1), 1, 254)
    scaled = (w * np.exp2(127.0 - byte)[:, None, :]).reshape(k, n).astype(np.float32)
    c = np.ascontiguousarray(scaled.reshape(k // 512, 128, 4, n).transpose(0, 1, 3, 2)).astype(ml_dtypes.float4_e2m1fn).view(np.uint8) & 0xF
    words = (c[..., 0::2] | (c[..., 1::2] << 4)).reshape(k // 512, 128, 2 * n)
    return np.ascontiguousarray(words), np.ascontiguousarray(byte.astype(np.uint8).reshape(k // 512, 16, n))


def unpack_fp4(words, scales):
    g, _, n = scales.shape
    words = np.ascontiguousarray(words).reshape(g, 128, n, 2)
    nib = np.empty((g, 128, n, 4), np.uint8)
    nib[..., 0::2] = words & 0xF
    nib[..., 1::2] = words >> 4
    vals = E2M1[nib] * np.repeat(np.exp2(scales.astype(np.float64) - 127.0), 8, axis=1)[..., None]
    return vals.transpose(0, 1, 3, 2).reshape(g * 512, n)


def silu(v):
    return v / (1.0 + np.exp(-np.maximum(v, -700.0)))


K, T, H, N = 512, 1024, 512, 128


def setup_inputs():
    n = np.random.standard_normal
    s = mx_kscale(K)[:, None]
    u = mx_kscale(H)
    packed_xT = pack_weight(n((K, T)) * s)
    packed_w2 = pack_fp4(n((H, N)) / np.sqrt(3 * H) / u[:, None])
    packed_w3 = pack_fp4(n((H, N)) / np.sqrt(3 * H) / u[:, None])
    packed_w4 = pack_fp4(n((H, N)) / np.sqrt(3 * H) / u[:, None])
    return {
        "x_words": packed_xT[0],
        "x_scales": packed_xT[1],
        "w1": (n((K, H)) / np.sqrt(K) / s * u).astype(np.float32),
        "w2_words": packed_w2[0],
        "w2_scales": packed_w2[1],
        "w3_words": packed_w3[0],
        "w3_scales": packed_w3[1],
        "w4_words": packed_w4[0],
        "w4_scales": packed_w4[1],
        "pos1": striped(np.random.permutation(T)),
        "pos2": striped(np.random.permutation(T)),
        "pos3": striped(np.random.permutation(T)),
    }


def reference(x_words, x_scales, w1, w2_words, w2_scales, w3_words, w3_scales, w4_words, w4_scales, pos1, pos2, pos3):
    xq = unpack_weight(x_words, x_scales)
    h = silu(mxq(f64(w1), 0, "e4m3").T @ xq)
    g0 = h[:, unstriped(pos1)]
    g1 = h[:, unstriped(pos2)]
    g2 = h[:, unstriped(pos3)]
    z1 = (g0 + g1 + g2) / 3
    z2 = np.maximum(np.maximum(g0, g1), g2)
    z3 = np.minimum(np.minimum(g0, g1), g2)
    return unpack_fp4(w2_words, w2_scales).T @ mxq(z1, 0, "e4m3") + unpack_fp4(w3_words, w3_scales).T @ mxq(z2, 0, "e4m3") + unpack_fp4(w4_words, w4_scales).T @ mxq(z3, 0, "e4m3")

@@ -1,0 +1,203 @@
+from contextlib import ExitStack
+
+import concourse.mybir as mybir
+from concourse.masks import make_identity
+
+K, T, H, N = 512, 1024, 512, 128
+D = 3
+FLOPS = 2 * K * H * T + D * 2 * H * N * T
+
+F32 = mybir.dt.float32
+BF16 = mybir.dt.bfloat16
+I32 = mybir.dt.int32
+U32 = mybir.dt.uint32
+U16 = mybir.dt.uint16
+U8 = mybir.dt.uint8
+FP8X4 = mybir.dt.float8_e4m3fn_x4
+FP4X4 = mybir.dt.float4_e2m1fn_x4
+ACT = mybir.ActivationFunctionType
+ALU = mybir.AluOpType
+
+P = 128
+PACK = 4
+BANK = 512
+CHUNKS = (256, 256, 256, 128, 128)
+GBUFS = 6
+
+
+def tile_picked_wpna_silu_l_kernel(
+    tc, x_words, x_scales, w1, w2_words, w2_scales, w3_words, w3_scales, w4_words, w4_scales, pos1, pos2, pos3, out
+):
+    nc = tc.nc
+    with ExitStack() as ctx:
+        keep = ctx.enter_context(tc.tile_pool(name="keep", bufs=1))
+        ring = ctx.enter_context(tc.tile_pool(name="ring", bufs=2))
+        psum = ctx.enter_context(tc.psum_pool(name="psum", bufs=2))
+
+        x_plane = keep.tile([P, T], U8, name="x_plane", align_bytes=64)
+        w_plane = keep.tile([P, D * N], U8, name="w_plane", align_bytes=64)
+        nc.vector.memset(x_plane[:].bitcast(I32), 0)
+        nc.vector.memset(w_plane[:].bitcast(I32), 0)
+        warm = keep.tile([P, 2], F32, name="warm")
+        nc.vector.memset(warm[:, 0:1], 0.0)
+
+        half = H // 2
+        w1_rows = w1.rearrange("(p j) c -> p j c", j=PACK)
+        w1_raw = []
+        for a in range(2):
+            raw = keep.tile([P, PACK, half], F32, name="w1_raw%d" % a)
+            nc.sync.dma_start(out=raw[:], in_=w1_rows[:, :, a * half : (a + 1) * half])
+            w1_raw.append(raw)
+        for q in range(4):
+            nc.scalar.dma_start(
+                out=x_plane[32 * q : 32 * q + 4, :].bitcast(I32), in_=x_scales[0][4 * q : 4 * q + 4, :].bitcast(I32)
+            )
+        nc.scalar.activation(warm[:, 1:2], warm[:, 0:1], ACT.Silu)
+        x_flat = x_words[0].rearrange("p n r -> p (n r)")
+        x_codes = []
+        for a in range(T // BANK):
+            codes = keep.tile([P, BANK], U32, name="x_codes%d" % a, align_bytes=64)
+            nc.sync.dma_start(
+                out=codes[:].bitcast(I32), in_=x_flat[:, PACK * BANK * a : PACK * BANK * (a + 1)].bitcast(I32)
+            )
+            x_codes.append(codes)
+        lists = []
+        for d, pos in enumerate((pos1, pos2, pos3)):
+            offsets = keep.tile([P, T // 16], U16, name="offsets%d" % d)
+            nc.sync.dma_start(offsets[:], pos)
+            lists.append(offsets)
+        w_codes = []
+        for s, (words, scales) in enumerate(((w2_words, w2_scales), (w3_words, w3_scales), (w4_words, w4_scales))):
+            codes = keep.tile([P, 2 * N], U8, name="w_codes%d" % s, align_bytes=64)
+            nc.sync.dma_start(out=codes[:].bitcast(I32), in_=words[0].bitcast(I32))
+            w_codes.append(codes)
+            for q in range(4):
+                nc.sync.dma_start(
+                    out=w_plane[32 * q : 32 * q + 4, s * N : (s + 1) * N].bitcast(I32),
+                    in_=scales[0][4 * q : 4 * q + 4, :].bitcast(I32),
+                )
+
+        ident = keep.tile([P, P], F32, name="ident")
+        make_identity(nc, ident[:])
+
+        w1_bf = keep.tile([P, PACK, P, PACK], BF16, name="w1_bf", align_bytes=64)
+        for a in range(2):
+            nc.vector.tensor_copy(
+                out=w1_bf[:, :, a * (P // 2) : (a + 1) * (P // 2), :].rearrange("p t m j -> p m j t"),
+                in_=w1_raw[a][:].rearrange("p j (m t) -> p m j t", t=PACK),
+            )
+        h = []
+        for t in range(PACK):
+            w1_codes = keep.tile([P, P], U32, name="w1_codes%d" % t, align_bytes=64)
+            w1_plane = keep.tile([P, P], U8, name="w1_plane%d" % t, align_bytes=64)
+            nc.vector.quantize_mx(
+                out=w1_codes[:].bitcast(FP8X4),
+                scales=w1_plane[:],
+                in_=w1_bf[:, t, :, :].rearrange("p m j -> p (m j)"),
+            )
+            h_t = keep.tile([P, T], F32, name="h%d" % t)
+            for a in range(T // BANK):
+                acc = psum.tile([P, BANK], F32, name="acc", tag="wide", bufs=4)
+                nc.tensor.matmul_mx(
+                    out=acc[:],
+                    lhsT=w1_codes[:].bitcast(FP8X4),
+                    lhsT_scale=w1_plane[:],
+                    rhs=x_codes[a][:].bitcast(FP8X4),
+                    rhs_scale=x_plane[:, a * BANK : (a + 1) * BANK],
+                    start=True,
+                    stop=True,
+                )
+                nc.scalar.activation(h_t[:, a * BANK : (a + 1) * BANK], acc[:], ACT.Silu)
+            h.append(h_t)
+
+        def fetch(v0, n, planes_first):
+            g = [ring.tile([P, PACK, n], F32, name="g", tag="g", bufs=GBUFS) for d in range(D)]
+            order = [(t, d) for t in range(PACK) for d in range(D)]
+            if not planes_first:
+                order = [(t, d) for d in range(D) for t in range(PACK)]
+            for t, d in order:
+                nc.vector.tensor_copy(g[d][:, t, :], h[t][:].indirect(lists[d][:, v0 // 16 : (v0 + n) // 16]))
+            rounded = []
+            for d in range(D):
+                gb = ring.tile([P, n, PACK], BF16, name="gb", tag="gb", bufs=9, align_bytes=64)
+                nc.scalar.copy(
+                    out=gb[:].rearrange("p (c i) t -> p c t i", i=4),
+                    in_=g[d][:].rearrange("p t (c i) -> p c t i", i=4),
+                )
+                rounded.append(gb)
+            blocks = n // P
+            back = psum.tile([P, blocks, 2, P], F32, name="back", tag="back", bufs=2)
+            for b in range(blocks):
+                sums = psum.tile([P, PACK, P], F32, name="sums", tag="wide", bufs=4)
+                for t in range(PACK):
+                    for d in range(D):
+                        nc.tensor.matmul(
+                            sums[:, t, :],
+                            lhsT=g[d][:, t, b * P : (b + 1) * P],
+                            rhs=ident[:],
+                            start=(d == 0),
+                            stop=(d == D - 1),
+                            is_transpose=True,
+                        )
+                turned = ring.tile([P, 2, P, 2], BF16, name="turned", tag="turned", bufs=3, align_bytes=64)
+                nc.scalar.activation(
+                    turned[:], sums[:].rearrange("v (u e) p -> v u p e", e=2), ACT.Copy, scale=1.0 / D
+                )
+                pairs = turned[:].rearrange("v u p e -> v u (p e)").bitcast(F32)
+                for u in range(2):
+                    nc.tensor.transpose(back[:, b, u, :], pairs[:, u, :], ident[:])
+            mean = ring.tile([P, n * PACK], BF16, name="mean", tag="mean", bufs=3, align_bytes=64)
+            nc.scalar.copy(
+                out=mean[:].bitcast(F32).rearrange("p (b v u) -> p b v u", b=blocks, u=2),
+                in_=back[:].rearrange("p b u v -> p b v u"),
+            )
+            return rounded, mean
+
+        def finish(v0, n, rounded, mean):
+            flat = [gb[:].rearrange("p c t -> p (c t)") for gb in rounded]
+            hi = ring.tile([P, n * PACK], BF16, name="hi", tag="hi", align_bytes=64)
+            lo = ring.tile([P, n * PACK], BF16, name="lo", tag="lo", align_bytes=64)
+            nc.vector.tensor_tensor(hi[:], flat[0], flat[1], ALU.max)
+            nc.vector.tensor_tensor(lo[:], flat[0], flat[1], ALU.min)
+            ends = ring.tile([P, 2, n * PACK], BF16, name="ends", tag="ends", align_bytes=64)
+            nc.vector.tensor_tensor(ends[:, 0, :], hi[:], flat[2], ALU.max)
+            nc.vector.tensor_tensor(ends[:, 1, :], lo[:], flat[2], ALU.min)
+            mean_codes = ring.tile([P, n], U32, name="mean_codes", tag="mean_codes", align_bytes=64)
+            mean_plane = ring.tile([P, n], U8, name="mean_plane", tag="mean_plane", align_bytes=64)
+            nc.vector.quantize_mx(out=mean_codes[:].bitcast(FP8X4), scales=mean_plane[:], in_=mean[:])
+            end_codes = ring.tile([P, 2 * n], U32, name="end_codes", tag="end_codes", align_bytes=64)
+            end_plane = ring.tile([P, 2 * n], U8, name="end_plane", tag="end_plane", align_bytes=64)
+            nc.vector.quantize_mx(
+                out=end_codes[:].bitcast(FP8X4), scales=end_plane[:], in_=ends[:].rearrange("p s c -> p (s c)")
+            )
+            total = psum.tile([P, n], F32, name="total", tag="total", bufs=2)
+            width = BANK if n == BANK else P
+            for c0 in range(0, n, width):
+                operands = [
+                    (mean_codes[:, c0 : c0 + width], mean_plane[:, c0 : c0 + width]),
+                    (end_codes[:, c0 : c0 + width], end_plane[:, c0 : c0 + width]),
+                    (end_codes[:, n + c0 : n + c0 + width], end_plane[:, n + c0 : n + c0 + width]),
+                ]
+                for s, (codes, plane) in enumerate(operands):
+                    nc.tensor.matmul_mx(
+                        out=total[:, c0 : c0 + width],
+                        lhsT=w_codes[s][:].bitcast(FP4X4),
+                        lhsT_scale=w_plane[:, s * N : (s + 1) * N],
+                        rhs=codes.bitcast(FP8X4),
+                        rhs_scale=plane,
+                        start=(s == 0),
+                        stop=(s == D - 1),
+                    )
+            result = ring.tile([P, n], F32, name="result", tag="result")
+            nc.scalar.copy(out=result[:], in_=total[:])
+            nc.sync.dma_start(out=out[:, v0 : v0 + n], in_=result[:])
+
+        pending = None
+        v0 = 0
+        for c, n in enumerate(CHUNKS):
+            rounded, mean = fetch(v0, n, c == 0)
+            if pending is not None:
+                finish(*pending)
+            pending = (v0, n, rounded, mean)
+            v0 = v0 + n
+        finish(*pending)

@@ -21,8 +21,10 @@ ALU = mybir.AluOpType
 P = 128
 PACK = 4
 BANK = 512
-CHUNKS = (256, 256, 256, 128, 128)
-GBUFS = 6
+CHUNKS = ((256,), (256,), (256,), (256,),)
+BANKS = 3
+ACC = 4
+GBUFS = 4
 
 
 def tile_picked_wpna_silu_l_kernel(
@@ -36,7 +38,7 @@ def tile_picked_wpna_silu_l_kernel(
 
         x_plane = keep.tile([P, T], U8, name="x_plane", align_bytes=64)
         w_plane = keep.tile([P, D * N], U8, name="w_plane", align_bytes=64)
-        nc.vector.memset(x_plane[:].bitcast(I32), 0)
+        nc.gpsimd.memset(x_plane[:].bitcast(I32), 0)
         nc.vector.memset(w_plane[:].bitcast(I32), 0)
         warm = keep.tile([P, 2], F32, name="warm")
         nc.vector.memset(warm[:, 0:1], 0.0)
@@ -48,10 +50,11 @@ def tile_picked_wpna_silu_l_kernel(
             raw = keep.tile([P, PACK, half], F32, name="w1_raw%d" % a)
             nc.sync.dma_start(out=raw[:], in_=w1_rows[:, :, a * half : (a + 1) * half])
             w1_raw.append(raw)
-        for q in range(4):
-            nc.scalar.dma_start(
-                out=x_plane[32 * q : 32 * q + 4, :].bitcast(I32), in_=x_scales[0][4 * q : 4 * q + 4, :].bitcast(I32)
-            )
+            for q in range(4 if a == 0 else 0):
+                nc.sync.dma_start(
+                    out=x_plane[32 * q : 32 * q + 4, :].bitcast(I32),
+                    in_=x_scales[0][4 * q : 4 * q + 4, :].bitcast(I32),
+                )
         nc.scalar.activation(warm[:, 1:2], warm[:, 0:1], ACT.Silu)
         x_flat = x_words[0].rearrange("p n r -> p (n r)")
         x_codes = []
@@ -97,7 +100,7 @@ def tile_picked_wpna_silu_l_kernel(
             )
             h_t = keep.tile([P, T], F32, name="h%d" % t)
             for a in range(T // BANK):
-                acc = psum.tile([P, BANK], F32, name="acc", tag="wide", bufs=4)
+                acc = psum.tile([P, BANK], F32, name="acc", tag="acc", bufs=ACC)
                 nc.tensor.matmul_mx(
                     out=acc[:],
                     lhsT=w1_codes[:].bitcast(FP8X4),
@@ -111,46 +114,53 @@ def tile_picked_wpna_silu_l_kernel(
             h.append(h_t)
 
         def fetch(v0, n, planes_first):
-            g = [ring.tile([P, PACK, n], F32, name="g", tag="g", bufs=GBUFS) for d in range(D)]
+            g = [ring.tile([P, PACK, n], F32, name="g", tag="g", bufs=GBUFS, align_bytes=64) for d in range(D)]
             order = [(t, d) for t in range(PACK) for d in range(D)]
             if not planes_first:
                 order = [(t, d) for d in range(D) for t in range(PACK)]
             for t, d in order:
                 nc.vector.tensor_copy(g[d][:, t, :], h[t][:].indirect(lists[d][:, v0 // 16 : (v0 + n) // 16]))
+            return g
+
+        def prepare(g, c0, n):
             rounded = []
             for d in range(D):
                 gb = ring.tile([P, n, PACK], BF16, name="gb", tag="gb", bufs=9, align_bytes=64)
                 nc.scalar.copy(
                     out=gb[:].rearrange("p (c i) t -> p c t i", i=4),
-                    in_=g[d][:].rearrange("p t (c i) -> p c t i", i=4),
+                    in_=g[d][:, :, c0 : c0 + n].rearrange("p t (c i) -> p c t i", i=4),
                 )
                 rounded.append(gb)
-            blocks = n // P
-            back = psum.tile([P, blocks, 2, P], F32, name="back", tag="back", bufs=2)
-            for b in range(blocks):
-                sums = psum.tile([P, PACK, P], F32, name="sums", tag="wide", bufs=4)
-                for t in range(PACK):
-                    for d in range(D):
-                        nc.tensor.matmul(
-                            sums[:, t, :],
-                            lhsT=g[d][:, t, b * P : (b + 1) * P],
-                            rhs=ident[:],
-                            start=(d == 0),
-                            stop=(d == D - 1),
-                            is_transpose=True,
-                        )
-                turned = ring.tile([P, 2, P, 2], BF16, name="turned", tag="turned", bufs=3, align_bytes=64)
-                nc.scalar.activation(
-                    turned[:], sums[:].rearrange("v (u e) p -> v u p e", e=2), ACT.Copy, scale=1.0 / D
-                )
-                pairs = turned[:].rearrange("v u p e -> v u (p e)").bitcast(F32)
-                for u in range(2):
-                    nc.tensor.transpose(back[:, b, u, :], pairs[:, u, :], ident[:])
             mean = ring.tile([P, n * PACK], BF16, name="mean", tag="mean", bufs=3, align_bytes=64)
-            nc.scalar.copy(
-                out=mean[:].bitcast(F32).rearrange("p (b v u) -> p b v u", b=blocks, u=2),
-                in_=back[:].rearrange("p b u v -> p b v u"),
-            )
+            for b0 in range(0, n // P, 2):
+                blocks = min(2, n // P - b0)
+                sums = [psum.tile([P, PACK, P], F32, name="sums", tag="bank", bufs=BANKS) for b in range(blocks)]
+                for t in range(PACK):
+                    for b in range(blocks):
+                        first = c0 + (b0 + b) * P
+                        for d in range(D):
+                            nc.tensor.matmul(
+                                sums[b][:, t, :],
+                                lhsT=g[d][:, t, first : first + P],
+                                rhs=ident[:],
+                                start=(d == 0),
+                                stop=(d == D - 1),
+                                is_transpose=True,
+                            )
+                back = psum.tile([P, blocks, 2, P], F32, name="back", tag="bank", bufs=BANKS)
+                for b in range(blocks):
+                    turned = ring.tile([P, 2, P, 2], BF16, name="turned", tag="turned", bufs=3, align_bytes=64)
+                    nc.scalar.activation(
+                        turned[:], sums[b][:].rearrange("v (u e) p -> v u p e", e=2), ACT.Copy, scale=1.0 / D
+                    )
+                    pairs = turned[:].rearrange("v u p e -> v u (p e)").bitcast(F32)
+                    for u in range(2):
+                        nc.tensor.transpose(back[:, b, u, :], pairs[:, u, :], ident[:])
+                words = mean[:, b0 * P * PACK : (b0 + blocks) * P * PACK].bitcast(F32)
+                nc.scalar.copy(
+                    out=words.rearrange("p (b v u) -> p b v u", b=blocks, u=2),
+                    in_=back[:].rearrange("p b u v -> p b v u"),
+                )
             return rounded, mean
 
         def finish(v0, n, rounded, mean):
@@ -162,15 +172,18 @@ def tile_picked_wpna_silu_l_kernel(
             ends = ring.tile([P, 2, n * PACK], BF16, name="ends", tag="ends", align_bytes=64)
             nc.vector.tensor_tensor(ends[:, 0, :], hi[:], flat[2], ALU.max)
             nc.vector.tensor_tensor(ends[:, 1, :], lo[:], flat[2], ALU.min)
+            end_codes = ring.tile([P, 2 * n], U32, name="end_codes", tag="end_codes", align_bytes=64)
+            end_plane = ring.tile([P, 2 * n], U8, name="end_plane", tag="end_plane", align_bytes=64)
+            for s in range(2):
+                nc.vector.quantize_mx(
+                    out=end_codes[:, s * n : (s + 1) * n].bitcast(FP8X4),
+                    scales=end_plane[:, s * n : (s + 1) * n],
+                    in_=ends[:, s, :],
+                )
             mean_codes = ring.tile([P, n], U32, name="mean_codes", tag="mean_codes", align_bytes=64)
             mean_plane = ring.tile([P, n], U8, name="mean_plane", tag="mean_plane", align_bytes=64)
             nc.vector.quantize_mx(out=mean_codes[:].bitcast(FP8X4), scales=mean_plane[:], in_=mean[:])
-            end_codes = ring.tile([P, 2 * n], U32, name="end_codes", tag="end_codes", align_bytes=64)
-            end_plane = ring.tile([P, 2 * n], U8, name="end_plane", tag="end_plane", align_bytes=64)
-            nc.vector.quantize_mx(
-                out=end_codes[:].bitcast(FP8X4), scales=end_plane[:], in_=ends[:].rearrange("p s c -> p (s c)")
-            )
-            total = psum.tile([P, n], F32, name="total", tag="total", bufs=2)
+            total = psum.tile([P, n], F32, name="total", tag="bank", bufs=BANKS)
             width = BANK if n == BANK else P
             for c0 in range(0, n, width):
                 operands = [
@@ -178,26 +191,32 @@ def tile_picked_wpna_silu_l_kernel(
                     (end_codes[:, c0 : c0 + width], end_plane[:, c0 : c0 + width]),
                     (end_codes[:, n + c0 : n + c0 + width], end_plane[:, n + c0 : n + c0 + width]),
                 ]
-                for s, (codes, plane) in enumerate(operands):
+                for s in (1, 2, 0):
+                    codes, plane = operands[s]
                     nc.tensor.matmul_mx(
                         out=total[:, c0 : c0 + width],
                         lhsT=w_codes[s][:].bitcast(FP4X4),
                         lhsT_scale=w_plane[:, s * N : (s + 1) * N],
                         rhs=codes.bitcast(FP8X4),
                         rhs_scale=plane,
-                        start=(s == 0),
-                        stop=(s == D - 1),
+                        start=(s == 1),
+                        stop=(s == 0),
                     )
             result = ring.tile([P, n], F32, name="result", tag="result")
             nc.scalar.copy(out=result[:], in_=total[:])
             nc.sync.dma_start(out=out[:, v0 : v0 + n], in_=result[:])
 
-        pending = None
+        pending = []
         v0 = 0
-        for c, n in enumerate(CHUNKS):
-            rounded, mean = fetch(v0, n, c == 0)
-            if pending is not None:
-                finish(*pending)
-            pending = (v0, n, rounded, mean)
-            v0 = v0 + n
-        finish(*pending)
+        for c, pieces in enumerate(CHUNKS):
+            g = fetch(v0, sum(pieces), c == 0)
+            c0 = 0
+            for n in pieces:
+                rounded, mean = prepare(g, c0, n)
+                pending.append((v0 + c0, n, rounded, mean))
+                if len(pending) > 1:
+                    finish(*pending.pop(0))
+                c0 = c0 + n
+            v0 = v0 + c0
+        for piece in pending:
+            finish(*piece)

@@ -21,9 +21,10 @@ ALU = mybir.AluOpType
 P = 128
 PACK = 4
 BANK = 512
-CHUNKS = ((256,), (256,), (256,), (256,),)
+FETCH = (256, 768,)
+FINISH = (256, 256, 256, 256,)
 BANKS = 3
-ACC = 4
+ACC = 6
 GBUFS = 4
 
 
@@ -50,11 +51,6 @@ def tile_picked_wpna_silu_l_kernel(
             raw = keep.tile([P, PACK, half], F32, name="w1_raw%d" % a)
             nc.sync.dma_start(out=raw[:], in_=w1_rows[:, :, a * half : (a + 1) * half])
             w1_raw.append(raw)
-            for q in range(4 if a == 0 else 0):
-                nc.sync.dma_start(
-                    out=x_plane[32 * q : 32 * q + 4, :].bitcast(I32),
-                    in_=x_scales[0][4 * q : 4 * q + 4, :].bitcast(I32),
-                )
         nc.scalar.activation(warm[:, 1:2], warm[:, 0:1], ACT.Silu)
         x_flat = x_words[0].rearrange("p n r -> p (n r)")
         x_codes = []
@@ -64,6 +60,11 @@ def tile_picked_wpna_silu_l_kernel(
                 out=codes[:].bitcast(I32), in_=x_flat[:, PACK * BANK * a : PACK * BANK * (a + 1)].bitcast(I32)
             )
             x_codes.append(codes)
+            for q in range(4 if a == 0 else 0):
+                nc.sync.dma_start(
+                    out=x_plane[32 * q : 32 * q + 4, :].bitcast(I32),
+                    in_=x_scales[0][4 * q : 4 * q + 4, :].bitcast(I32),
+                )
         lists = []
         for d, pos in enumerate((pos1, pos2, pos3)):
             offsets = keep.tile([P, T // 16], U16, name="offsets%d" % d)
@@ -84,10 +85,10 @@ def tile_picked_wpna_silu_l_kernel(
         make_identity(nc, ident[:])
 
         w1_bf = keep.tile([P, PACK, P, PACK], BF16, name="w1_bf", align_bytes=64)
-        for a in range(2):
-            nc.vector.tensor_copy(
-                out=w1_bf[:, :, a * (P // 2) : (a + 1) * (P // 2), :].rearrange("p t m j -> p m j t"),
-                in_=w1_raw[a][:].rearrange("p j (m t) -> p m j t", t=PACK),
+        for a, m0, m1, copy in ((0, 0, 64, nc.vector.tensor_copy), (1, 0, 44, nc.vector.tensor_copy), (1, 44, 64, nc.scalar.copy)):
+            copy(
+                out=w1_bf[:, :, a * 64 + m0 : a * 64 + m1, :].rearrange("p t m j -> p m j t"),
+                in_=w1_raw[a][:, :, PACK * m0 : PACK * m1].rearrange("p j (m t) -> p m j t", t=PACK),
             )
         h = []
         for t in range(PACK):
@@ -99,18 +100,19 @@ def tile_picked_wpna_silu_l_kernel(
                 in_=w1_bf[:, t, :, :].rearrange("p m j -> p (m j)"),
             )
             h_t = keep.tile([P, T], F32, name="h%d" % t)
-            for a in range(T // BANK):
-                acc = psum.tile([P, BANK], F32, name="acc", tag="acc", bufs=ACC)
+            width = 256 if t == 0 else BANK
+            for c0 in range(0, T, width):
+                acc = psum.tile([P, width], F32, name="acc", tag="acc", bufs=ACC)
                 nc.tensor.matmul_mx(
                     out=acc[:],
                     lhsT=w1_codes[:].bitcast(FP8X4),
                     lhsT_scale=w1_plane[:],
-                    rhs=x_codes[a][:].bitcast(FP8X4),
-                    rhs_scale=x_plane[:, a * BANK : (a + 1) * BANK],
+                    rhs=x_codes[c0 // BANK][:, c0 % BANK : c0 % BANK + width].bitcast(FP8X4),
+                    rhs_scale=x_plane[:, c0 : c0 + width],
                     start=True,
                     stop=True,
                 )
-                nc.scalar.activation(h_t[:, a * BANK : (a + 1) * BANK], acc[:], ACT.Silu)
+                nc.scalar.activation(h_t[:, c0 : c0 + width], acc[:], ACT.Silu)
             h.append(h_t)
 
         def fetch(v0, n, planes_first):
@@ -122,49 +124,53 @@ def tile_picked_wpna_silu_l_kernel(
                 nc.vector.tensor_copy(g[d][:, t, :], h[t][:].indirect(lists[d][:, v0 // 16 : (v0 + n) // 16]))
             return g
 
-        def prepare(g, c0, n):
-            rounded = []
-            for d in range(D):
-                gb = ring.tile([P, n, PACK], BF16, name="gb", tag="gb", bufs=9, align_bytes=64)
-                nc.scalar.copy(
-                    out=gb[:].rearrange("p (c i) t -> p c t i", i=4),
-                    in_=g[d][:, :, c0 : c0 + n].rearrange("p t (c i) -> p c t i", i=4),
+        def round_off(g_d, c0, n, gb):
+            nc.scalar.copy(
+                out=gb.rearrange("p (c i) t -> p c t i", i=4),
+                in_=g_d[:, :, c0 : c0 + n].rearrange("p t (c i) -> p c t i", i=4),
+            )
+
+        def add_up(g, n, planes_first):
+            order = [(d, t) for d in range(D) for t in range(PACK)]
+            if planes_first:
+                order = [(d, t) for t in range(PACK) for d in range(D)]
+            sums = [psum.tile([P, PACK, P], F32, name="sums", tag="acc", bufs=ACC) for b in range(n // P)]
+            for d, t in order:
+                for b in range(n // P):
+                    if True:
+                        nc.tensor.matmul(
+                            sums[b][:, t, :],
+                            lhsT=g[d][:, t, b * P : (b + 1) * P],
+                            rhs=ident[:],
+                            start=((d, t) == order[0]),
+                            stop=((d, t) == order[-1]),
+                            is_transpose=True,
+                        )
+            return sums
+
+        def turn_back(sums, tag):
+            blocks = len(sums)
+            back = psum.tile([P, blocks, 2, P], F32, name="back", tag=tag, bufs=1)
+            for b in range(blocks):
+                turned = ring.tile([P, 2, P, 2], BF16, name="turned", tag="turned", bufs=3, align_bytes=64)
+                nc.scalar.activation(
+                    turned[:], sums[b][:].rearrange("v (u e) p -> v u p e", e=2), ACT.Copy, scale=1.0 / D
                 )
-                rounded.append(gb)
-            mean = ring.tile([P, n * PACK], BF16, name="mean", tag="mean", bufs=3, align_bytes=64)
-            for b0 in range(0, n // P, 2):
-                blocks = min(2, n // P - b0)
-                sums = [psum.tile([P, PACK, P], F32, name="sums", tag="bank", bufs=BANKS) for b in range(blocks)]
-                for t in range(PACK):
-                    for b in range(blocks):
-                        first = c0 + (b0 + b) * P
-                        for d in range(D):
-                            nc.tensor.matmul(
-                                sums[b][:, t, :],
-                                lhsT=g[d][:, t, first : first + P],
-                                rhs=ident[:],
-                                start=(d == 0),
-                                stop=(d == D - 1),
-                                is_transpose=True,
-                            )
-                back = psum.tile([P, blocks, 2, P], F32, name="back", tag="bank", bufs=BANKS)
-                for b in range(blocks):
-                    turned = ring.tile([P, 2, P, 2], BF16, name="turned", tag="turned", bufs=3, align_bytes=64)
-                    nc.scalar.activation(
-                        turned[:], sums[b][:].rearrange("v (u e) p -> v u p e", e=2), ACT.Copy, scale=1.0 / D
-                    )
-                    pairs = turned[:].rearrange("v u p e -> v u (p e)").bitcast(F32)
-                    for u in range(2):
-                        nc.tensor.transpose(back[:, b, u, :], pairs[:, u, :], ident[:])
-                words = mean[:, b0 * P * PACK : (b0 + blocks) * P * PACK].bitcast(F32)
-                nc.scalar.copy(
-                    out=words.rearrange("p (b v u) -> p b v u", b=blocks, u=2),
-                    in_=back[:].rearrange("p b u v -> p b v u"),
-                )
-            return rounded, mean
+                pairs = turned[:].rearrange("v u p e -> v u (p e)").bitcast(F32)
+                for u in range(2):
+                    nc.tensor.transpose(back[:, b, u, :], pairs[:, u, :], ident[:])
+            return back
+
+        def lay_out(back, words):
+            blocks = back.shape[1]
+            nc.scalar.copy(
+                out=words.rearrange("p (b v u) -> p b v u", b=blocks, u=2),
+                in_=back[:].rearrange("p b u v -> p b v u"),
+            )
 
         def finish(v0, n, rounded, mean):
-            flat = [gb[:].rearrange("p c t -> p (c t)") for gb in rounded]
+            last = v0 + n == T
+            flat = [gb.rearrange("p c t -> p (c t)") for gb in rounded]
             hi = ring.tile([P, n * PACK], BF16, name="hi", tag="hi", align_bytes=64)
             lo = ring.tile([P, n * PACK], BF16, name="lo", tag="lo", align_bytes=64)
             nc.vector.tensor_tensor(hi[:], flat[0], flat[1], ALU.max)
@@ -182,10 +188,15 @@ def tile_picked_wpna_silu_l_kernel(
                 )
             mean_codes = ring.tile([P, n], U32, name="mean_codes", tag="mean_codes", align_bytes=64)
             mean_plane = ring.tile([P, n], U8, name="mean_plane", tag="mean_plane", align_bytes=64)
-            nc.vector.quantize_mx(out=mean_codes[:].bitcast(FP8X4), scales=mean_plane[:], in_=mean[:])
-            total = psum.tile([P, n], F32, name="total", tag="bank", bufs=BANKS)
+            nc.vector.quantize_mx(out=mean_codes[:].bitcast(FP8X4), scales=mean_plane[:], in_=mean)
             width = BANK if n == BANK else P
+            result = ring.tile([P, n], F32, name="result", tag="result")
+            total = psum.tile([P, n], F32, name="total", tag="bank", bufs=1)
+            other = total
+            if last:
+                other = psum.tile([P, n], F32, name="other", tag="spare", bufs=1)
             for c0 in range(0, n, width):
+                bank = total if c0 == 0 else other
                 operands = [
                     (mean_codes[:, c0 : c0 + width], mean_plane[:, c0 : c0 + width]),
                     (end_codes[:, c0 : c0 + width], end_plane[:, c0 : c0 + width]),
@@ -194,7 +205,7 @@ def tile_picked_wpna_silu_l_kernel(
                 for s in (1, 2, 0):
                     codes, plane = operands[s]
                     nc.tensor.matmul_mx(
-                        out=total[:, c0 : c0 + width],
+                        out=bank[:, c0 : c0 + width],
                         lhsT=w_codes[s][:].bitcast(FP4X4),
                         lhsT_scale=w_plane[:, s * N : (s + 1) * N],
                         rhs=codes.bitcast(FP8X4),
@@ -202,21 +213,45 @@ def tile_picked_wpna_silu_l_kernel(
                         start=(s == 1),
                         stop=(s == 0),
                     )
-            result = ring.tile([P, n], F32, name="result", tag="result")
-            nc.scalar.copy(out=result[:], in_=total[:])
+            if last:
+                nc.scalar.copy(out=result[:, :P], in_=total[:, :P])
+                nc.vector.tensor_copy(out=result[:, P:], in_=other[:, P:])
+            else:
+                nc.scalar.copy(out=result[:], in_=total[:])
             nc.sync.dma_start(out=out[:, v0 : v0 + n], in_=result[:])
 
+        rounded = [keep.tile([P, T, PACK], BF16, name="rounded%d" % d, align_bytes=64) for d in range(D)]
+        mean = keep.tile([P, T * PACK], BF16, name="mean", align_bytes=64)
         pending = []
-        v0 = 0
-        for c, pieces in enumerate(CHUNKS):
-            g = fetch(v0, sum(pieces), c == 0)
-            c0 = 0
-            for n in pieces:
-                rounded, mean = prepare(g, c0, n)
-                pending.append((v0 + c0, n, rounded, mean))
-                if len(pending) > 1:
-                    finish(*pending.pop(0))
-                c0 = c0 + n
-            v0 = v0 + c0
+        g0 = 0
+        waiting = []
+        for width in FETCH:
+            g = fetch(g0, width, g0 == 0)
+            for d in range(D - 1):
+                for c0 in range(0, width, width):
+                    c1 = min(width, c0 + width)
+                    round_off(g[d], c0, c1 - c0, rounded[d][:, g0 + c0 : g0 + c1, :])
+            for late in waiting:
+                lay_out(*late)
+            waiting = []
+            sums = add_up(g, width, g0 == 0)
+            v0 = g0
+            while v0 < g0 + width:
+                v1 = min(g0 + width, (v0 // 256 + 1) * 256)
+                round_off(g[D - 1], v0 - g0, v1 - v0, rounded[D - 1][:, v0:v1, :])
+                back = turn_back(sums[(v0 - g0) // P : (v1 - g0) // P], "spare" if v1 == T else "bank")
+                words = mean[:, v0 * PACK : v1 * PACK].bitcast(F32)
+                if v1 == g0 + width and v1 < T:
+                    waiting.append((back, words))
+                else:
+                    lay_out(back, words)
+                if v1 % 256 == 0:
+                    pending.append(
+                        (v1 - 256, 256, [r[:, v1 - 256 : v1, :] for r in rounded], mean[:, (v1 - 256) * PACK : v1 * PACK])
+                    )
+                    if len(pending) > 1:
+                        finish(*pending.pop(0))
+                v0 = v1
+            g0 = g0 + width
         for piece in pending:
             finish(*piece)

@@ -41,17 +41,9 @@ def tile_picked_wpna_silu_l_kernel(
         w_plane = keep.tile([P, D * N], U8, name="w_plane", align_bytes=64)
         nc.gpsimd.memset(x_plane[:].bitcast(I32), 0)
         nc.vector.memset(w_plane[:].bitcast(I32), 0)
-        warm = keep.tile([P, 2], F32, name="warm")
-        nc.vector.memset(warm[:, 0:1], 0.0)
 
-        half = H // 2
-        w1_rows = w1.rearrange("(p j) c -> p j c", j=PACK)
-        w1_raw = []
-        for a in range(2):
-            raw = keep.tile([P, PACK, half], F32, name="w1_raw%d" % a)
-            nc.sync.dma_start(out=raw[:], in_=w1_rows[:, :, a * half : (a + 1) * half])
-            w1_raw.append(raw)
-        nc.scalar.activation(warm[:, 1:2], warm[:, 0:1], ACT.Silu)
+        w1_raw = keep.tile([P, PACK, H], F32, name="w1_raw")
+        nc.sync.dma_start(out=w1_raw[:], in_=w1.rearrange("(p j) c -> p j c", j=PACK))
         x_flat = x_words[0].rearrange("p n r -> p (n r)")
         x_codes = []
         for a in range(T // BANK):
@@ -84,12 +76,11 @@ def tile_picked_wpna_silu_l_kernel(
         ident = keep.tile([P, P], F32, name="ident")
         make_identity(nc, ident[:])
 
-        w1_bf = keep.tile([P, PACK, P, PACK], BF16, name="w1_bf", align_bytes=64)
-        for a, m0, m1, copy in ((0, 0, 64, nc.vector.tensor_copy), (1, 0, 44, nc.vector.tensor_copy), (1, 44, 64, nc.scalar.copy)):
-            copy(
-                out=w1_bf[:, :, a * 64 + m0 : a * 64 + m1, :].rearrange("p t m j -> p m j t"),
-                in_=w1_raw[a][:, :, PACK * m0 : PACK * m1].rearrange("p j (m t) -> p m j t", t=PACK),
-            )
+        w1_first = keep.tile([P, P, PACK], BF16, name="w1_first", tag="w1_bf", align_bytes=64)
+        w1_rest = keep.tile([P, PACK - 1, P, PACK], BF16, name="w1_rest", tag="w1_bf", align_bytes=64)
+        dealt = w1_raw[:].rearrange("p j (m t) -> p m j t", t=PACK)
+        nc.vector.tensor_copy(out=w1_first[:], in_=dealt[:, :, :, 0])
+        w1_bf = [w1_first[:]] + [w1_rest[:, t, :, :] for t in range(PACK - 1)]
         h = []
         for t in range(PACK):
             w1_codes = keep.tile([P, P], U32, name="w1_codes%d" % t, align_bytes=64)
@@ -97,8 +88,10 @@ def tile_picked_wpna_silu_l_kernel(
             nc.vector.quantize_mx(
                 out=w1_codes[:].bitcast(FP8X4),
                 scales=w1_plane[:],
-                in_=w1_bf[:, t, :, :].rearrange("p m j -> p (m j)"),
+                in_=w1_bf[t].rearrange("p m j -> p (m j)"),
             )
+            if t == 0:
+                nc.vector.tensor_copy(out=w1_rest[:].rearrange("p t m j -> p m j t"), in_=dealt[:, :, :, 1:PACK])
             h_t = keep.tile([P, T], F32, name="h%d" % t)
             width = 256 if t == 0 else BANK
             for c0 in range(0, T, width):

@@ -21,11 +21,9 @@ ALU = mybir.AluOpType
 P = 128
 PACK = 4
 BANK = 512
-FETCH = (256, 768,)
-FINISH = (256, 256, 256, 256,)
-BANKS = 3
-ACC = 6
-GBUFS = 4
+BANKS = 8
+HALF = 512
+SPARE = 352
 
 
 def tile_picked_wpna_silu_l_kernel(
@@ -44,19 +42,13 @@ def tile_picked_wpna_silu_l_kernel(
 
         w1_raw = keep.tile([P, PACK, H], F32, name="w1_raw")
         nc.sync.dma_start(out=w1_raw[:], in_=w1.rearrange("(p j) c -> p j c", j=PACK))
-        x_flat = x_words[0].rearrange("p n r -> p (n r)")
-        x_codes = []
-        for a in range(T // BANK):
-            codes = keep.tile([P, BANK], U32, name="x_codes%d" % a, align_bytes=64)
+        for q in range(4):
             nc.sync.dma_start(
-                out=codes[:].bitcast(I32), in_=x_flat[:, PACK * BANK * a : PACK * BANK * (a + 1)].bitcast(I32)
+                out=x_plane[32 * q : 32 * q + 4, :].bitcast(I32),
+                in_=x_scales[0][4 * q : 4 * q + 4, :].bitcast(I32),
             )
-            x_codes.append(codes)
-            for q in range(4 if a == 0 else 0):
-                nc.sync.dma_start(
-                    out=x_plane[32 * q : 32 * q + 4, :].bitcast(I32),
-                    in_=x_scales[0][4 * q : 4 * q + 4, :].bitcast(I32),
-                )
+        x_codes = keep.tile([P, T], U32, name="x_codes", align_bytes=64)
+        nc.sync.dma_start(out=x_codes[:].bitcast(I32), in_=x_words[0].rearrange("p n r -> p (n r)").bitcast(I32))
         lists = []
         for d, pos in enumerate((pos1, pos2, pos3)):
             offsets = keep.tile([P, T // 16], U16, name="offsets%d" % d)
@@ -76,12 +68,20 @@ def tile_picked_wpna_silu_l_kernel(
         ident = keep.tile([P, P], F32, name="ident")
         make_identity(nc, ident[:])
 
+        def bank(b, shape, name):
+            return psum.tile(shape, F32, name=name, tag="bank%d" % b, bufs=1)
+
+        h_all = keep.tile([P, PACK * T + 2 * SPARE], F32, name="h_all", align_bytes=64)
+        starts = [2 * T, T, 0, 3 * T + SPARE]
+        nc.gpsimd.memset(h_all[:, 3 * T : 3 * T + SPARE], 0.0)
+        nc.gpsimd.memset(h_all[:, 4 * T + SPARE :], 0.0)
+
         w1_first = keep.tile([P, P, PACK], BF16, name="w1_first", tag="w1_bf", align_bytes=64)
         w1_rest = keep.tile([P, PACK - 1, P, PACK], BF16, name="w1_rest", tag="w1_bf", align_bytes=64)
         dealt = w1_raw[:].rearrange("p j (m t) -> p m j t", t=PACK)
         nc.vector.tensor_copy(out=w1_first[:], in_=dealt[:, :, :, 0])
         w1_bf = [w1_first[:]] + [w1_rest[:, t, :, :] for t in range(PACK - 1)]
-        h = []
+        used = 0
         for t in range(PACK):
             w1_codes = keep.tile([P, P], U32, name="w1_codes%d" % t, align_bytes=64)
             w1_plane = keep.tile([P, P], U8, name="w1_plane%d" % t, align_bytes=64)
@@ -92,159 +92,133 @@ def tile_picked_wpna_silu_l_kernel(
             )
             if t == 0:
                 nc.vector.tensor_copy(out=w1_rest[:].rearrange("p t m j -> p m j t"), in_=dealt[:, :, :, 1:PACK])
-            h_t = keep.tile([P, T], F32, name="h%d" % t)
+            h0 = starts[t]
             width = 256 if t == 0 else BANK
-            for c0 in range(0, T, width):
-                acc = psum.tile([P, width], F32, name="acc", tag="acc", bufs=ACC)
+            for c0 in range(0, T, width) if t < PACK - 1 else range(T - width, -1, -width):
+                acc = bank(used % BANKS, [P, width], "acc")
+                used = used + 1
                 nc.tensor.matmul_mx(
                     out=acc[:],
                     lhsT=w1_codes[:].bitcast(FP8X4),
                     lhsT_scale=w1_plane[:],
-                    rhs=x_codes[c0 // BANK][:, c0 % BANK : c0 % BANK + width].bitcast(FP8X4),
+                    rhs=x_codes[:, c0 : c0 + width].bitcast(FP8X4),
                     rhs_scale=x_plane[:, c0 : c0 + width],
                     start=True,
                     stop=True,
                 )
-                nc.scalar.activation(h_t[:, c0 : c0 + width], acc[:], ACT.Silu)
-            h.append(h_t)
+                nc.scalar.activation(h_all[:, h0 + c0 : h0 + c0 + width], acc[:], ACT.Silu)
 
-        def fetch(v0, n, planes_first):
-            g = [ring.tile([P, PACK, n], F32, name="g", tag="g", bufs=GBUFS, align_bytes=64) for d in range(D)]
-            order = [(t, d) for t in range(PACK) for d in range(D)]
-            if not planes_first:
-                order = [(t, d) for d in range(D) for t in range(PACK)]
-            for t, d in order:
-                nc.vector.tensor_copy(g[d][:, t, :], h[t][:].indirect(lists[d][:, v0 // 16 : (v0 + n) // 16]))
+        rounded = [keep.tile([P, T, PACK], BF16, name="rounded%d" % d, align_bytes=64) for d in range(D)]
+        mean = keep.tile([P, T * PACK], BF16, name="mean", align_bytes=64)
+        sums = [bank(b, [P, PACK, P], "sums") for b in range(T // P)]
+
+        def fetch(d, v0, n):
+            g = keep.tile([P, PACK, n], F32, name="g%d_%d" % (d, v0), align_bytes=64)
+            for t in range(PACK):
+                h0 = starts[t]
+                h1 = h0 + T + SPARE if d == 0 or t == PACK - 1 else starts[PACK - 1] + 8
+                nc.vector.tensor_copy(
+                    g[:, t, :],
+                    h_all[:, h0:h1].indirect(lists[d][:, v0 // 16 : (v0 + n) // 16]),
+                )
+                for b in range(v0 // P, (v0 + n) // P):
+                    nc.tensor.matmul(
+                        sums[b][:, t, :],
+                        lhsT=g[:, t, b * P - v0 : (b + 1) * P - v0],
+                        rhs=ident[:],
+                        start=(d == 0 and t == 0),
+                        stop=(d == D - 1 and t == PACK - 1),
+                        is_transpose=True,
+                    )
+            nc.scalar.copy(
+                out=rounded[d][:, v0 : v0 + n, :].rearrange("p (c i) t -> p c t i", i=4),
+                in_=g[:].rearrange("p t (c i) -> p c t i", i=4),
+            )
             return g
 
-        def round_off(g_d, c0, n, gb):
-            nc.scalar.copy(
-                out=gb.rearrange("p (c i) t -> p c t i", i=4),
-                in_=g_d[:, :, c0 : c0 + n].rearrange("p t (c i) -> p c t i", i=4),
-            )
-
-        def add_up(g, n, planes_first):
-            order = [(d, t) for d in range(D) for t in range(PACK)]
-            if planes_first:
-                order = [(d, t) for t in range(PACK) for d in range(D)]
-            sums = [psum.tile([P, PACK, P], F32, name="sums", tag="acc", bufs=ACC) for b in range(n // P)]
-            for d, t in order:
-                for b in range(n // P):
-                    if True:
-                        nc.tensor.matmul(
-                            sums[b][:, t, :],
-                            lhsT=g[d][:, t, b * P : (b + 1) * P],
-                            rhs=ident[:],
-                            start=((d, t) == order[0]),
-                            stop=((d, t) == order[-1]),
-                            is_transpose=True,
-                        )
-            return sums
-
-        def turn_back(sums, tag):
-            blocks = len(sums)
-            back = psum.tile([P, blocks, 2, P], F32, name="back", tag=tag, bufs=1)
-            for b in range(blocks):
-                turned = ring.tile([P, 2, P, 2], BF16, name="turned", tag="turned", bufs=3, align_bytes=64)
+        def turn_back(b0, b1, group):
+            backs = []
+            for b in range(b0, b1):
+                turned = ring.tile([P, 2, P, 2], BF16, name="turned", tag="turned", bufs=4, align_bytes=64)
                 nc.scalar.activation(
                     turned[:], sums[b][:].rearrange("v (u e) p -> v u p e", e=2), ACT.Copy, scale=1.0 / D
                 )
                 pairs = turned[:].rearrange("v u p e -> v u (p e)").bitcast(F32)
+                if (b - b0) % group == 0:
+                    backs.append(bank(b, [P, group, 2, P], "back"))
                 for u in range(2):
-                    nc.tensor.transpose(back[:, b, u, :], pairs[:, u, :], ident[:])
-            return back
+                    nc.tensor.transpose(backs[-1][:, (b - b0) % group, u, :], pairs[:, u, :], ident[:])
+            for i, back in enumerate(backs):
+                v0 = (b0 + i * group) * P
+                words = mean[:, v0 * PACK : (v0 + group * P) * PACK].bitcast(F32)
+                nc.scalar.copy(
+                    out=words.rearrange("p (b v u) -> p b v u", b=group, u=2),
+                    in_=back[:].rearrange("p b u v -> p b v u"),
+                )
 
-        def lay_out(back, words):
-            blocks = back.shape[1]
-            nc.scalar.copy(
-                out=words.rearrange("p (b v u) -> p b v u", b=blocks, u=2),
-                in_=back[:].rearrange("p b u v -> p b v u"),
+        g_0 = fetch(0, 0, T)
+        g_1 = fetch(1, 0, T)
+        fetch(2, 0, HALF)
+        turn_back(0, HALF // P, 2)
+        g_last = fetch(2, HALF, T - HALF)
+        turn_back(HALF // P, T // P, 1)
+
+        flat = [r[:].rearrange("p v t -> p (v t)") for r in rounded]
+        hi = keep.tile([P, T * PACK], BF16, name="hi", align_bytes=64)
+        lo = keep.tile([P, T * PACK], BF16, name="lo", align_bytes=64)
+        nc.vector.tensor_tensor(hi[:], flat[0], flat[1], ALU.max)
+        nc.vector.tensor_tensor(lo[:], flat[0], flat[1], ALU.min)
+        largest = keep.tile([P, T * PACK], BF16, name="largest", align_bytes=64)
+        smallest = keep.tile([P, T * PACK], BF16, name="smallest", align_bytes=64)
+        stats = [mean, largest, smallest]
+        z_codes = [keep.tile([P, T], U32, name="z_codes%d" % s, align_bytes=64) for s in range(D)]
+        z_plane = [keep.tile([P, T], U8, name="z_plane%d" % s, align_bytes=64) for s in range(D)]
+
+        def compare(v0, n):
+            cols = slice(v0 * PACK, (v0 + n) * PACK)
+            nc.vector.tensor_tensor(largest[:, cols], hi[:, cols], flat[2][:, cols], ALU.max)
+            nc.vector.tensor_tensor(smallest[:, cols], lo[:, cols], flat[2][:, cols], ALU.min)
+
+        def quantise(s, v0, n):
+            nc.vector.quantize_mx(
+                out=z_codes[s][:, v0 : v0 + n].bitcast(FP8X4),
+                scales=z_plane[s][:, v0 : v0 + n],
+                in_=stats[s][:, v0 * PACK : (v0 + n) * PACK],
             )
 
-        def finish(v0, n, rounded, mean):
-            last = v0 + n == T
-            flat = [gb.rearrange("p c t -> p (c t)") for gb in rounded]
-            hi = ring.tile([P, n * PACK], BF16, name="hi", tag="hi", align_bytes=64)
-            lo = ring.tile([P, n * PACK], BF16, name="lo", tag="lo", align_bytes=64)
-            nc.vector.tensor_tensor(hi[:], flat[0], flat[1], ALU.max)
-            nc.vector.tensor_tensor(lo[:], flat[0], flat[1], ALU.min)
-            ends = ring.tile([P, 2, n * PACK], BF16, name="ends", tag="ends", align_bytes=64)
-            nc.vector.tensor_tensor(ends[:, 0, :], hi[:], flat[2], ALU.max)
-            nc.vector.tensor_tensor(ends[:, 1, :], lo[:], flat[2], ALU.min)
-            end_codes = ring.tile([P, 2 * n], U32, name="end_codes", tag="end_codes", align_bytes=64)
-            end_plane = ring.tile([P, 2 * n], U8, name="end_plane", tag="end_plane", align_bytes=64)
-            for s in range(2):
-                nc.vector.quantize_mx(
-                    out=end_codes[:, s * n : (s + 1) * n].bitcast(FP8X4),
-                    scales=end_plane[:, s * n : (s + 1) * n],
-                    in_=ends[:, s, :],
-                )
-            mean_codes = ring.tile([P, n], U32, name="mean_codes", tag="mean_codes", align_bytes=64)
-            mean_plane = ring.tile([P, n], U8, name="mean_plane", tag="mean_plane", align_bytes=64)
-            nc.vector.quantize_mx(out=mean_codes[:].bitcast(FP8X4), scales=mean_plane[:], in_=mean)
-            width = BANK if n == BANK else P
-            result = ring.tile([P, n], F32, name="result", tag="result")
-            total = psum.tile([P, n], F32, name="total", tag="bank", bufs=1)
-            other = total
-            if last:
-                other = psum.tile([P, n], F32, name="other", tag="spare", bufs=1)
-            for c0 in range(0, n, width):
-                bank = total if c0 == 0 else other
-                operands = [
-                    (mean_codes[:, c0 : c0 + width], mean_plane[:, c0 : c0 + width]),
-                    (end_codes[:, c0 : c0 + width], end_plane[:, c0 : c0 + width]),
-                    (end_codes[:, n + c0 : n + c0 + width], end_plane[:, n + c0 : n + c0 + width]),
-                ]
-                for s in (1, 2, 0):
-                    codes, plane = operands[s]
-                    nc.tensor.matmul_mx(
-                        out=bank[:, c0 : c0 + width],
-                        lhsT=w_codes[s][:].bitcast(FP4X4),
-                        lhsT_scale=w_plane[:, s * N : (s + 1) * N],
-                        rhs=codes.bitcast(FP8X4),
-                        rhs_scale=plane,
-                        start=(s == 1),
-                        stop=(s == 0),
-                    )
-            if last:
-                nc.scalar.copy(out=result[:, :P], in_=total[:, :P])
-                nc.vector.tensor_copy(out=result[:, P:], in_=other[:, P:])
-            else:
-                nc.scalar.copy(out=result[:], in_=total[:])
-            nc.sync.dma_start(out=out[:, v0 : v0 + n], in_=result[:])
+        def multiply(total, s, v0, n):
+            nc.tensor.matmul_mx(
+                out=total[:],
+                lhsT=w_codes[s][:].bitcast(FP4X4),
+                lhsT_scale=w_plane[:, s * N : (s + 1) * N],
+                rhs=z_codes[s][:, v0 : v0 + n].bitcast(FP8X4),
+                rhs_scale=z_plane[s][:, v0 : v0 + n],
+                start=(s == 1),
+                stop=(s == 0),
+            )
 
-        rounded = [keep.tile([P, T, PACK], BF16, name="rounded%d" % d, align_bytes=64) for d in range(D)]
-        mean = keep.tile([P, T * PACK], BF16, name="mean", align_bytes=64)
-        pending = []
-        g0 = 0
-        waiting = []
-        for width in FETCH:
-            g = fetch(g0, width, g0 == 0)
-            for d in range(D - 1):
-                for c0 in range(0, width, width):
-                    c1 = min(width, c0 + width)
-                    round_off(g[d], c0, c1 - c0, rounded[d][:, g0 + c0 : g0 + c1, :])
-            for late in waiting:
-                lay_out(*late)
-            waiting = []
-            sums = add_up(g, width, g0 == 0)
-            v0 = g0
-            while v0 < g0 + width:
-                v1 = min(g0 + width, (v0 // 256 + 1) * 256)
-                round_off(g[D - 1], v0 - g0, v1 - v0, rounded[D - 1][:, v0:v1, :])
-                back = turn_back(sums[(v0 - g0) // P : (v1 - g0) // P], "spare" if v1 == T else "bank")
-                words = mean[:, v0 * PACK : v1 * PACK].bitcast(F32)
-                if v1 == g0 + width and v1 < T:
-                    waiting.append((back, words))
+        result = keep.tile([P, T], F32, name="result", align_bytes=64)
+        compare(0, HALF)
+        total = bank(HALF // P, [P, HALF], "total")
+        for s in (1, 2, 0):
+            quantise(s, 0, HALF)
+            multiply(total, s, 0, HALF)
+        nc.scalar.copy(out=result[:, :HALF], in_=total[:])
+        nc.sync.dma_start(out=out[:, :HALF], in_=result[:, :HALF])
+
+        compare(HALF, T - HALF)
+        blocks = range(HALF // P, T // P)
+        totals = {b: bank(b, [P, P], "total") for b in blocks}
+        for s in (1, 2):
+            quantise(s, HALF, T - HALF)
+            for b in blocks:
+                multiply(totals[b], s, b * P, P)
+        for v0 in range(HALF, T, 2 * P):
+            quantise(0, v0, 2 * P)
+            for b in (v0 // P, v0 // P + 1):
+                multiply(totals[b], 0, b * P, P)
+                if b == T // P - 1:
+                    nc.vector.tensor_copy(out=result[:, b * P : (b + 1) * P], in_=totals[b][:])
                 else:
-                    lay_out(back, words)
-                if v1 % 256 == 0:
-                    pending.append(
-                        (v1 - 256, 256, [r[:, v1 - 256 : v1, :] for r in rounded], mean[:, (v1 - 256) * PACK : v1 * PACK])
-                    )
-                    if len(pending) > 1:
-                        finish(*pending.pop(0))
-                v0 = v1
-            g0 = g0 + width
-        for piece in pending:
-            finish(*piece)
+                    nc.scalar.copy(out=result[:, b * P : (b + 1) * P], in_=totals[b][:])
+            nc.sync.dma_start(out=out[:, v0 : v0 + 2 * P], in_=result[:, v0 : v0 + 2 * P])

@@ -22,6 +22,7 @@ P = 128
 PACK = 4
 BANK = 512
 BANKS = 8
+CHUNK = 256
 HALF = 512
 SPARE = 352
 
@@ -35,20 +36,30 @@ def tile_picked_wpna_silu_l_kernel(
         ring = ctx.enter_context(tc.tile_pool(name="ring", bufs=2))
         psum = ctx.enter_context(tc.psum_pool(name="psum", bufs=2))
 
-        x_plane = keep.tile([P, T], U8, name="x_plane", align_bytes=64)
+        x_plane = keep.tile([P, CHUNK], U8, name="x_plane", align_bytes=64)
         w_plane = keep.tile([P, D * N], U8, name="w_plane", align_bytes=64)
-        nc.gpsimd.memset(x_plane[:].bitcast(I32), 0)
+        nc.vector.memset(x_plane[:].bitcast(I32), 0)
         nc.vector.memset(w_plane[:].bitcast(I32), 0)
 
-        w1_raw = keep.tile([P, PACK, H], F32, name="w1_raw")
-        nc.sync.dma_start(out=w1_raw[:], in_=w1.rearrange("(p j) c -> p j c", j=PACK))
+        w1_rows = w1.rearrange("(p j) c -> p j c", j=PACK)
+        w1_raw = []
+        for a in range(2):
+            raw = keep.tile([P, 2, H], F32, name="w1_raw%d" % a)
+            nc.sync.dma_start(out=raw[:], in_=w1_rows[:, 2 * a : 2 * a + 2, :])
+            w1_raw.append(raw)
         for q in range(4):
             nc.sync.dma_start(
-                out=x_plane[32 * q : 32 * q + 4, :].bitcast(I32),
-                in_=x_scales[0][4 * q : 4 * q + 4, :].bitcast(I32),
+                out=x_plane[32 * q : 32 * q + 16, :].bitcast(I32),
+                in_=x_scales[0][4 * q : 4 * q + 4, :].bitcast(I32).rearrange("r (c n) -> c r n", c=T // CHUNK),
             )
-        x_codes = keep.tile([P, T], U32, name="x_codes", align_bytes=64)
-        nc.sync.dma_start(out=x_codes[:].bitcast(I32), in_=x_words[0].rearrange("p n r -> p (n r)").bitcast(I32))
+        x_flat = x_words[0].rearrange("p n r -> p (n r)")
+        x_codes = []
+        for a in range(T // BANK):
+            codes = keep.tile([P, BANK], U32, name="x_codes%d" % a, align_bytes=64)
+            nc.sync.dma_start(
+                out=codes[:].bitcast(I32), in_=x_flat[:, PACK * BANK * a : PACK * BANK * (a + 1)].bitcast(I32)
+            )
+            x_codes.append(codes)
         lists = []
         for d, pos in enumerate((pos1, pos2, pos3)):
             offsets = keep.tile([P, T // 16], U16, name="offsets%d" % d)
@@ -78,38 +89,49 @@ def tile_picked_wpna_silu_l_kernel(
 
         w1_first = keep.tile([P, P, PACK], BF16, name="w1_first", tag="w1_bf", align_bytes=64)
         w1_rest = keep.tile([P, PACK - 1, P, PACK], BF16, name="w1_rest", tag="w1_bf", align_bytes=64)
-        dealt = w1_raw[:].rearrange("p j (m t) -> p m j t", t=PACK)
-        nc.vector.tensor_copy(out=w1_first[:], in_=dealt[:, :, :, 0])
-        w1_bf = [w1_first[:]] + [w1_rest[:, t, :, :] for t in range(PACK - 1)]
+        dealt = [raw[:].rearrange("p j (m t) -> p m j t", t=PACK) for raw in w1_raw]
+        for a in range(2):
+            nc.vector.tensor_copy(out=w1_first[:, :, 2 * a : 2 * a + 2], in_=dealt[a][:, :, :, 0])
+        first_codes = keep.tile([P, P], U32, name="first_codes", tag="w1_codes", align_bytes=64)
+        w1_planes = keep.tile([P, PACK * P], U8, name="w1_planes", align_bytes=64)
+        nc.vector.quantize_mx(
+            out=first_codes[:].bitcast(FP8X4), scales=w1_planes[:, :P], in_=w1_first[:].rearrange("p m j -> p (m j)")
+        )
+        for a in range(2):
+            nc.vector.tensor_copy(
+                out=w1_rest[:, :, :, 2 * a : 2 * a + 2].rearrange("p t m j -> p m j t"), in_=dealt[a][:, :, :, 1:PACK]
+            )
         used = 0
         for t in range(PACK):
-            w1_codes = keep.tile([P, P], U32, name="w1_codes%d" % t, align_bytes=64)
-            w1_plane = keep.tile([P, P], U8, name="w1_plane%d" % t, align_bytes=64)
-            nc.vector.quantize_mx(
-                out=w1_codes[:].bitcast(FP8X4),
-                scales=w1_plane[:],
-                in_=w1_bf[t].rearrange("p m j -> p (m j)"),
-            )
-            if t == 0:
-                nc.vector.tensor_copy(out=w1_rest[:].rearrange("p t m j -> p m j t"), in_=dealt[:, :, :, 1:PACK])
+            if t == 1:
+                rest_codes = keep.tile([P, (PACK - 1) * P], U32, name="rest_codes", tag="w1_codes", align_bytes=64)
+                rest_flat = w1_rest[:].rearrange("p t m j -> p (t m j)")
+                for a, b in ((0, 1), (1, 3)):
+                    nc.vector.quantize_mx(
+                        out=rest_codes[:, a * P : b * P].bitcast(FP8X4),
+                        scales=w1_planes[:, (a + 1) * P : (b + 1) * P],
+                        in_=rest_flat[:, a * P * PACK : b * P * PACK],
+                    )
+            w1_codes = first_codes[:] if t == 0 else rest_codes[:, (t - 1) * P : t * P]
+            w1_plane = w1_planes[:, t * P : (t + 1) * P]
             h0 = starts[t]
             width = 256 if t == 0 else BANK
             for c0 in range(0, T, width) if t < PACK - 1 else range(T - width, -1, -width):
                 acc = bank(used % BANKS, [P, width], "acc")
                 used = used + 1
-                nc.tensor.matmul_mx(
-                    out=acc[:],
-                    lhsT=w1_codes[:].bitcast(FP8X4),
-                    lhsT_scale=w1_plane[:],
-                    rhs=x_codes[:, c0 : c0 + width].bitcast(FP8X4),
-                    rhs_scale=x_plane[:, c0 : c0 + width],
-                    start=True,
-                    stop=True,
-                )
+                for c in range(c0 // CHUNK, (c0 + width) // CHUNK):
+                    nc.tensor.matmul_mx(
+                        out=acc[:, c * CHUNK - c0 : (c + 1) * CHUNK - c0],
+                        lhsT=w1_codes.bitcast(FP8X4),
+                        lhsT_scale=w1_plane,
+                        rhs=x_codes[c // 2][:, c % 2 * CHUNK : (c % 2 + 1) * CHUNK].bitcast(FP8X4),
+                        rhs_scale=x_plane[4 * c :, :],
+                        start=True,
+                        stop=True,
+                    )
                 nc.scalar.activation(h_all[:, h0 + c0 : h0 + c0 + width], acc[:], ACT.Silu)
 
         rounded = [keep.tile([P, T, PACK], BF16, name="rounded%d" % d, align_bytes=64) for d in range(D)]
-        mean = keep.tile([P, T * PACK], BF16, name="mean", align_bytes=64)
         sums = [bank(b, [P, PACK, P], "sums") for b in range(T // P)]
 
         def fetch(d, v0, n):
@@ -148,9 +170,12 @@ def tile_picked_wpna_silu_l_kernel(
                     backs.append(bank(b, [P, group, 2, P], "back"))
                 for u in range(2):
                     nc.tensor.transpose(backs[-1][:, (b - b0) % group, u, :], pairs[:, u, :], ident[:])
+            return backs
+
+        def lay_out(backs, mean):
             for i, back in enumerate(backs):
-                v0 = (b0 + i * group) * P
-                words = mean[:, v0 * PACK : (v0 + group * P) * PACK].bitcast(F32)
+                group = back.shape[1]
+                words = mean[:, i * group * P * PACK : (i + 1) * group * P * PACK].bitcast(F32)
                 nc.scalar.copy(
                     out=words.rearrange("p (b v u) -> p b v u", b=group, u=2),
                     in_=back[:].rearrange("p b u v -> p b v u"),
@@ -159,66 +184,74 @@ def tile_picked_wpna_silu_l_kernel(
         g_0 = fetch(0, 0, T)
         g_1 = fetch(1, 0, T)
         fetch(2, 0, HALF)
-        turn_back(0, HALF // P, 2)
+        backs = turn_back(0, HALF // P, 2)
         g_last = fetch(2, HALF, T - HALF)
-        turn_back(HALF // P, T // P, 1)
+        mean_a = keep.tile([P, HALF * PACK], BF16, name="mean_a", align_bytes=64)
+        lay_out(backs, mean_a)
+        mean_b = keep.tile([P, HALF * PACK], BF16, name="mean_b", tag="late", align_bytes=64)
+        lay_out(turn_back(HALF // P, T // P, 1), mean_b)
 
         flat = [r[:].rearrange("p v t -> p (v t)") for r in rounded]
         hi = keep.tile([P, T * PACK], BF16, name="hi", align_bytes=64)
         lo = keep.tile([P, T * PACK], BF16, name="lo", align_bytes=64)
         nc.vector.tensor_tensor(hi[:], flat[0], flat[1], ALU.max)
         nc.vector.tensor_tensor(lo[:], flat[0], flat[1], ALU.min)
-        largest = keep.tile([P, T * PACK], BF16, name="largest", align_bytes=64)
-        smallest = keep.tile([P, T * PACK], BF16, name="smallest", align_bytes=64)
-        stats = [mean, largest, smallest]
         z_codes = [keep.tile([P, T], U32, name="z_codes%d" % s, align_bytes=64) for s in range(D)]
         z_plane = [keep.tile([P, T], U8, name="z_plane%d" % s, align_bytes=64) for s in range(D)]
 
-        def compare(v0, n):
+        def compare(op, pair, v0, n, into):
             cols = slice(v0 * PACK, (v0 + n) * PACK)
-            nc.vector.tensor_tensor(largest[:, cols], hi[:, cols], flat[2][:, cols], ALU.max)
-            nc.vector.tensor_tensor(smallest[:, cols], lo[:, cols], flat[2][:, cols], ALU.min)
+            nc.vector.tensor_tensor(into, pair[:, cols], flat[2][:, cols], op)
 
-        def quantise(s, v0, n):
+        def quantise(s, v0, n, values):
             nc.vector.quantize_mx(
-                out=z_codes[s][:, v0 : v0 + n].bitcast(FP8X4),
-                scales=z_plane[s][:, v0 : v0 + n],
-                in_=stats[s][:, v0 * PACK : (v0 + n) * PACK],
+                out=z_codes[s][:, v0 : v0 + n].bitcast(FP8X4), scales=z_plane[s][:, v0 : v0 + n], in_=values
             )
 
-        def multiply(total, s, v0, n):
+        def multiply(total, s, v0, n, start, stop):
             nc.tensor.matmul_mx(
                 out=total[:],
                 lhsT=w_codes[s][:].bitcast(FP4X4),
                 lhsT_scale=w_plane[:, s * N : (s + 1) * N],
                 rhs=z_codes[s][:, v0 : v0 + n].bitcast(FP8X4),
                 rhs_scale=z_plane[s][:, v0 : v0 + n],
-                start=(s == 1),
-                stop=(s == 0),
+                start=start,
+                stop=stop,
             )
 
         result = keep.tile([P, T], F32, name="result", align_bytes=64)
-        compare(0, HALF)
+        largest_a = keep.tile([P, HALF * PACK], BF16, name="largest_a", align_bytes=64)
+        smallest_a = keep.tile([P, HALF * PACK], BF16, name="smallest_a", align_bytes=64)
+        largest_b = keep.tile([P, HALF * PACK], BF16, name="largest_b", align_bytes=64)
+        compare(ALU.max, hi, 0, HALF, largest_a[:])
+        compare(ALU.min, lo, 0, HALF, smallest_a[:])
         total = bank(HALF // P, [P, HALF], "total")
-        for s in (1, 2, 0):
-            quantise(s, 0, HALF)
-            multiply(total, s, 0, HALF)
+        quantise(1, 0, HALF, largest_a[:])
+        multiply(total, 1, 0, HALF, True, False)
+        quantise(2, 0, HALF, smallest_a[:])
+        multiply(total, 2, 0, HALF, False, False)
+        compare(ALU.max, hi, HALF, HALF, largest_b[:])
+        quantise(0, 0, HALF, mean_a[:])
+        multiply(total, 0, 0, HALF, False, True)
         nc.scalar.copy(out=result[:, :HALF], in_=total[:])
         nc.sync.dma_start(out=out[:, :HALF], in_=result[:, :HALF])
 
-        compare(HALF, T - HALF)
-        blocks = range(HALF // P, T // P)
+        blocks = [5, 6, 7, 4]
         totals = {b: bank(b, [P, P], "total") for b in blocks}
-        for s in (1, 2):
-            quantise(s, HALF, T - HALF)
+        for s, values in ((1, largest_b), (0, mean_b)):
+            quantise(s, HALF, HALF, values[:])
             for b in blocks:
-                multiply(totals[b], s, b * P, P)
+                multiply(totals[b], s, b * P, P, s == 1, False)
+        smallest_b = keep.tile([P, HALF * PACK], BF16, name="smallest_b", tag="late", align_bytes=64)
         for v0 in range(HALF, T, 2 * P):
-            quantise(0, v0, 2 * P)
-            for b in (v0 // P, v0 // P + 1):
-                multiply(totals[b], 0, b * P, P)
-                if b == T // P - 1:
+            compare(ALU.min, lo, v0, 2 * P, smallest_b[:, (v0 - HALF) * PACK : (v0 - HALF + 2 * P) * PACK])
+        for v0, n in ((HALF, 2 * P), (T - 2 * P, P), (T - P, P)):
+            quantise(2, v0, n, smallest_b[:, (v0 - HALF) * PACK : (v0 - HALF + n) * PACK])
+            for b in range(v0 // P, (v0 + n) // P):
+                multiply(totals[b], 2, b * P, P, False, True)
+                if n == P:
                     nc.vector.tensor_copy(out=result[:, b * P : (b + 1) * P], in_=totals[b][:])
                 else:
                     nc.scalar.copy(out=result[:, b * P : (b + 1) * P], in_=totals[b][:])
-            nc.sync.dma_start(out=out[:, v0 : v0 + 2 * P], in_=result[:, v0 : v0 + 2 * P])
+            if (v0 + n) % (2 * P) == 0:
+                nc.sync.dma_start(out=out[:, v0 + n - 2 * P : v0 + n], in_=result[:, v0 + n - 2 * P : v0 + n])

@@ -42,11 +42,9 @@ def tile_picked_wpna_silu_l_kernel(
         nc.vector.memset(w_plane[:].bitcast(I32), 0)
 
         w1_rows = w1.rearrange("(p j) c -> p j c", j=PACK)
-        w1_raw = []
+        w1_raw = keep.tile([P, PACK, H], F32, name="w1_raw")
         for a in range(2):
-            raw = keep.tile([P, 2, H], F32, name="w1_raw%d" % a)
-            nc.sync.dma_start(out=raw[:], in_=w1_rows[:, 2 * a : 2 * a + 2, :])
-            w1_raw.append(raw)
+            nc.sync.dma_start(out=w1_raw[:, 2 * a : 2 * a + 2, :], in_=w1_rows[:, 2 * a : 2 * a + 2, :])
         for q in range(4):
             nc.sync.dma_start(
                 out=x_plane[32 * q : 32 * q + 16, :].bitcast(I32),
@@ -87,30 +85,31 @@ def tile_picked_wpna_silu_l_kernel(
         nc.gpsimd.memset(h_all[:, 3 * T : 3 * T + SPARE], 0.0)
         nc.gpsimd.memset(h_all[:, 4 * T + SPARE :], 0.0)
 
+        warm = keep.tile([P, 1], F32, name="warm")
+        nc.scalar.activation(warm[:], h_all[:, 3 * T : 3 * T + 1], ACT.Silu)
         w1_first = keep.tile([P, P, PACK], BF16, name="w1_first", tag="w1_bf", align_bytes=64)
-        w1_rest = keep.tile([P, PACK - 1, P, PACK], BF16, name="w1_rest", tag="w1_bf", align_bytes=64)
-        dealt = [raw[:].rearrange("p j (m t) -> p m j t", t=PACK) for raw in w1_raw]
+        w1_mid = keep.tile([P, 2, P, PACK], BF16, name="w1_mid", align_bytes=64)
+        w1_last = keep.tile([P, P, PACK], BF16, name="w1_last", tag="w1_bf", align_bytes=64)
+        dealt = w1_raw[:].rearrange("p j (m t) -> p m j t", t=PACK)
         for a in range(2):
-            nc.vector.tensor_copy(out=w1_first[:, :, 2 * a : 2 * a + 2], in_=dealt[a][:, :, :, 0])
+            nc.vector.tensor_copy(out=w1_first[:, :, 2 * a : 2 * a + 2], in_=dealt[:, :, 2 * a : 2 * a + 2, 0])
         first_codes = keep.tile([P, P], U32, name="first_codes", tag="w1_codes", align_bytes=64)
         w1_planes = keep.tile([P, PACK * P], U8, name="w1_planes", align_bytes=64)
         nc.vector.quantize_mx(
             out=first_codes[:].bitcast(FP8X4), scales=w1_planes[:, :P], in_=w1_first[:].rearrange("p m j -> p (m j)")
         )
-        for a in range(2):
-            nc.vector.tensor_copy(
-                out=w1_rest[:, :, :, 2 * a : 2 * a + 2].rearrange("p t m j -> p m j t"), in_=dealt[a][:, :, :, 1:PACK]
-            )
+        nc.scalar.copy(out=w1_mid[:].rearrange("p t m j -> p m j t"), in_=dealt[:, :, :, 1:3])
+        nc.vector.tensor_copy(out=w1_last[:], in_=dealt[:, :, :, 3])
         used = 0
         for t in range(PACK):
             if t == 1:
                 rest_codes = keep.tile([P, (PACK - 1) * P], U32, name="rest_codes", tag="w1_codes", align_bytes=64)
-                rest_flat = w1_rest[:].rearrange("p t m j -> p (t m j)")
-                for a, b in ((0, 1), (1, 3)):
+                mid = w1_mid[:].rearrange("p t m j -> p (t m j)")
+                for a, b, flat_in in ((0, 2, mid), (2, 3, w1_last[:].rearrange("p m j -> p (m j)"))):
                     nc.vector.quantize_mx(
                         out=rest_codes[:, a * P : b * P].bitcast(FP8X4),
                         scales=w1_planes[:, (a + 1) * P : (b + 1) * P],
-                        in_=rest_flat[:, a * P * PACK : b * P * PACK],
+                        in_=flat_in,
                     )
             w1_codes = first_codes[:] if t == 0 else rest_codes[:, (t - 1) * P : t * P]
             w1_plane = w1_planes[:, t * P : (t + 1) * P]
@@ -131,77 +130,86 @@ def tile_picked_wpna_silu_l_kernel(
                     )
                 nc.scalar.activation(h_all[:, h0 + c0 : h0 + c0 + width], acc[:], ACT.Silu)
 
-        rounded = [keep.tile([P, T, PACK], BF16, name="rounded%d" % d, align_bytes=64) for d in range(D)]
-        sums = [bank(b, [P, PACK, P], "sums") for b in range(T // P)]
-
         def fetch(d, v0, n):
             g = keep.tile([P, PACK, n], F32, name="g%d_%d" % (d, v0), align_bytes=64)
             for t in range(PACK):
                 h0 = starts[t]
                 h1 = h0 + T + SPARE if d == 0 or t == PACK - 1 else starts[PACK - 1] + 8
-                nc.vector.tensor_copy(
-                    g[:, t, :],
-                    h_all[:, h0:h1].indirect(lists[d][:, v0 // 16 : (v0 + n) // 16]),
-                )
-                for b in range(v0 // P, (v0 + n) // P):
-                    nc.tensor.matmul(
-                        sums[b][:, t, :],
-                        lhsT=g[:, t, b * P - v0 : (b + 1) * P - v0],
-                        rhs=ident[:],
-                        start=(d == 0 and t == 0),
-                        stop=(d == D - 1 and t == PACK - 1),
-                        is_transpose=True,
-                    )
-            nc.scalar.copy(
-                out=rounded[d][:, v0 : v0 + n, :].rearrange("p (c i) t -> p c t i", i=4),
-                in_=g[:].rearrange("p t (c i) -> p c t i", i=4),
-            )
+                nc.vector.tensor_copy(g[:, t, :], h_all[:, h0:h1].indirect(lists[d][:, v0 // 16 : (v0 + n) // 16]))
             return g
 
-        def turn_back(b0, b1, group):
+        def round_off(parts, tag):
+            n = parts[0].shape[2]
+            rounded = keep.tile([P, n * len(parts), PACK], BF16, name="rounded", tag=tag, align_bytes=64)
+            for i, g in enumerate(parts):
+                nc.scalar.copy(
+                    out=rounded[:, i * n : (i + 1) * n, :].rearrange("p (c i) t -> p c t i", i=4),
+                    in_=g[:].rearrange("p t (c i) -> p c t i", i=4),
+                )
+            return rounded[:].rearrange("p v t -> p (v t)")
+
+        def add_up(parts):
+            sums = [bank(b, [P, PACK, P], "sums") for b in range(HALF // P)]
+            for d, part in enumerate(parts):
+                for t in range(PACK):
+                    for b in range(HALF // P):
+                        nc.tensor.matmul(
+                            sums[b][:, t, :],
+                            lhsT=part[:, t, b * P : (b + 1) * P],
+                            rhs=ident[:],
+                            start=(d == 0 and t == 0),
+                            stop=(d == D - 1 and t == PACK - 1),
+                            is_transpose=True,
+                        )
+            return sums
+
+        def turn_back(sums, first_bank, tag):
             backs = []
-            for b in range(b0, b1):
-                turned = ring.tile([P, 2, P, 2], BF16, name="turned", tag="turned", bufs=4, align_bytes=64)
+            for b, total in enumerate(sums):
+                turned = keep.tile([P, 2, P, 2], BF16, name="turned", tag="%s%d" % (tag, b), align_bytes=64)
                 nc.scalar.activation(
-                    turned[:], sums[b][:].rearrange("v (u e) p -> v u p e", e=2), ACT.Copy, scale=1.0 / D
+                    turned[:], total[:].rearrange("v (u e) p -> v u p e", e=2), ACT.Copy, scale=1.0 / D
                 )
                 pairs = turned[:].rearrange("v u p e -> v u (p e)").bitcast(F32)
-                if (b - b0) % group == 0:
-                    backs.append(bank(b, [P, group, 2, P], "back"))
+                if b % 2 == 0:
+                    backs.append(bank(first_bank + b // 2, [P, 2, 2, P], "back"))
                 for u in range(2):
-                    nc.tensor.transpose(backs[-1][:, (b - b0) % group, u, :], pairs[:, u, :], ident[:])
+                    nc.tensor.transpose(backs[-1][:, b % 2, u, :], pairs[:, u, :], ident[:])
             return backs
 
         def lay_out(backs, mean):
             for i, back in enumerate(backs):
-                group = back.shape[1]
-                words = mean[:, i * group * P * PACK : (i + 1) * group * P * PACK].bitcast(F32)
+                words = mean[:, i * 2 * P * PACK : (i + 1) * 2 * P * PACK].bitcast(F32)
                 nc.scalar.copy(
-                    out=words.rearrange("p (b v u) -> p b v u", b=group, u=2),
+                    out=words.rearrange("p (b v u) -> p b v u", b=2, u=2),
                     in_=back[:].rearrange("p b u v -> p b v u"),
                 )
 
         g_0 = fetch(0, 0, T)
-        g_1 = fetch(1, 0, T)
-        fetch(2, 0, HALF)
-        backs = turn_back(0, HALF // P, 2)
-        g_last = fetch(2, HALF, T - HALF)
+        r_0 = round_off([g_0], "r0")
+        g_a = [fetch(d, 0, HALF) for d in (1, 2)]
+        r_2a = round_off([g_a[1]], "r2a")
+        backs = turn_back(add_up([g_0[:, :, :HALF]] + g_a), 4, "early")
         mean_a = keep.tile([P, HALF * PACK], BF16, name="mean_a", align_bytes=64)
         lay_out(backs, mean_a)
-        mean_b = keep.tile([P, HALF * PACK], BF16, name="mean_b", tag="late", align_bytes=64)
-        lay_out(turn_back(HALF // P, T // P, 1), mean_b)
+        g_b = [fetch(d, HALF, HALF) for d in (1, 2)]
+        r_1 = round_off([g_a[0], g_b[0]], "early0")
+        r_2b = round_off([g_b[1]], "early3")
+        g_last = g_b[1]
+        mean_b = keep.tile([P, HALF * PACK], BF16, name="mean_b", align_bytes=64)
+        lay_out(turn_back(add_up([g_0[:, :, HALF:]] + g_b), 6, "late"), mean_b)
 
-        flat = [r[:].rearrange("p v t -> p (v t)") for r in rounded]
         hi = keep.tile([P, T * PACK], BF16, name="hi", align_bytes=64)
         lo = keep.tile([P, T * PACK], BF16, name="lo", align_bytes=64)
-        nc.vector.tensor_tensor(hi[:], flat[0], flat[1], ALU.max)
-        nc.vector.tensor_tensor(lo[:], flat[0], flat[1], ALU.min)
+        nc.vector.tensor_tensor(hi[:], r_0, r_1, ALU.max)
+        nc.vector.tensor_tensor(lo[:], r_0, r_1, ALU.min)
         z_codes = [keep.tile([P, T], U32, name="z_codes%d" % s, align_bytes=64) for s in range(D)]
         z_plane = [keep.tile([P, T], U8, name="z_plane%d" % s, align_bytes=64) for s in range(D)]
 
         def compare(op, pair, v0, n, into):
             cols = slice(v0 * PACK, (v0 + n) * PACK)
-            nc.vector.tensor_tensor(into, pair[:, cols], flat[2][:, cols], op)
+            third = (r_2a, r_2b)[v0 // HALF][:, v0 % HALF * PACK : (v0 % HALF + n) * PACK]
+            nc.vector.tensor_tensor(into, pair[:, cols], third, op)
 
         def quantise(s, v0, n, values):
             nc.vector.quantize_mx(
@@ -225,25 +233,25 @@ def tile_picked_wpna_silu_l_kernel(
         largest_b = keep.tile([P, HALF * PACK], BF16, name="largest_b", align_bytes=64)
         compare(ALU.max, hi, 0, HALF, largest_a[:])
         compare(ALU.min, lo, 0, HALF, smallest_a[:])
-        total = bank(HALF // P, [P, HALF], "total")
+        total = bank(6, [P, HALF], "total")
         quantise(1, 0, HALF, largest_a[:])
         multiply(total, 1, 0, HALF, True, False)
         quantise(2, 0, HALF, smallest_a[:])
         multiply(total, 2, 0, HALF, False, False)
-        compare(ALU.max, hi, HALF, HALF, largest_b[:])
         quantise(0, 0, HALF, mean_a[:])
         multiply(total, 0, 0, HALF, False, True)
         nc.scalar.copy(out=result[:, :HALF], in_=total[:])
         nc.sync.dma_start(out=out[:, :HALF], in_=result[:, :HALF])
 
-        blocks = [5, 6, 7, 4]
-        totals = {b: bank(b, [P, P], "total") for b in blocks}
-        for s, values in ((1, largest_b), (0, mean_b)):
+        blocks = [4, 5, 6, 7]
+        totals = {b: bank(b - 4, [P, P], "total") for b in blocks}
+        smallest_b = keep.tile([P, HALF * PACK], BF16, name="smallest_b", align_bytes=64)
+        compare(ALU.max, hi, HALF, HALF, largest_b[:])
+        for i, (s, values) in enumerate(((0, mean_b), (1, largest_b))):
             quantise(s, HALF, HALF, values[:])
             for b in blocks:
-                multiply(totals[b], s, b * P, P, s == 1, False)
-        smallest_b = keep.tile([P, HALF * PACK], BF16, name="smallest_b", tag="late", align_bytes=64)
-        for v0 in range(HALF, T, 2 * P):
+                multiply(totals[b], s, b * P, P, s == 0, False)
+            v0 = HALF + i * 2 * P
             compare(ALU.min, lo, v0, 2 * P, smallest_b[:, (v0 - HALF) * PACK : (v0 - HALF + 2 * P) * PACK])
         for v0, n in ((HALF, 2 * P), (T - 2 * P, P), (T - P, P)):
             quantise(2, v0, n, smallest_b[:, (v0 - HALF) * PACK : (v0 - HALF + n) * PACK])

@@ -74,9 +74,6 @@ def tile_picked_wpna_silu_l_kernel(
                     in_=scales[0][4 * q : 4 * q + 4, :].bitcast(I32),
                 )
 
-        ident = keep.tile([P, P], F32, name="ident")
-        make_identity(nc, ident[:])
-
         def bank(b, shape, name):
             return psum.tile(shape, F32, name=name, tag="bank%d" % b, bufs=1)
 
@@ -84,6 +81,9 @@ def tile_picked_wpna_silu_l_kernel(
         starts = [2 * T, T, 0, 3 * T + SPARE]
         nc.gpsimd.memset(h_all[:, 3 * T : 3 * T + SPARE], 0.0)
         nc.gpsimd.memset(h_all[:, 4 * T + SPARE :], 0.0)
+
+        ident = keep.tile([P, P], F32, name="ident")
+        make_identity(nc, ident[:])
 
         warm = keep.tile([P, 1], F32, name="warm")
         nc.scalar.activation(warm[:], h_all[:, 3 * T : 3 * T + 1], ACT.Silu)
@@ -93,17 +93,16 @@ def tile_picked_wpna_silu_l_kernel(
         dealt = w1_raw[:].rearrange("p j (m t) -> p m j t", t=PACK)
         for a in range(2):
             nc.vector.tensor_copy(out=w1_first[:, :, 2 * a : 2 * a + 2], in_=dealt[:, :, 2 * a : 2 * a + 2, 0])
-        first_codes = keep.tile([P, P], U32, name="first_codes", tag="w1_codes", align_bytes=64)
+        first_codes = keep.tile([P, P], U32, name="first_codes", align_bytes=64)
         w1_planes = keep.tile([P, PACK * P], U8, name="w1_planes", align_bytes=64)
         nc.vector.quantize_mx(
             out=first_codes[:].bitcast(FP8X4), scales=w1_planes[:, :P], in_=w1_first[:].rearrange("p m j -> p (m j)")
         )
         nc.scalar.copy(out=w1_mid[:].rearrange("p t m j -> p m j t"), in_=dealt[:, :, :, 1:3])
         nc.vector.tensor_copy(out=w1_last[:], in_=dealt[:, :, :, 3])
-        used = 0
         for t in range(PACK):
             if t == 1:
-                rest_codes = keep.tile([P, (PACK - 1) * P], U32, name="rest_codes", tag="w1_codes", align_bytes=64)
+                rest_codes = keep.tile([P, (PACK - 1) * P], U32, name="rest_codes", align_bytes=64)
                 mid = w1_mid[:].rearrange("p t m j -> p (t m j)")
                 for a, b, flat_in in ((0, 2, mid), (2, 3, w1_last[:].rearrange("p m j -> p (m j)"))):
                     nc.vector.quantize_mx(
@@ -115,9 +114,8 @@ def tile_picked_wpna_silu_l_kernel(
             w1_plane = w1_planes[:, t * P : (t + 1) * P]
             h0 = starts[t]
             width = 256 if t == 0 else BANK
-            for c0 in range(0, T, width) if t < PACK - 1 else range(T - width, -1, -width):
-                acc = bank(used % BANKS, [P, width], "acc")
-                used = used + 1
+            for c0 in range(0, T, width) if t == 0 else range(T - width, -1, -width):
+                acc = bank(c0 // width if t == 0 else (3 + t if c0 else 2 + (t - 1) % 2), [P, width], "acc")
                 for c in range(c0 // CHUNK, (c0 + width) // CHUNK):
                     nc.tensor.matmul_mx(
                         out=acc[:, c * CHUNK - c0 : (c + 1) * CHUNK - c0],
@@ -130,86 +128,85 @@ def tile_picked_wpna_silu_l_kernel(
                     )
                 nc.scalar.activation(h_all[:, h0 + c0 : h0 + c0 + width], acc[:], ACT.Silu)
 
-        def fetch(d, v0, n):
-            g = keep.tile([P, PACK, n], F32, name="g%d_%d" % (d, v0), align_bytes=64)
+        def fetch(d, t, v0, n, into):
+            h0 = starts[t]
+            h1 = h0 + T + SPARE if d == 0 or t == PACK - 1 else starts[PACK - 1] + 8
+            nc.vector.tensor_copy(into, h_all[:, h0:h1].indirect(lists[d][:, v0 // 16 : (v0 + n) // 16]))
+
+        g = [keep.tile([P, PACK, T], F32, name="g%d" % d, align_bytes=64) for d in range(D - 1)]
+        for d in range(D - 1):
             for t in range(PACK):
-                h0 = starts[t]
-                h1 = h0 + T + SPARE if d == 0 or t == PACK - 1 else starts[PACK - 1] + 8
-                nc.vector.tensor_copy(g[:, t, :], h_all[:, h0:h1].indirect(lists[d][:, v0 // 16 : (v0 + n) // 16]))
-            return g
+                fetch(d, t, 0, T, g[d][:, t, :])
+        g_2 = keep.tile([P, HALF + 6 * T], F32, name="g_2", align_bytes=64)
+        third = [
+            g_2[:, : 4 * T].rearrange("p (u e c) -> p u e c", u=2, e=2)[:, :, :, :HALF],
+            g_2[:, HALF:].rearrange("p (u e c) -> p u e c", u=2, e=3)[:, :, :2, :HALF],
+        ]
+        for t in range(2):
+            fetch(2, t, 0, T, g_2[:, t * T : (t + 1) * T])
+        for i in range(2):
+            for e in range(2):
+                fetch(2, 2 + e, i * HALF, HALF, third[i][:, 1, e, :])
 
-        def round_off(parts, tag):
-            n = parts[0].shape[2]
-            rounded = keep.tile([P, n * len(parts), PACK], BF16, name="rounded", tag=tag, align_bytes=64)
-            for i, g in enumerate(parts):
-                nc.scalar.copy(
-                    out=rounded[:, i * n : (i + 1) * n, :].rearrange("p (c i) t -> p c t i", i=4),
-                    in_=g[:].rearrange("p t (c i) -> p c t i", i=4),
-                )
-            return rounded[:].rearrange("p v t -> p (v t)")
+        rounded = [keep.tile([P, T, PACK], BF16, name="rounded%d" % d, align_bytes=64) for d in range(D)]
+        for d in range(D - 1):
+            nc.scalar.copy(
+                out=rounded[d][:].rearrange("p (c i) t -> p c t i", i=4),
+                in_=g[d][:].rearrange("p t (c i) -> p c t i", i=4),
+            )
+        backs = [bank(4 + j, [P, 2, 2, P], "back") for j in range(4)]
 
-        def add_up(parts):
-            sums = [bank(b, [P, PACK, P], "sums") for b in range(HALF // P)]
-            for d, part in enumerate(parts):
-                for t in range(PACK):
-                    for b in range(HALF // P):
+        def turn_means(u):
+            sums = [bank(j, [P, 2, 2, P], "sums") for j in range(4)]
+            for d in range(D):
+                for e in range(2):
+                    for b in range(T // P):
+                        if d < D - 1:
+                            part = g[d][:, 2 * u + e, b * P : (b + 1) * P]
+                        else:
+                            part = third[b * P // HALF][:, u, e, b * P % HALF : b * P % HALF + P]
                         nc.tensor.matmul(
-                            sums[b][:, t, :],
-                            lhsT=part[:, t, b * P : (b + 1) * P],
+                            sums[b // 2][:, b % 2, e, :],
+                            lhsT=part,
                             rhs=ident[:],
-                            start=(d == 0 and t == 0),
-                            stop=(d == D - 1 and t == PACK - 1),
+                            start=(d == 0 and e == 0 and b % 2 == 0),
+                            stop=(d == D - 1 and e == 1 and b % 2 == 1),
                             is_transpose=True,
                         )
-            return sums
+            for j in range(4):
+                turned = keep.tile([P, 2, P, 2], BF16, name="turned", tag="turned%d%d" % (u, j), align_bytes=64)
+                nc.scalar.activation(turned[:], sums[j][:].rearrange("v b e p -> v b p e"), ACT.Copy, scale=1.0 / D)
+                pairs = turned[:].rearrange("v b p e -> v b (p e)").bitcast(F32)
+                for b in range(2):
+                    nc.tensor.transpose(backs[j][:, b, u, :], pairs[:, b, :], ident[:])
 
-        def turn_back(sums, first_bank, tag):
-            backs = []
-            for b, total in enumerate(sums):
-                turned = keep.tile([P, 2, P, 2], BF16, name="turned", tag="%s%d" % (tag, b), align_bytes=64)
-                nc.scalar.activation(
-                    turned[:], total[:].rearrange("v (u e) p -> v u p e", e=2), ACT.Copy, scale=1.0 / D
-                )
-                pairs = turned[:].rearrange("v u p e -> v u (p e)").bitcast(F32)
-                if b % 2 == 0:
-                    backs.append(bank(first_bank + b // 2, [P, 2, 2, P], "back"))
-                for u in range(2):
-                    nc.tensor.transpose(backs[-1][:, b % 2, u, :], pairs[:, u, :], ident[:])
-            return backs
+        turn_means(0)
+        for i in range(2):
+            nc.scalar.copy(
+                out=rounded[2][:, i * HALF : (i + 1) * HALF, :].rearrange("p (c i) (u e) -> p c u e i", i=4, u=2),
+                in_=third[i].rearrange("p u e (c i) -> p c u e i", i=4),
+            )
+        turn_means(1)
+        mean = keep.tile([P, T * PACK], BF16, name="mean", align_bytes=64)
+        for j, back in enumerate(backs):
+            words = mean[:, j * 2 * P * PACK : (j + 1) * 2 * P * PACK].bitcast(F32)
+            nc.scalar.copy(
+                out=words.rearrange("p (b v u) -> p b v u", b=2, u=2), in_=back[:].rearrange("p b u v -> p b v u")
+            )
+        mean_a = mean[:, : HALF * PACK]
+        mean_b = mean[:, HALF * PACK :]
 
-        def lay_out(backs, mean):
-            for i, back in enumerate(backs):
-                words = mean[:, i * 2 * P * PACK : (i + 1) * 2 * P * PACK].bitcast(F32)
-                nc.scalar.copy(
-                    out=words.rearrange("p (b v u) -> p b v u", b=2, u=2),
-                    in_=back[:].rearrange("p b u v -> p b v u"),
-                )
-
-        g_0 = fetch(0, 0, T)
-        r_0 = round_off([g_0], "r0")
-        g_a = [fetch(d, 0, HALF) for d in (1, 2)]
-        r_2a = round_off([g_a[1]], "r2a")
-        backs = turn_back(add_up([g_0[:, :, :HALF]] + g_a), 4, "early")
-        mean_a = keep.tile([P, HALF * PACK], BF16, name="mean_a", align_bytes=64)
-        lay_out(backs, mean_a)
-        g_b = [fetch(d, HALF, HALF) for d in (1, 2)]
-        r_1 = round_off([g_a[0], g_b[0]], "early0")
-        r_2b = round_off([g_b[1]], "early3")
-        g_last = g_b[1]
-        mean_b = keep.tile([P, HALF * PACK], BF16, name="mean_b", align_bytes=64)
-        lay_out(turn_back(add_up([g_0[:, :, HALF:]] + g_b), 6, "late"), mean_b)
-
-        hi = keep.tile([P, T * PACK], BF16, name="hi", align_bytes=64)
-        lo = keep.tile([P, T * PACK], BF16, name="lo", align_bytes=64)
-        nc.vector.tensor_tensor(hi[:], r_0, r_1, ALU.max)
-        nc.vector.tensor_tensor(lo[:], r_0, r_1, ALU.min)
+        flat = [r[:].rearrange("p v t -> p (v t)") for r in rounded]
+        hi = keep.tile([P, T * PACK], BF16, name="hi", tag="turned02", align_bytes=64)
+        lo = keep.tile([P, T * PACK], BF16, name="lo", tag="turned03", align_bytes=64)
+        nc.vector.tensor_tensor(hi[:], flat[0], flat[1], ALU.max)
+        nc.vector.tensor_tensor(lo[:], flat[0], flat[1], ALU.min)
         z_codes = [keep.tile([P, T], U32, name="z_codes%d" % s, align_bytes=64) for s in range(D)]
         z_plane = [keep.tile([P, T], U8, name="z_plane%d" % s, align_bytes=64) for s in range(D)]
 
         def compare(op, pair, v0, n, into):
             cols = slice(v0 * PACK, (v0 + n) * PACK)
-            third = (r_2a, r_2b)[v0 // HALF][:, v0 % HALF * PACK : (v0 % HALF + n) * PACK]
-            nc.vector.tensor_tensor(into, pair[:, cols], third, op)
+            nc.vector.tensor_tensor(into, pair[:, cols], flat[2][:, cols], op)
 
         def quantise(s, v0, n, values):
             nc.vector.quantize_mx(
@@ -233,12 +230,13 @@ def tile_picked_wpna_silu_l_kernel(
         largest_b = keep.tile([P, HALF * PACK], BF16, name="largest_b", align_bytes=64)
         compare(ALU.max, hi, 0, HALF, largest_a[:])
         compare(ALU.min, lo, 0, HALF, smallest_a[:])
-        total = bank(6, [P, HALF], "total")
+        total = bank(4, [P, HALF], "total")
         quantise(1, 0, HALF, largest_a[:])
         multiply(total, 1, 0, HALF, True, False)
         quantise(2, 0, HALF, smallest_a[:])
         multiply(total, 2, 0, HALF, False, False)
-        quantise(0, 0, HALF, mean_a[:])
+        compare(ALU.max, hi, HALF, HALF, largest_b[:])
+        quantise(0, 0, HALF, mean_a)
         multiply(total, 0, 0, HALF, False, True)
         nc.scalar.copy(out=result[:, :HALF], in_=total[:])
         nc.sync.dma_start(out=out[:, :HALF], in_=result[:, :HALF])
@@ -246,12 +244,11 @@ def tile_picked_wpna_silu_l_kernel(
         blocks = [4, 5, 6, 7]
         totals = {b: bank(b - 4, [P, P], "total") for b in blocks}
         smallest_b = keep.tile([P, HALF * PACK], BF16, name="smallest_b", align_bytes=64)
-        compare(ALU.max, hi, HALF, HALF, largest_b[:])
-        for i, (s, values) in enumerate(((0, mean_b), (1, largest_b))):
-            quantise(s, HALF, HALF, values[:])
+        for s, values in ((1, largest_b[:]), (0, mean_b)):
+            quantise(s, HALF, HALF, values)
             for b in blocks:
-                multiply(totals[b], s, b * P, P, s == 0, False)
-            v0 = HALF + i * 2 * P
+                multiply(totals[b], s, b * P, P, s == 1, False)
+        for v0 in range(HALF, T, 2 * P):
             compare(ALU.min, lo, v0, 2 * P, smallest_b[:, (v0 - HALF) * PACK : (v0 - HALF + 2 * P) * PACK])
         for v0, n in ((HALF, 2 * P), (T - 2 * P, P), (T - P, P)):
             quantise(2, v0, n, smallest_b[:, (v0 - HALF) * PACK : (v0 - HALF + n) * PACK])

@@ -133,60 +133,42 @@ def tile_picked_wpna_silu_l_kernel(
             h1 = h0 + T + SPARE if d == 0 or t == PACK - 1 else starts[PACK - 1] + 8
             nc.vector.tensor_copy(into, h_all[:, h0:h1].indirect(lists[d][:, v0 // 16 : (v0 + n) // 16]))
 
-        g = [keep.tile([P, PACK, T], F32, name="g%d" % d, align_bytes=64) for d in range(D - 1)]
-        for d in range(D - 1):
+        g = [keep.tile([P, PACK, T], F32, name="g%d" % d, align_bytes=64) for d in range(D)]
+        for d in range(D):
             for t in range(PACK):
                 fetch(d, t, 0, T, g[d][:, t, :])
-        g_2 = keep.tile([P, HALF + 6 * T], F32, name="g_2", align_bytes=64)
-        third = [
-            g_2[:, : 4 * T].rearrange("p (u e c) -> p u e c", u=2, e=2)[:, :, :, :HALF],
-            g_2[:, HALF:].rearrange("p (u e c) -> p u e c", u=2, e=3)[:, :, :2, :HALF],
-        ]
-        for t in range(2):
-            fetch(2, t, 0, T, g_2[:, t * T : (t + 1) * T])
-        for i in range(2):
-            for e in range(2):
-                fetch(2, 2 + e, i * HALF, HALF, third[i][:, 1, e, :])
 
-        rounded = [keep.tile([P, T, PACK], BF16, name="rounded%d" % d, align_bytes=64) for d in range(D)]
+        rounded = [keep.tile([P, T, PACK], BF16, name="rounded%d" % d, align_bytes=64) for d in range(D - 1)]
         for d in range(D - 1):
             nc.scalar.copy(
                 out=rounded[d][:].rearrange("p (c i) t -> p c t i", i=4),
                 in_=g[d][:].rearrange("p t (c i) -> p c t i", i=4),
             )
-        backs = [bank(4 + j, [P, 2, 2, P], "back") for j in range(4)]
-
-        def turn_means(u):
-            sums = [bank(j, [P, 2, 2, P], "sums") for j in range(4)]
-            for d in range(D):
-                for e in range(2):
-                    for b in range(T // P):
-                        if d < D - 1:
-                            part = g[d][:, 2 * u + e, b * P : (b + 1) * P]
-                        else:
-                            part = third[b * P // HALF][:, u, e, b * P % HALF : b * P % HALF + P]
-                        nc.tensor.matmul(
-                            sums[b // 2][:, b % 2, e, :],
-                            lhsT=part,
-                            rhs=ident[:],
-                            start=(d == 0 and e == 0 and b % 2 == 0),
-                            stop=(d == D - 1 and e == 1 and b % 2 == 1),
-                            is_transpose=True,
-                        )
+        sums = [[bank(4 * u + j, [P, 2, 2, P], "sums") for j in range(4)] for u in range(2)]
+        for d in range(D):
+            for t in range(PACK):
+                u, e = divmod(t, 2)
+                for b in range(T // P):
+                    nc.tensor.matmul(
+                        sums[u][b // 2][:, b % 2, e, :],
+                        lhsT=g[d][:, t, b * P : (b + 1) * P],
+                        rhs=ident[:],
+                        start=(d == 0 and e == 0 and b % 2 == 0),
+                        stop=(d == D - 1 and e == 1 and b % 2 == 1),
+                        is_transpose=True,
+                    )
+        third = keep.tile([P, 2, T, 2], BF16, name="third", align_bytes=64)
+        backs = []
+        for u in range(2):
+            nc.scalar.copy(out=third[:, u, :, :], in_=g[2][:, 2 * u : 2 * u + 2, :].rearrange("p e v -> p v e"))
             for j in range(4):
                 turned = keep.tile([P, 2, P, 2], BF16, name="turned", tag="turned%d%d" % (u, j), align_bytes=64)
-                nc.scalar.activation(turned[:], sums[j][:].rearrange("v b e p -> v b p e"), ACT.Copy, scale=1.0 / D)
+                nc.scalar.activation(turned[:], sums[u][j][:].rearrange("v b e p -> v b p e"), ACT.Copy, scale=1.0 / D)
                 pairs = turned[:].rearrange("v b p e -> v b (p e)").bitcast(F32)
+                if u == 0:
+                    backs.append(bank(j, [P, 2, 2, P], "back"))
                 for b in range(2):
                     nc.tensor.transpose(backs[j][:, b, u, :], pairs[:, b, :], ident[:])
-
-        turn_means(0)
-        for i in range(2):
-            nc.scalar.copy(
-                out=rounded[2][:, i * HALF : (i + 1) * HALF, :].rearrange("p (c i) (u e) -> p c u e i", i=4, u=2),
-                in_=third[i].rearrange("p u e (c i) -> p c u e i", i=4),
-            )
-        turn_means(1)
         mean = keep.tile([P, T * PACK], BF16, name="mean", align_bytes=64)
         for j, back in enumerate(backs):
             words = mean[:, j * 2 * P * PACK : (j + 1) * 2 * P * PACK].bitcast(F32)
@@ -197,8 +179,8 @@ def tile_picked_wpna_silu_l_kernel(
         mean_b = mean[:, HALF * PACK :]
 
         flat = [r[:].rearrange("p v t -> p (v t)") for r in rounded]
-        hi = keep.tile([P, T * PACK], BF16, name="hi", tag="turned02", align_bytes=64)
-        lo = keep.tile([P, T * PACK], BF16, name="lo", tag="turned03", align_bytes=64)
+        hi = keep.tile([P, T * PACK], BF16, name="hi", align_bytes=64)
+        lo = keep.tile([P, T * PACK], BF16, name="lo", align_bytes=64)
         nc.vector.tensor_tensor(hi[:], flat[0], flat[1], ALU.max)
         nc.vector.tensor_tensor(lo[:], flat[0], flat[1], ALU.min)
         z_codes = [keep.tile([P, T], U32, name="z_codes%d" % s, align_bytes=64) for s in range(D)]
@@ -206,7 +188,12 @@ def tile_picked_wpna_silu_l_kernel(
 
         def compare(op, pair, v0, n, into):
             cols = slice(v0 * PACK, (v0 + n) * PACK)
-            nc.vector.tensor_tensor(into, pair[:, cols], flat[2][:, cols], op)
+            nc.vector.tensor_tensor(
+                into.rearrange("p (v u e) -> p v u e", u=2, e=2),
+                pair[:, cols].rearrange("p (v u e) -> p v u e", u=2, e=2),
+                third[:, :, v0 : v0 + n, :].rearrange("p u v e -> p v u e"),
+                op,
+            )
 
         def quantise(s, v0, n, values):
             nc.vector.quantize_mx(
@@ -230,7 +217,7 @@ def tile_picked_wpna_silu_l_kernel(
         largest_b = keep.tile([P, HALF * PACK], BF16, name="largest_b", align_bytes=64)
         compare(ALU.max, hi, 0, HALF, largest_a[:])
         compare(ALU.min, lo, 0, HALF, smallest_a[:])
-        total = bank(4, [P, HALF], "total")
+        total = bank(1, [P, HALF], "total")
         quantise(1, 0, HALF, largest_a[:])
         multiply(total, 1, 0, HALF, True, False)
         quantise(2, 0, HALF, smallest_a[:])
@@ -242,7 +229,7 @@ def tile_picked_wpna_silu_l_kernel(
         nc.sync.dma_start(out=out[:, :HALF], in_=result[:, :HALF])
 
         blocks = [4, 5, 6, 7]
-        totals = {b: bank(b - 4, [P, P], "total") for b in blocks}
+        totals = {b: bank(b, [P, P], "total") for b in blocks}
         smallest_b = keep.tile([P, HALF * PACK], BF16, name="smallest_b", align_bytes=64)
         for s, values in ((1, largest_b[:]), (0, mean_b)):
             quantise(s, HALF, HALF, values)

@@ -43,8 +43,8 @@ def tile_picked_wpna_silu_l_kernel(
 
         w1_rows = w1.rearrange("(p j) c -> p j c", j=PACK)
         w1_raw = keep.tile([P, PACK, H], F32, name="w1_raw")
-        for a in range(2):
-            nc.sync.dma_start(out=w1_raw[:, 2 * a : 2 * a + 2, :], in_=w1_rows[:, 2 * a : 2 * a + 2, :])
+        for j0, j1 in ((0, 3), (3, 4)):
+            nc.sync.dma_start(out=w1_raw[:, j0:j1, :], in_=w1_rows[:, j0:j1, :])
         for q in range(4):
             nc.sync.dma_start(
                 out=x_plane[32 * q : 32 * q + 16, :].bitcast(I32),
@@ -88,23 +88,23 @@ def tile_picked_wpna_silu_l_kernel(
         warm = keep.tile([P, 1], F32, name="warm")
         nc.scalar.activation(warm[:], h_all[:, 3 * T : 3 * T + 1], ACT.Silu)
         w1_first = keep.tile([P, P, PACK], BF16, name="w1_first", tag="w1_bf", align_bytes=64)
-        w1_mid = keep.tile([P, 2, P, PACK], BF16, name="w1_mid", align_bytes=64)
-        w1_last = keep.tile([P, P, PACK], BF16, name="w1_last", tag="w1_bf", align_bytes=64)
+        w1_mid = keep.tile([P, P, PACK], BF16, name="w1_mid", align_bytes=64)
+        w1_last = keep.tile([P, 2, P, PACK], BF16, name="w1_last", tag="w1_bf", align_bytes=64)
         dealt = w1_raw[:].rearrange("p j (m t) -> p m j t", t=PACK)
-        for a in range(2):
-            nc.vector.tensor_copy(out=w1_first[:, :, 2 * a : 2 * a + 2], in_=dealt[:, :, 2 * a : 2 * a + 2, 0])
+        for j0, j1 in ((0, 3), (3, 4)):
+            nc.vector.tensor_copy(out=w1_first[:, :, j0:j1], in_=dealt[:, :, j0:j1, 0])
         first_codes = keep.tile([P, P], U32, name="first_codes", align_bytes=64)
         w1_planes = keep.tile([P, PACK * P], U8, name="w1_planes", align_bytes=64)
         nc.vector.quantize_mx(
             out=first_codes[:].bitcast(FP8X4), scales=w1_planes[:, :P], in_=w1_first[:].rearrange("p m j -> p (m j)")
         )
-        nc.scalar.copy(out=w1_mid[:].rearrange("p t m j -> p m j t"), in_=dealt[:, :, :, 1:3])
-        nc.vector.tensor_copy(out=w1_last[:], in_=dealt[:, :, :, 3])
+        nc.scalar.copy(out=w1_mid[:], in_=dealt[:, :, :, 1])
+        nc.vector.tensor_copy(out=w1_last[:].rearrange("p t m j -> p m j t"), in_=dealt[:, :, :, 2:4])
         for t in range(PACK):
             if t == 1:
                 rest_codes = keep.tile([P, (PACK - 1) * P], U32, name="rest_codes", align_bytes=64)
-                mid = w1_mid[:].rearrange("p t m j -> p (t m j)")
-                for a, b, flat_in in ((0, 2, mid), (2, 3, w1_last[:].rearrange("p m j -> p (m j)"))):
+                mid = w1_mid[:].rearrange("p m j -> p (m j)")
+                for a, b, flat_in in ((0, 1, mid), (1, 3, w1_last[:].rearrange("p t m j -> p (t m j)"))):
                     nc.vector.quantize_mx(
                         out=rest_codes[:, a * P : b * P].bitcast(FP8X4),
                         scales=w1_planes[:, (a + 1) * P : (b + 1) * P],
@@ -245,5 +245,4 @@ def tile_picked_wpna_silu_l_kernel(
                     nc.vector.tensor_copy(out=result[:, b * P : (b + 1) * P], in_=totals[b][:])
                 else:
                     nc.scalar.copy(out=result[:, b * P : (b + 1) * P], in_=totals[b][:])
-            if (v0 + n) % (2 * P) == 0:
-                nc.sync.dma_start(out=out[:, v0 + n - 2 * P : v0 + n], in_=result[:, v0 + n - 2 * P : v0 + n])
+            nc.sync.dma_start(out=out[:, v0 : v0 + n], in_=result[:, v0 : v0 + n])

@@ -157,90 +157,97 @@ def tile_picked_wpna_silu_l_kernel(
                         stop=(d == D - 1 and e == 1 and b % 2 == 1),
                         is_transpose=True,
                     )
-        third = keep.tile([P, 2, T, 2], BF16, name="third", align_bytes=64)
-        backs = []
-        for u in range(2):
-            nc.scalar.copy(out=third[:, u, :, :], in_=g[2][:, 2 * u : 2 * u + 2, :].rearrange("p e v -> p v e"))
-            for j in range(4):
-                turned = keep.tile([P, 2, P, 2], BF16, name="turned", tag="turned%d%d" % (u, j), align_bytes=64)
-                nc.scalar.activation(turned[:], sums[u][j][:].rearrange("v b e p -> v b p e"), ACT.Copy, scale=1.0 / D)
-                pairs = turned[:].rearrange("v b p e -> v b (p e)").bitcast(F32)
-                if u == 0:
-                    backs.append(bank(j, [P, 2, 2, P], "back"))
-                for b in range(2):
-                    nc.tensor.transpose(backs[j][:, b, u, :], pairs[:, b, :], ident[:])
+        third = keep.tile([P, T, PACK], BF16, name="third", align_bytes=64)
         mean = keep.tile([P, T * PACK], BF16, name="mean", align_bytes=64)
-        for j, back in enumerate(backs):
-            words = mean[:, j * 2 * P * PACK : (j + 1) * 2 * P * PACK].bitcast(F32)
-            nc.scalar.copy(
-                out=words.rearrange("p (b v u) -> p b v u", b=2, u=2), in_=back[:].rearrange("p b u v -> p b v u")
-            )
-        mean_a = mean[:, : HALF * PACK]
-        mean_b = mean[:, HALF * PACK :]
+        backs = [bank(j, [P, 2, 2, P], "back") for j in range(4)]
 
-        flat = [r[:].rearrange("p v t -> p (v t)") for r in rounded]
+        def turn(u, j):
+            turned = keep.tile([P, 2, P, 2], BF16, name="turned", tag="turned%d%d" % (u, j), align_bytes=64)
+            nc.scalar.activation(turned[:], sums[u][j][:].rearrange("v b e p -> v b p e"), ACT.Copy, scale=1.0 / D)
+            pairs = turned[:].rearrange("v b p e -> v b (p e)").bitcast(F32)
+            for b in range(2):
+                nc.tensor.transpose(backs[j][:, b, u, :], pairs[:, b, :], ident[:])
+
+        for j in range(4):
+            turn(0, j)
+        for a in range(2):
+            nc.scalar.copy(
+                out=third[:, a * HALF : (a + 1) * HALF, :].rearrange("p (c i) t -> p c t i", i=4),
+                in_=g[2][:, :, a * HALF : (a + 1) * HALF].rearrange("p t (c i) -> p c t i", i=4),
+            )
+        for a in range(2):
+            for j in (2 * a, 2 * a + 1):
+                turn(1, j)
+            for j in (2 * a, 2 * a + 1):
+                words = mean[:, j * 2 * P * PACK : (j + 1) * 2 * P * PACK].bitcast(F32)
+                nc.scalar.copy(
+                    out=words.rearrange("p (b v u) -> p b v u", b=2, u=2),
+                    in_=backs[j][:].rearrange("p b u v -> p b v u"),
+                )
+
+        flat = [r[:].rearrange("p v t -> p (v t)") for r in rounded + [third]]
         hi = keep.tile([P, T * PACK], BF16, name="hi", align_bytes=64)
         lo = keep.tile([P, T * PACK], BF16, name="lo", align_bytes=64)
         nc.vector.tensor_tensor(hi[:], flat[0], flat[1], ALU.max)
         nc.vector.tensor_tensor(lo[:], flat[0], flat[1], ALU.min)
+        largest = keep.tile([P, T * PACK], BF16, name="largest", align_bytes=64)
+        smallest = keep.tile([P, T * PACK], BF16, name="smallest", align_bytes=64)
+        z = [mean, largest, smallest]
         z_codes = [keep.tile([P, T], U32, name="z_codes%d" % s, align_bytes=64) for s in range(D)]
         z_plane = [keep.tile([P, T], U8, name="z_plane%d" % s, align_bytes=64) for s in range(D)]
 
-        def compare(op, pair, v0, n, into):
+        def compare(s, v0, n):
             cols = slice(v0 * PACK, (v0 + n) * PACK)
-            nc.vector.tensor_tensor(
-                into.rearrange("p (v u e) -> p v u e", u=2, e=2),
-                pair[:, cols].rearrange("p (v u e) -> p v u e", u=2, e=2),
-                third[:, :, v0 : v0 + n, :].rearrange("p u v e -> p v u e"),
-                op,
-            )
+            pair, op = (hi, ALU.max) if s == 1 else (lo, ALU.min)
+            nc.vector.tensor_tensor(z[s][:, cols], pair[:, cols], flat[2][:, cols], op)
 
-        def quantise(s, v0, n, values):
+        def quantise(s, v0, n):
             nc.vector.quantize_mx(
-                out=z_codes[s][:, v0 : v0 + n].bitcast(FP8X4), scales=z_plane[s][:, v0 : v0 + n], in_=values
+                out=z_codes[s][:, v0 : v0 + n].bitcast(FP8X4),
+                scales=z_plane[s][:, v0 : v0 + n],
+                in_=z[s][:, v0 * PACK : (v0 + n) * PACK],
             )
 
-        def multiply(total, s, v0, n, start, stop):
+        def multiply(total, s, v0, n):
             nc.tensor.matmul_mx(
                 out=total[:],
                 lhsT=w_codes[s][:].bitcast(FP4X4),
                 lhsT_scale=w_plane[:, s * N : (s + 1) * N],
                 rhs=z_codes[s][:, v0 : v0 + n].bitcast(FP8X4),
                 rhs_scale=z_plane[s][:, v0 : v0 + n],
-                start=start,
-                stop=stop,
+                start=s == 1,
+                stop=s == 0,
             )
 
         result = keep.tile([P, T], F32, name="result", align_bytes=64)
-        largest_a = keep.tile([P, HALF * PACK], BF16, name="largest_a", align_bytes=64)
-        smallest_a = keep.tile([P, HALF * PACK], BF16, name="smallest_a", align_bytes=64)
-        largest_b = keep.tile([P, HALF * PACK], BF16, name="largest_b", align_bytes=64)
-        compare(ALU.max, hi, 0, HALF, largest_a[:])
-        compare(ALU.min, lo, 0, HALF, smallest_a[:])
         total = bank(1, [P, HALF], "total")
-        quantise(1, 0, HALF, largest_a[:])
-        multiply(total, 1, 0, HALF, True, False)
-        quantise(2, 0, HALF, smallest_a[:])
-        multiply(total, 2, 0, HALF, False, False)
-        compare(ALU.max, hi, HALF, HALF, largest_b[:])
-        quantise(0, 0, HALF, mean_a)
-        multiply(total, 0, 0, HALF, False, True)
+        blocks = range(HALF // P, T // P)
+        totals = {b: bank(b, [P, P], "total") for b in blocks}
+
+        def finish(s, v0, n):
+            quantise(s, v0, n)
+            if v0 < HALF:
+                multiply(total, s, v0, n)
+            else:
+                for b in range(v0 // P, (v0 + n) // P):
+                    multiply(totals[b], s, b * P, P)
+
+        compare(1, 0, HALF)
+        compare(2, 0, HALF)
+        finish(1, 0, HALF)
+        finish(2, 0, HALF)
+        compare(1, HALF, HALF)
+        compare(2, HALF, 2 * P)
+        finish(1, HALF, HALF)
+        finish(0, 0, HALF)
         nc.scalar.copy(out=result[:, :HALF], in_=total[:])
         nc.sync.dma_start(out=out[:, :HALF], in_=result[:, :HALF])
-
-        blocks = [4, 5, 6, 7]
-        totals = {b: bank(b, [P, P], "total") for b in blocks}
-        smallest_b = keep.tile([P, HALF * PACK], BF16, name="smallest_b", align_bytes=64)
-        for s, values in ((1, largest_b[:]), (0, mean_b)):
-            quantise(s, HALF, HALF, values)
-            for b in blocks:
-                multiply(totals[b], s, b * P, P, s == 1, False)
-        for v0 in range(HALF, T, 2 * P):
-            compare(ALU.min, lo, v0, 2 * P, smallest_b[:, (v0 - HALF) * PACK : (v0 - HALF + 2 * P) * PACK])
+        compare(2, T - 2 * P, 2 * P)
+        finish(2, HALF, 2 * P)
+        finish(2, T - 2 * P, 2 * P)
         for v0, n in ((HALF, 2 * P), (T - 2 * P, P), (T - P, P)):
-            quantise(2, v0, n, smallest_b[:, (v0 - HALF) * PACK : (v0 - HALF + n) * PACK])
+            finish(0, v0, n)
             for b in range(v0 // P, (v0 + n) // P):
-                multiply(totals[b], 2, b * P, P, False, True)
                 if n == P:
                     nc.vector.tensor_copy(out=result[:, b * P : (b + 1) * P], in_=totals[b][:])
                 else:

@@ -138,12 +138,16 @@ def tile_picked_wpna_silu_l_kernel(
             for t in range(PACK):
                 fetch(d, t, 0, T, g[d][:, t, :])
 
-        rounded = [keep.tile([P, T, PACK], BF16, name="rounded%d" % d, align_bytes=64) for d in range(D - 1)]
-        for d in range(D - 1):
+        rounded = [keep.tile([P, 2, T, 2], BF16, name="rounded%d" % d, align_bytes=64) for d in range(D)]
+
+        def round_pair(d, u, v0, n):
             nc.scalar.copy(
-                out=rounded[d][:].rearrange("p (c i) t -> p c t i", i=4),
-                in_=g[d][:].rearrange("p t (c i) -> p c t i", i=4),
+                out=rounded[d][:, u, v0 : v0 + n, :].rearrange("p (c i) e -> p c e i", i=4),
+                in_=g[d][:, 2 * u : 2 * u + 2, v0 : v0 + n].rearrange("p e (c i) -> p c e i", i=4),
             )
+
+        for d, u in ((0, 0), (0, 1), (1, 0), (1, 1), (2, 0)):
+            round_pair(d, u, 0, T)
         sums = [[bank(4 * u + j, [P, 2, 2, P], "sums") for j in range(4)] for u in range(2)]
         for d in range(D):
             for t in range(PACK):
@@ -157,7 +161,6 @@ def tile_picked_wpna_silu_l_kernel(
                         stop=(d == D - 1 and e == 1 and b % 2 == 1),
                         is_transpose=True,
                     )
-        third = keep.tile([P, T, PACK], BF16, name="third", align_bytes=64)
         mean = keep.tile([P, T * PACK], BF16, name="mean", align_bytes=64)
         backs = [bank(j, [P, 2, 2, P], "back") for j in range(4)]
 
@@ -171,10 +174,7 @@ def tile_picked_wpna_silu_l_kernel(
         for j in range(4):
             turn(0, j)
         for a in range(2):
-            nc.scalar.copy(
-                out=third[:, a * HALF : (a + 1) * HALF, :].rearrange("p (c i) t -> p c t i", i=4),
-                in_=g[2][:, :, a * HALF : (a + 1) * HALF].rearrange("p t (c i) -> p c t i", i=4),
-            )
+            round_pair(2, 1, a * HALF, HALF)
         for a in range(2):
             for j in (2 * a, 2 * a + 1):
                 turn(1, j)
@@ -185,7 +185,7 @@ def tile_picked_wpna_silu_l_kernel(
                     in_=backs[j][:].rearrange("p b u v -> p b v u"),
                 )
 
-        flat = [r[:].rearrange("p v t -> p (v t)") for r in rounded + [third]]
+        flat = [r[:].rearrange("p u v e -> p (u v e)") for r in rounded]
         hi = keep.tile([P, T * PACK], BF16, name="hi", align_bytes=64)
         lo = keep.tile([P, T * PACK], BF16, name="lo", align_bytes=64)
         nc.vector.tensor_tensor(hi[:], flat[0], flat[1], ALU.max)
@@ -199,7 +199,12 @@ def tile_picked_wpna_silu_l_kernel(
         def compare(s, v0, n):
             cols = slice(v0 * PACK, (v0 + n) * PACK)
             pair, op = (hi, ALU.max) if s == 1 else (lo, ALU.min)
-            nc.vector.tensor_tensor(z[s][:, cols], pair[:, cols], flat[2][:, cols], op)
+            nc.vector.tensor_tensor(
+                z[s][:, cols].rearrange("p (v u e) -> p v u e", u=2, e=2),
+                pair[:].rearrange("p (u v e) -> p v u e", u=2, e=2)[:, v0 : v0 + n],
+                rounded[2][:].rearrange("p u v e -> p v u e")[:, v0 : v0 + n],
+                op,
+            )
 
         def quantise(s, v0, n):
             nc.vector.quantize_mx(

@@ -25,6 +25,7 @@ BANKS = 8
 CHUNK = 256
 HALF = 512
 SPARE = 352
+SHARE = 384
 
 
 def tile_picked_wpna_silu_l_kernel(
@@ -33,7 +34,6 @@ def tile_picked_wpna_silu_l_kernel(
     nc = tc.nc
     with ExitStack() as ctx:
         keep = ctx.enter_context(tc.tile_pool(name="keep", bufs=1))
-        ring = ctx.enter_context(tc.tile_pool(name="ring", bufs=2))
         psum = ctx.enter_context(tc.psum_pool(name="psum", bufs=2))
 
         x_plane = keep.tile([P, CHUNK], U8, name="x_plane", align_bytes=64)
@@ -130,13 +130,35 @@ def tile_picked_wpna_silu_l_kernel(
 
         def fetch(d, t, v0, n, into):
             h0 = starts[t]
-            h1 = h0 + T + SPARE if d == 0 or t == PACK - 1 else starts[PACK - 1] + 8
+            h1 = h0 + T + SPARE if d < D - 1 or t == PACK - 1 else starts[PACK - 1] + 8
             nc.vector.tensor_copy(into, h_all[:, h0:h1].indirect(lists[d][:, v0 // 16 : (v0 + n) // 16]))
 
         g = [keep.tile([P, PACK, T], F32, name="g%d" % d, align_bytes=64) for d in range(D)]
-        for d in range(D):
-            for t in range(PACK):
-                fetch(d, t, 0, T, g[d][:, t, :])
+        order = [(d, t) for t in range(PACK) for d in range(D - 1)] + [(D - 1, t) for t in range(PACK)]
+        for d, t in order:
+            fetch(d, t, 0, T, g[d][:, t, :])
+
+        hi = keep.tile([P, T * PACK], BF16, name="hi", align_bytes=64)
+        lo = keep.tile([P, T * PACK], BF16, name="lo", align_bytes=64)
+        kept = [keep.tile([P, 2, SHARE], F32, name="kept%d" % i, align_bytes=64) for i in range(2)]
+        rest = [keep.tile([P, 2, SHARE], F32, name="rest%d" % i, align_bytes=64) for i in range(2)]
+        for t in range(2):
+            pair = [g[d][:, t, :SHARE] for d in range(2)]
+            apart = keep.tile([P, SHARE], F32, name="apart", align_bytes=64)
+            ahead = keep.tile([P, SHARE], F32, name="ahead", align_bytes=64)
+            nc.gpsimd.tensor_tensor(apart[:], pair[0], pair[1], ALU.subtract)
+            nc.gpsimd.tensor_scalar(ahead[:], apart[:], 0.0, 1.0, ALU.is_ge, ALU.mult)
+            for i in range(2):
+                nc.gpsimd.tensor_tensor(kept[i][:, t, :], ahead[:], pair[i], ALU.mult)
+            for i in range(2):
+                nc.gpsimd.tensor_tensor(rest[i][:, t, :], pair[i], kept[i][:, t, :], ALU.subtract)
+        for i, into in enumerate((hi, lo)):
+            nc.gpsimd.tensor_tensor(
+                into[:, : 2 * SHARE].rearrange("p (v e) -> p v e", e=2),
+                kept[i][:].rearrange("p e v -> p v e"),
+                rest[1 - i][:].rearrange("p e v -> p v e"),
+                ALU.add,
+            )
 
         rounded = [keep.tile([P, 2, T, 2], BF16, name="rounded%d" % d, align_bytes=64) for d in range(D)]
 
@@ -146,21 +168,22 @@ def tile_picked_wpna_silu_l_kernel(
                 in_=g[d][:, 2 * u : 2 * u + 2, v0 : v0 + n].rearrange("p e (c i) -> p c e i", i=4),
             )
 
-        for d, u in ((0, 0), (0, 1), (1, 0), (1, 1), (2, 0)):
+        for d in range(2):
+            round_pair(d, 0, SHARE, T - SHARE)
+        for d, u in ((0, 1), (1, 1), (2, 0)):
             round_pair(d, u, 0, T)
         sums = [[bank(4 * u + j, [P, 2, 2, P], "sums") for j in range(4)] for u in range(2)]
-        for d in range(D):
-            for t in range(PACK):
-                u, e = divmod(t, 2)
-                for b in range(T // P):
-                    nc.tensor.matmul(
-                        sums[u][b // 2][:, b % 2, e, :],
-                        lhsT=g[d][:, t, b * P : (b + 1) * P],
-                        rhs=ident[:],
-                        start=(d == 0 and e == 0 and b % 2 == 0),
-                        stop=(d == D - 1 and e == 1 and b % 2 == 1),
-                        is_transpose=True,
-                    )
+        for d, t in order:
+            u, e = divmod(t, 2)
+            for b in range(T // P):
+                nc.tensor.matmul(
+                    sums[u][b // 2][:, b % 2, e, :],
+                    lhsT=g[d][:, t, b * P : (b + 1) * P],
+                    rhs=ident[:],
+                    start=(d == 0 and e == 0 and b % 2 == 0),
+                    stop=(d == D - 1 and e == 1 and b % 2 == 1),
+                    is_transpose=True,
+                )
         mean = keep.tile([P, T * PACK], BF16, name="mean", align_bytes=64)
         backs = [bank(j, [P, 2, 2, P], "back") for j in range(4)]
 
@@ -186,10 +209,8 @@ def tile_picked_wpna_silu_l_kernel(
                 )
 
         flat = [r[:].rearrange("p u v e -> p (u v e)") for r in rounded]
-        hi = keep.tile([P, T * PACK], BF16, name="hi", align_bytes=64)
-        lo = keep.tile([P, T * PACK], BF16, name="lo", align_bytes=64)
-        nc.vector.tensor_tensor(hi[:], flat[0], flat[1], ALU.max)
-        nc.vector.tensor_tensor(lo[:], flat[0], flat[1], ALU.min)
+        nc.vector.tensor_tensor(hi[:, 2 * SHARE :], flat[0][:, 2 * SHARE :], flat[1][:, 2 * SHARE :], ALU.max)
+        nc.vector.tensor_tensor(lo[:, 2 * SHARE :], flat[0][:, 2 * SHARE :], flat[1][:, 2 * SHARE :], ALU.min)
         largest = keep.tile([P, T * PACK], BF16, name="largest", align_bytes=64)
         smallest = keep.tile([P, T * PACK], BF16, name="smallest", align_bytes=64)
         z = [mean, largest, smallest]

@@ -21,11 +21,9 @@ ALU = mybir.AluOpType
 P = 128
 PACK = 4
 BANK = 512
-BANKS = 8
 CHUNK = 256
 HALF = 512
 SPARE = 352
-SHARE = 384
 
 
 def tile_picked_wpna_silu_l_kernel(
@@ -34,7 +32,7 @@ def tile_picked_wpna_silu_l_kernel(
     nc = tc.nc
     with ExitStack() as ctx:
         keep = ctx.enter_context(tc.tile_pool(name="keep", bufs=1))
-        psum = ctx.enter_context(tc.psum_pool(name="psum", bufs=2))
+        psum = ctx.enter_context(tc.psum_pool(name="psum", bufs=1))
 
         x_plane = keep.tile([P, CHUNK], U8, name="x_plane", align_bytes=64)
         w_plane = keep.tile([P, D * N], U8, name="w_plane", align_bytes=64)
@@ -53,7 +51,7 @@ def tile_picked_wpna_silu_l_kernel(
         x_flat = x_words[0].rearrange("p n r -> p (n r)")
         x_codes = []
         for a in range(T // BANK):
-            codes = keep.tile([P, BANK], U32, name="x_codes%d" % a, align_bytes=64)
+            codes = keep.tile([P, BANK], U32, name="x_codes", tag="x_codes%d" % a, align_bytes=64)
             nc.sync.dma_start(
                 out=codes[:].bitcast(I32), in_=x_flat[:, PACK * BANK * a : PACK * BANK * (a + 1)].bitcast(I32)
             )
@@ -75,18 +73,17 @@ def tile_picked_wpna_silu_l_kernel(
                 )
 
         def bank(b, shape, name):
-            return psum.tile(shape, F32, name=name, tag="bank%d" % b, bufs=1)
+            return psum.tile(shape, F32, name=name, tag="bank%d" % b)
 
-        h_all = keep.tile([P, PACK * T + 2 * SPARE], F32, name="h_all", align_bytes=64)
-        starts = [2 * T, T, 0, 3 * T + SPARE]
-        nc.gpsimd.memset(h_all[:, 3 * T : 3 * T + SPARE], 0.0)
-        nc.gpsimd.memset(h_all[:, 4 * T + SPARE :], 0.0)
+        h = [keep.tile([P, T + SPARE], F32, name="h%d" % t, align_bytes=64) for t in range(PACK)]
+        for t in range(PACK):
+            nc.gpsimd.memset(h[t][:, T:], 0.0)
 
         ident = keep.tile([P, P], F32, name="ident")
         make_identity(nc, ident[:])
 
         warm = keep.tile([P, 1], F32, name="warm")
-        nc.scalar.activation(warm[:], h_all[:, 3 * T : 3 * T + 1], ACT.Silu)
+        nc.scalar.activation(warm[:], h[0][:, T : T + 1], ACT.Silu)
         w1_first = keep.tile([P, P, PACK], BF16, name="w1_first", tag="w1_bf", align_bytes=64)
         w1_mid = keep.tile([P, P, PACK], BF16, name="w1_mid", align_bytes=64)
         w1_last = keep.tile([P, 2, P, PACK], BF16, name="w1_last", tag="w1_bf", align_bytes=64)
@@ -112,10 +109,9 @@ def tile_picked_wpna_silu_l_kernel(
                     )
             w1_codes = first_codes[:] if t == 0 else rest_codes[:, (t - 1) * P : t * P]
             w1_plane = w1_planes[:, t * P : (t + 1) * P]
-            h0 = starts[t]
             width = 256 if t == 0 else BANK
-            for c0 in range(0, T, width) if t == 0 else range(T - width, -1, -width):
-                acc = bank(c0 // width if t == 0 else (3 + t if c0 else 2 + (t - 1) % 2), [P, width], "acc")
+            for c0 in range(0, T, width):
+                acc = bank(c0 // width if t == 0 else 4 + (2 * (t - 1) + c0 // width) % 4, [P, width], "acc")
                 for c in range(c0 // CHUNK, (c0 + width) // CHUNK):
                     nc.tensor.matmul_mx(
                         out=acc[:, c * CHUNK - c0 : (c + 1) * CHUNK - c0],
@@ -126,66 +122,62 @@ def tile_picked_wpna_silu_l_kernel(
                         start=True,
                         stop=True,
                     )
-                nc.scalar.activation(h_all[:, h0 + c0 : h0 + c0 + width], acc[:], ACT.Silu)
+                nc.scalar.activation(h[t][:, c0 : c0 + width], acc[:], ACT.Silu)
 
-        def fetch(d, t, v0, n, into):
-            h0 = starts[t]
-            h1 = h0 + T + SPARE if d < D - 1 or t == PACK - 1 else starts[PACK - 1] + 8
-            nc.vector.tensor_copy(into, h_all[:, h0:h1].indirect(lists[d][:, v0 // 16 : (v0 + n) // 16]))
-
-        g = [keep.tile([P, PACK, T], F32, name="g%d" % d, align_bytes=64) for d in range(D)]
-        order = [(d, t) for t in range(PACK) for d in range(D - 1)] + [(D - 1, t) for t in range(PACK)]
-        for d, t in order:
-            fetch(d, t, 0, T, g[d][:, t, :])
-
-        hi = keep.tile([P, T * PACK], BF16, name="hi", align_bytes=64)
-        lo = keep.tile([P, T * PACK], BF16, name="lo", align_bytes=64)
-        kept = [keep.tile([P, 2, SHARE], F32, name="kept%d" % i, align_bytes=64) for i in range(2)]
-        rest = [keep.tile([P, 2, SHARE], F32, name="rest%d" % i, align_bytes=64) for i in range(2)]
-        for t in range(2):
-            pair = [g[d][:, t, :SHARE] for d in range(2)]
-            apart = keep.tile([P, SHARE], F32, name="apart", align_bytes=64)
-            ahead = keep.tile([P, SHARE], F32, name="ahead", align_bytes=64)
-            nc.gpsimd.tensor_tensor(apart[:], pair[0], pair[1], ALU.subtract)
-            nc.gpsimd.tensor_scalar(ahead[:], apart[:], 0.0, 1.0, ALU.is_ge, ALU.mult)
-            for i in range(2):
-                nc.gpsimd.tensor_tensor(kept[i][:, t, :], ahead[:], pair[i], ALU.mult)
-            for i in range(2):
-                nc.gpsimd.tensor_tensor(rest[i][:, t, :], pair[i], kept[i][:, t, :], ALU.subtract)
-        for i, into in enumerate((hi, lo)):
-            nc.gpsimd.tensor_tensor(
-                into[:, : 2 * SHARE].rearrange("p (v e) -> p v e", e=2),
-                kept[i][:].rearrange("p e v -> p v e"),
-                rest[1 - i][:].rearrange("p e v -> p v e"),
-                ALU.add,
-            )
-
-        rounded = [keep.tile([P, 2, T, 2], BF16, name="rounded%d" % d, align_bytes=64) for d in range(D)]
-
-        def round_pair(d, u, v0, n):
-            nc.scalar.copy(
-                out=rounded[d][:, u, v0 : v0 + n, :].rearrange("p (c i) e -> p c e i", i=4),
-                in_=g[d][:, 2 * u : 2 * u + 2, v0 : v0 + n].rearrange("p e (c i) -> p c e i", i=4),
-            )
-
-        for d in range(2):
-            round_pair(d, 0, SHARE, T - SHARE)
-        for d, u in ((0, 1), (1, 1), (2, 0)):
-            round_pair(d, u, 0, T)
+        g = [[keep.tile([P, 2, T], F32, name="g%d%d" % (d, u), align_bytes=64) for u in range(2)] for d in range(2)]
+        third = [
+            [
+                keep.tile([P, 2, HALF], F32, name="third", tag=("x_codes%d" if u == 0 else "third%d") % a, align_bytes=64)
+                for u in range(2)
+            ]
+            for a in range(2)
+        ]
         sums = [[bank(4 * u + j, [P, 2, 2, P], "sums") for j in range(4)] for u in range(2)]
-        for d, t in order:
+
+        def fetch(on_vector, d, t, v0, n):
             u, e = divmod(t, 2)
-            for b in range(T // P):
+            into = g[d][u][:, e, :] if d < 2 else third[v0 // HALF][u][:, e, :]
+            picked = h[t][:].indirect(lists[d][:, v0 // 16 : (v0 + n) // 16])
+            if on_vector:
+                nc.vector.tensor_copy(into, picked)
+            else:
+                nc.scalar.activation(into, picked, ACT.Copy)
+            for b in range(v0 // P, (v0 + n) // P):
                 nc.tensor.matmul(
                     sums[u][b // 2][:, b % 2, e, :],
-                    lhsT=g[d][:, t, b * P : (b + 1) * P],
+                    lhsT=into[:, b * P - v0 : (b + 1) * P - v0],
                     rhs=ident[:],
                     start=(d == 0 and e == 0 and b % 2 == 0),
                     stop=(d == D - 1 and e == 1 and b % 2 == 1),
                     is_transpose=True,
                 )
-        mean = keep.tile([P, T * PACK], BF16, name="mean", align_bytes=64)
+
+        for t in range(PACK):
+            for d in range(2):
+                fetch(t < 2, d, t, 0, T)
+        for a in range(2):
+            for t in range(PACK):
+                fetch(False, 2, t, a * HALF, HALF)
+
+        hi = keep.tile([P, 2, T, 2], BF16, name="hi", align_bytes=64)
+        lo = keep.tile([P, 2, T, 2], BF16, name="lo", align_bytes=64)
+        for u in range(2):
+            for into, op in ((hi, ALU.max), (lo, ALU.min)):
+                nc.vector.tensor_tensor(
+                    into[:, u], g[0][u][:].rearrange("p e v -> p v e"), g[1][u][:].rearrange("p e v -> p v e"), op
+                )
+
+        z = [[keep.tile([P, HALF * PACK], BF16, name="z%d%d" % (s, a), align_bytes=64) for a in range(2)] for s in range(D)]
+        z_codes = [keep.tile([P, T], U32, name="z_codes%d" % s, align_bytes=64) for s in range(D)]
+        z_plane = [keep.tile([P, T], U8, name="z_plane%d" % s, align_bytes=64) for s in range(D)]
+        rounded = [keep.tile([P, 2, HALF, 2], BF16, name="rounded%d" % a, align_bytes=64) for a in range(2)]
         backs = [bank(j, [P, 2, 2, P], "back") for j in range(4)]
+
+        def round_third(a, u):
+            nc.vector.tensor_copy(
+                out=rounded[a][:, u].rearrange("p (c i) e -> p c e i", i=4),
+                in_=third[a][u][:].rearrange("p e (c i) -> p c e i", i=4),
+            )
 
         def turn(u, j):
             turned = keep.tile([P, 2, P, 2], BF16, name="turned", tag="turned%d%d" % (u, j), align_bytes=64)
@@ -194,88 +186,63 @@ def tile_picked_wpna_silu_l_kernel(
             for b in range(2):
                 nc.tensor.transpose(backs[j][:, b, u, :], pairs[:, b, :], ident[:])
 
-        for j in range(4):
-            turn(0, j)
-        for a in range(2):
-            round_pair(2, 1, a * HALF, HALF)
-        for a in range(2):
-            for j in (2 * a, 2 * a + 1):
-                turn(1, j)
-            for j in (2 * a, 2 * a + 1):
-                words = mean[:, j * 2 * P * PACK : (j + 1) * 2 * P * PACK].bitcast(F32)
-                nc.scalar.copy(
-                    out=words.rearrange("p (b v u) -> p b v u", b=2, u=2),
-                    in_=backs[j][:].rearrange("p b u v -> p b v u"),
-                )
+        def lay_mean(j):
+            words = z[0][j // 2][:, j % 2 * 2 * P * PACK : (j % 2 + 1) * 2 * P * PACK].bitcast(F32)
+            nc.scalar.copy(
+                out=words.rearrange("p (b v u) -> p b v u", b=2, u=2),
+                in_=backs[j][:].rearrange("p b u v -> p b v u"),
+            )
 
-        flat = [r[:].rearrange("p u v e -> p (u v e)") for r in rounded]
-        nc.vector.tensor_tensor(hi[:, 2 * SHARE :], flat[0][:, 2 * SHARE :], flat[1][:, 2 * SHARE :], ALU.max)
-        nc.vector.tensor_tensor(lo[:, 2 * SHARE :], flat[0][:, 2 * SHARE :], flat[1][:, 2 * SHARE :], ALU.min)
-        largest = keep.tile([P, T * PACK], BF16, name="largest", align_bytes=64)
-        smallest = keep.tile([P, T * PACK], BF16, name="smallest", align_bytes=64)
-        z = [mean, largest, smallest]
-        z_codes = [keep.tile([P, T], U32, name="z_codes%d" % s, align_bytes=64) for s in range(D)]
-        z_plane = [keep.tile([P, T], U8, name="z_plane%d" % s, align_bytes=64) for s in range(D)]
-
-        def compare(s, v0, n):
-            cols = slice(v0 * PACK, (v0 + n) * PACK)
+        def compare(s, a):
             pair, op = (hi, ALU.max) if s == 1 else (lo, ALU.min)
             nc.vector.tensor_tensor(
-                z[s][:, cols].rearrange("p (v u e) -> p v u e", u=2, e=2),
-                pair[:].rearrange("p (u v e) -> p v u e", u=2, e=2)[:, v0 : v0 + n],
-                rounded[2][:].rearrange("p u v e -> p v u e")[:, v0 : v0 + n],
+                z[s][a][:].rearrange("p (v u e) -> p v u e", u=2, e=2),
+                pair[:].rearrange("p u v e -> p v u e")[:, a * HALF : (a + 1) * HALF],
+                rounded[a][:].rearrange("p u v e -> p v u e"),
                 op,
             )
 
-        def quantise(s, v0, n):
+        def finish(total, s, v0, n, first, last):
+            a, w0 = divmod(v0, HALF)
             nc.vector.quantize_mx(
                 out=z_codes[s][:, v0 : v0 + n].bitcast(FP8X4),
                 scales=z_plane[s][:, v0 : v0 + n],
-                in_=z[s][:, v0 * PACK : (v0 + n) * PACK],
+                in_=z[s][a][:, w0 * PACK : (w0 + n) * PACK],
             )
-
-        def multiply(total, s, v0, n):
-            nc.tensor.matmul_mx(
-                out=total[:],
-                lhsT=w_codes[s][:].bitcast(FP4X4),
-                lhsT_scale=w_plane[:, s * N : (s + 1) * N],
-                rhs=z_codes[s][:, v0 : v0 + n].bitcast(FP8X4),
-                rhs_scale=z_plane[s][:, v0 : v0 + n],
-                start=s == 1,
-                stop=s == 0,
-            )
+            for c0, width, acc in total:
+                if v0 <= c0 < v0 + n:
+                    nc.tensor.matmul_mx(
+                        out=acc[:],
+                        lhsT=w_codes[s][:].bitcast(FP4X4),
+                        lhsT_scale=w_plane[:, s * N : (s + 1) * N],
+                        rhs=z_codes[s][:, c0 : c0 + width].bitcast(FP8X4),
+                        rhs_scale=z_plane[s][:, c0 : c0 + width],
+                        start=first,
+                        stop=last,
+                    )
 
         result = keep.tile([P, T], F32, name="result", align_bytes=64)
-        total = bank(1, [P, HALF], "total")
-        blocks = range(HALF // P, T // P)
-        totals = {b: bank(b, [P, P], "total") for b in blocks}
-
-        def finish(s, v0, n):
-            quantise(s, v0, n)
-            if v0 < HALF:
-                multiply(total, s, v0, n)
-            else:
-                for b in range(v0 // P, (v0 + n) // P):
-                    multiply(totals[b], s, b * P, P)
-
-        compare(1, 0, HALF)
-        compare(2, 0, HALF)
-        finish(1, 0, HALF)
-        finish(2, 0, HALF)
-        compare(1, HALF, HALF)
-        compare(2, HALF, 2 * P)
-        finish(1, HALF, HALF)
-        finish(0, 0, HALF)
-        nc.scalar.copy(out=result[:, :HALF], in_=total[:])
-        nc.sync.dma_start(out=out[:, :HALF], in_=result[:, :HALF])
-        compare(2, T - 2 * P, 2 * P)
-        finish(2, HALF, 2 * P)
-        finish(2, T - 2 * P, 2 * P)
-        for v0, n in ((HALF, 2 * P), (T - 2 * P, P), (T - P, P)):
-            finish(0, v0, n)
-            for b in range(v0 // P, (v0 + n) // P):
-                if n == P:
-                    nc.vector.tensor_copy(out=result[:, b * P : (b + 1) * P], in_=totals[b][:])
-                else:
-                    nc.scalar.copy(out=result[:, b * P : (b + 1) * P], in_=totals[b][:])
+        for u in range(2):
+            for j in range(2):
+                turn(u, j)
+        for j in range(2, 4):
+            turn(0, j)
+        for j in range(2):
+            lay_mean(j)
+        for j in range(2, 4):
+            turn(1, j)
+        for j in range(2, 4):
+            lay_mean(j)
+        totals = [[(0, HALF, bank(4, [P, HALF], "total"))], [(HALF, CHUNK, bank(5, [P, CHUNK], "total")), (HALF + CHUNK, CHUNK, bank(6, [P, CHUNK], "total"))]]
+        for a in range(2):
+            for u in range(2):
+                round_third(a, u)
+            compare(1, a)
+            compare(2, a)
+            finish(totals[a], 1, a * HALF, HALF, True, False)
+            finish(totals[a], 2, a * HALF, HALF, False, False)
+        for v0, n in ((0, HALF), (HALF, CHUNK), (HALF + CHUNK, CHUNK)):
+            finish(totals[v0 // HALF], 0, v0, n, False, True)
+            acc = [x for c0, width, x in totals[v0 // HALF] if c0 == v0][0]
+            nc.vector.tensor_copy(out=result[:, v0 : v0 + n], in_=acc[:])
             nc.sync.dma_start(out=out[:, v0 : v0 + n], in_=result[:, v0 : v0 + n])

@@ -99,7 +99,7 @@ def tile_picked_wpna_silu_l_kernel(
         nc.vector.tensor_copy(out=w1_last[:].rearrange("p t m j -> p m j t"), in_=dealt[:, :, :, 2:4])
         for t in range(PACK):
             if t == 1:
-                rest_codes = keep.tile([P, (PACK - 1) * P], U32, name="rest_codes", align_bytes=64)
+                rest_codes = keep.tile([P, (PACK - 1) * P], U32, name="rest_codes", tag="rest_codes", align_bytes=64)
                 mid = w1_mid[:].rearrange("p m j -> p (m j)")
                 for a, b, flat_in in ((0, 1, mid), (1, 3, w1_last[:].rearrange("p t m j -> p (t m j)"))):
                     nc.vector.quantize_mx(
@@ -110,8 +110,8 @@ def tile_picked_wpna_silu_l_kernel(
             w1_codes = first_codes[:] if t == 0 else rest_codes[:, (t - 1) * P : t * P]
             w1_plane = w1_planes[:, t * P : (t + 1) * P]
             width = 256 if t == 0 else BANK
-            for c0 in range(0, T, width):
-                acc = bank(c0 // width if t == 0 else 4 + (2 * (t - 1) + c0 // width) % 4, [P, width], "acc")
+            for c0 in range(0, T, width) if t == 0 else range(T - width, -1, -width):
+                acc = bank(c0 // width if t == 0 else (3 + t if c0 else 2 + (t - 1) % 2), [P, width], "acc")
                 for c in range(c0 // CHUNK, (c0 + width) // CHUNK):
                     nc.tensor.matmul_mx(
                         out=acc[:, c * CHUNK - c0 : (c + 1) * CHUNK - c0],
@@ -124,59 +124,60 @@ def tile_picked_wpna_silu_l_kernel(
                     )
                 nc.scalar.activation(h[t][:, c0 : c0 + width], acc[:], ACT.Silu)
 
-        g = [[keep.tile([P, 2, T], F32, name="g%d%d" % (d, u), align_bytes=64) for u in range(2)] for d in range(2)]
-        third = [
-            [
-                keep.tile([P, 2, HALF], F32, name="third", tag=("x_codes%d" if u == 0 else "third%d") % a, align_bytes=64)
-                for u in range(2)
-            ]
-            for a in range(2)
+        slots = {(1, 0): "x_codes0", (2, 0): "rest_codes"}
+        g = [
+            [keep.tile([P, 2, T], F32, name="g", tag=slots.get((d, u), "g%d%d" % (d, u)), align_bytes=64) for u in range(2)]
+            for d in range(D)
         ]
         sums = [[bank(4 * u + j, [P, 2, 2, P], "sums") for j in range(4)] for u in range(2)]
+        added = [0, 0]
 
-        def fetch(on_vector, d, t, v0, n):
+        def fetch(on_vector, d, t):
             u, e = divmod(t, 2)
-            into = g[d][u][:, e, :] if d < 2 else third[v0 // HALF][u][:, e, :]
-            picked = h[t][:].indirect(lists[d][:, v0 // 16 : (v0 + n) // 16])
+            into = g[d][u][:, e, :]
+            picked = h[t][:].indirect(lists[d][:])
             if on_vector:
                 nc.vector.tensor_copy(into, picked)
             else:
                 nc.scalar.activation(into, picked, ACT.Copy)
-            for b in range(v0 // P, (v0 + n) // P):
+            for b in range(T // P):
                 nc.tensor.matmul(
                     sums[u][b // 2][:, b % 2, e, :],
-                    lhsT=into[:, b * P - v0 : (b + 1) * P - v0],
+                    lhsT=into[:, b * P : (b + 1) * P],
                     rhs=ident[:],
-                    start=(d == 0 and e == 0 and b % 2 == 0),
-                    stop=(d == D - 1 and e == 1 and b % 2 == 1),
+                    start=(added[u] == 0 and b % 2 == 0),
+                    stop=(added[u] == 2 * D - 1 and b % 2 == 1),
                     is_transpose=True,
                 )
+            added[u] = added[u] + 1
 
-        for t in range(PACK):
-            for d in range(2):
-                fetch(t < 2, d, t, 0, T)
-        for a in range(2):
-            for t in range(PACK):
-                fetch(False, 2, t, a * HALF, HALF)
+        for d, u, on_vector in ((0, 0, True), (1, 0, False), (2, 0, True), (1, 1, False), (0, 1, True), (2, 1, False)):
+            for e in range(2):
+                fetch(on_vector, d, 2 * u + e)
+
+        early = [keep.tile([P, T, 2], BF16, name="early%d" % d, align_bytes=64) for d in range(2)]
+        rounded = keep.tile([P, 2, T, 2], BF16, name="rounded", tag="x_codes0", align_bytes=64)
+        for d, into in enumerate((early[0][:], early[1][:], rounded[:, 0])):
+            nc.gpsimd.tensor_scalar(into, g[d][0][:].rearrange("p e v -> p v e"), 1.0, 0.0, ALU.mult, ALU.add)
 
         hi = keep.tile([P, 2, T, 2], BF16, name="hi", align_bytes=64)
         lo = keep.tile([P, 2, T, 2], BF16, name="lo", align_bytes=64)
-        for u in range(2):
-            for into, op in ((hi, ALU.max), (lo, ALU.min)):
-                nc.vector.tensor_tensor(
-                    into[:, u], g[0][u][:].rearrange("p e v -> p v e"), g[1][u][:].rearrange("p e v -> p v e"), op
-                )
+        for into, op in ((hi, ALU.max), (lo, ALU.min)):
+            nc.vector.tensor_tensor(into[:, 0], early[0][:], early[1][:], op)
+        for into, op in ((hi, ALU.max), (lo, ALU.min)):
+            nc.vector.tensor_tensor(
+                into[:, 1], g[0][1][:].rearrange("p e v -> p v e"), g[1][1][:].rearrange("p e v -> p v e"), op
+            )
 
         z = [[keep.tile([P, HALF * PACK], BF16, name="z%d%d" % (s, a), align_bytes=64) for a in range(2)] for s in range(D)]
-        z_codes = [keep.tile([P, T], U32, name="z_codes%d" % s, align_bytes=64) for s in range(D)]
         z_plane = [keep.tile([P, T], U8, name="z_plane%d" % s, align_bytes=64) for s in range(D)]
-        rounded = [keep.tile([P, 2, HALF, 2], BF16, name="rounded%d" % a, align_bytes=64) for a in range(2)]
         backs = [bank(j, [P, 2, 2, P], "back") for j in range(4)]
 
-        def round_third(a, u):
-            nc.vector.tensor_copy(
-                out=rounded[a][:, u].rearrange("p (c i) e -> p c e i", i=4),
-                in_=third[a][u][:].rearrange("p e (c i) -> p c e i", i=4),
+        def round_third(a):
+            cols = slice(a * HALF, (a + 1) * HALF)
+            nc.scalar.copy(
+                out=rounded[:, 1, cols].rearrange("p (c i) e -> p c e i", i=4),
+                in_=g[2][1][:, :, cols].rearrange("p e (c i) -> p c e i", i=4),
             )
 
         def turn(u, j):
@@ -198,7 +199,7 @@ def tile_picked_wpna_silu_l_kernel(
             nc.vector.tensor_tensor(
                 z[s][a][:].rearrange("p (v u e) -> p v u e", u=2, e=2),
                 pair[:].rearrange("p u v e -> p v u e")[:, a * HALF : (a + 1) * HALF],
-                rounded[a][:].rearrange("p u v e -> p v u e"),
+                rounded[:].rearrange("p u v e -> p v u e")[:, a * HALF : (a + 1) * HALF],
                 op,
             )
 
@@ -222,27 +223,30 @@ def tile_picked_wpna_silu_l_kernel(
                     )
 
         result = keep.tile([P, T], F32, name="result", align_bytes=64)
-        for u in range(2):
-            for j in range(2):
-                turn(u, j)
-        for j in range(2, 4):
-            turn(0, j)
-        for j in range(2):
-            lay_mean(j)
-        for j in range(2, 4):
-            turn(1, j)
-        for j in range(2, 4):
-            lay_mean(j)
-        totals = [[(0, HALF, bank(4, [P, HALF], "total"))], [(HALF, CHUNK, bank(5, [P, CHUNK], "total")), (HALF + CHUNK, CHUNK, bank(6, [P, CHUNK], "total"))]]
+        turn(0, 0)
         for a in range(2):
-            for u in range(2):
-                round_third(a, u)
+            round_third(a)
+        for j in range(1, 4):
+            turn(0, j)
+        for j in range(4):
+            turn(1, j)
+        for j in range(4):
+            lay_mean(j)
+        z_codes = [
+            keep.tile([P, T], U32, name="z_codes", tag=tag, align_bytes=64) for tag in ("z_codes0", "turned13", "z_codes2")
+        ]
+        pieces = ((0, HALF), (HALF, CHUNK), (T - CHUNK, P), (T - P, P))
+        totals = [(c0, width, bank(4 + i, [P, width], "total")) for i, (c0, width) in enumerate(pieces)]
+        for a in range(2):
             compare(1, a)
             compare(2, a)
-            finish(totals[a], 1, a * HALF, HALF, True, False)
-            finish(totals[a], 2, a * HALF, HALF, False, False)
-        for v0, n in ((0, HALF), (HALF, CHUNK), (HALF + CHUNK, CHUNK)):
-            finish(totals[v0 // HALF], 0, v0, n, False, True)
-            acc = [x for c0, width, x in totals[v0 // HALF] if c0 == v0][0]
-            nc.vector.tensor_copy(out=result[:, v0 : v0 + n], in_=acc[:])
+        for a in range(2):
+            finish(totals, 1, a * HALF, HALF, True, False)
+            finish(totals, 2, a * HALF, HALF, False, False)
+        for v0, n, acc in totals:
+            finish(totals, 0, v0, n, False, True)
+            if v0 + n < T:
+                nc.scalar.copy(out=result[:, v0 : v0 + n], in_=acc[:])
+            else:
+                nc.vector.tensor_copy(out=result[:, v0 : v0 + n], in_=acc[:])
             nc.sync.dma_start(out=out[:, v0 : v0 + n], in_=result[:, v0 : v0 + n])

@@ -91,7 +91,7 @@ def tile_picked_wpna_silu_l_kernel(
         for j0, j1 in ((0, 3), (3, 4)):
             nc.vector.tensor_copy(out=w1_first[:, :, j0:j1], in_=dealt[:, :, j0:j1, 0])
         first_codes = keep.tile([P, P], U32, name="first_codes", align_bytes=64)
-        w1_planes = keep.tile([P, PACK * P], U8, name="w1_planes", align_bytes=64)
+        w1_planes = keep.tile([P, PACK * P], U8, name="w1_planes", tag="w1_planes", align_bytes=64)
         nc.vector.quantize_mx(
             out=first_codes[:].bitcast(FP8X4), scales=w1_planes[:, :P], in_=w1_first[:].rearrange("p m j -> p (m j)")
         )
@@ -124,129 +124,152 @@ def tile_picked_wpna_silu_l_kernel(
                     )
                 nc.scalar.activation(h[t][:, c0 : c0 + width], acc[:], ACT.Silu)
 
-        slots = {(1, 0): "x_codes0", (2, 0): "rest_codes"}
-        g = [
-            [keep.tile([P, 2, T], F32, name="g", tag=slots.get((d, u), "g%d%d" % (d, u)), align_bytes=64) for u in range(2)]
-            for d in range(D)
-        ]
+        slots = {(1, 0): "x_codes0"}
+        g = {}
+        for d, u in ((0, 0), (1, 0), (0, 1), (1, 1)):
+            g[d, u] = keep.tile([P, 2, T], F32, name="g", tag=slots.get((d, u), "g%d%d" % (d, u)), align_bytes=64)
+        late = [keep.tile([P, PACK, HALF], F32, name="late", tag=tag, align_bytes=64) for tag in ("rest_codes", "w1_planes")]
         sums = [[bank(4 * u + j, [P, 2, 2, P], "sums") for j in range(4)] for u in range(2)]
-        added = [0, 0]
+        added = [0] * 8
 
-        def fetch(on_vector, d, t):
+        def fetch(on_vector, d, t, v0, n):
             u, e = divmod(t, 2)
-            into = g[d][u][:, e, :]
-            picked = h[t][:].indirect(lists[d][:])
+            into = g[d, u][:, e, :] if n == T else late[v0 // HALF][:, t, :]
+            picked = h[t][:].indirect(lists[d][:, v0 // 16 : (v0 + n) // 16])
             if on_vector:
                 nc.vector.tensor_copy(into, picked)
             else:
                 nc.scalar.activation(into, picked, ACT.Copy)
-            for b in range(T // P):
+            for b in range(v0 // P, (v0 + n) // P):
+                j = 4 * u + b // 2
                 nc.tensor.matmul(
                     sums[u][b // 2][:, b % 2, e, :],
-                    lhsT=into[:, b * P : (b + 1) * P],
+                    lhsT=into[:, b * P - v0 : (b + 1) * P - v0],
                     rhs=ident[:],
-                    start=(added[u] == 0 and b % 2 == 0),
-                    stop=(added[u] == 2 * D - 1 and b % 2 == 1),
+                    start=added[j] == 0,
+                    stop=added[j] == 4 * D - 1,
                     is_transpose=True,
                 )
-            added[u] = added[u] + 1
-
-        for d, u, on_vector in ((0, 0, True), (1, 0, False), (2, 0, True), (1, 1, False), (0, 1, True), (2, 1, False)):
-            for e in range(2):
-                fetch(on_vector, d, 2 * u + e)
-
-        early = [keep.tile([P, T, 2], BF16, name="early%d" % d, align_bytes=64) for d in range(2)]
-        rounded = keep.tile([P, 2, T, 2], BF16, name="rounded", tag="x_codes0", align_bytes=64)
-        for d, into in enumerate((early[0][:], early[1][:], rounded[:, 0])):
-            nc.gpsimd.tensor_scalar(into, g[d][0][:].rearrange("p e v -> p v e"), 1.0, 0.0, ALU.mult, ALU.add)
-
-        hi = keep.tile([P, 2, T, 2], BF16, name="hi", align_bytes=64)
-        lo = keep.tile([P, 2, T, 2], BF16, name="lo", align_bytes=64)
-        for into, op in ((hi, ALU.max), (lo, ALU.min)):
-            nc.vector.tensor_tensor(into[:, 0], early[0][:], early[1][:], op)
-        for into, op in ((hi, ALU.max), (lo, ALU.min)):
-            nc.vector.tensor_tensor(
-                into[:, 1], g[0][1][:].rearrange("p e v -> p v e"), g[1][1][:].rearrange("p e v -> p v e"), op
-            )
-
-        z = [[keep.tile([P, HALF * PACK], BF16, name="z%d%d" % (s, a), align_bytes=64) for a in range(2)] for s in range(D)]
-        z_plane = [keep.tile([P, T], U8, name="z_plane%d" % s, align_bytes=64) for s in range(D)]
-        backs = [bank(j, [P, 2, 2, P], "back") for j in range(4)]
-
-        def round_third(a):
-            cols = slice(a * HALF, (a + 1) * HALF)
-            nc.scalar.copy(
-                out=rounded[:, 1, cols].rearrange("p (c i) e -> p c e i", i=4),
-                in_=g[2][1][:, :, cols].rearrange("p e (c i) -> p c e i", i=4),
-            )
+                added[j] = added[j] + 1
 
         def turn(u, j):
             turned = keep.tile([P, 2, P, 2], BF16, name="turned", tag="turned%d%d" % (u, j), align_bytes=64)
-            nc.scalar.activation(turned[:], sums[u][j][:].rearrange("v b e p -> v b p e"), ACT.Copy, scale=1.0 / D)
+            summed = sums[u][j][:].rearrange("v b e p -> v b p e")
+            nc.scalar.activation(turned[:], summed, ACT.Copy, scale=1.0 / D)
             pairs = turned[:].rearrange("v b p e -> v b (p e)").bitcast(F32)
+            if u == 0:
+                backs[j] = bank(j, [P, 2, 2, P], "back")
             for b in range(2):
                 nc.tensor.transpose(backs[j][:, b, u, :], pairs[:, b, :], ident[:])
 
-        def lay_mean(j):
-            words = z[0][j // 2][:, j % 2 * 2 * P * PACK : (j % 2 + 1) * 2 * P * PACK].bitcast(F32)
+        backs = {}
+        for u in range(2):
+            for d in range(2):
+                fetch(True, d, 2 * u, 0, T)
+                fetch(d + u == 0, d, 2 * u + 1, 0, T)
+        for a in range(2):
+            for t in range(PACK):
+                fetch(False, 2, t, a * HALF, HALF)
+
+        def round_on_vector(into, pair):
+            nc.vector.tensor_copy(
+                out=into.rearrange("p (c i) e -> p c e i", i=4), in_=pair.rearrange("p e (c i) -> p c e i", i=4)
+            )
+
+        early = {}
+        for u in range(2):
+            for d in range(2):
+                early[d, u] = keep.tile([P, T, 2], BF16, name="early", tag="early%d%d" % (d, u), align_bytes=64)
+                if d + u < 2:
+                    nc.gpsimd.tensor_scalar(
+                        early[d, u][:], g[d, u][:].rearrange("p e v -> p v e"), 1.0, 0.0, ALU.mult, ALU.add
+                    )
+                else:
+                    round_on_vector(early[d, u][:], g[d, u][:])
+        rounded = [keep.tile([P, 2, HALF, 2], BF16, name="rounded", tag=tag, align_bytes=64) for tag in ("g01", "early01")]
+
+        def round_third(a):
+            nc.vector.tensor_copy(
+                out=rounded[a][:].rearrange("p u (c i) e -> p u c e i", i=4),
+                in_=late[a][:].rearrange("p (u e) (c i) -> p u c e i", e=2, i=4),
+            )
+
+        hi = keep.tile([P, 2, T, 2], BF16, name="hi", align_bytes=64)
+        lo = keep.tile([P, 2, T, 2], BF16, name="lo", align_bytes=64)
+        for u in range(2):
+            for into, op in ((hi, ALU.max), (lo, ALU.min)):
+                if u == 1 and op == ALU.min:
+                    round_third(0)
+                nc.vector.tensor_tensor(into[:, u], early[0, u][:], early[1, u][:], op)
+
+        means = [keep.tile([P, HALF * PACK], BF16, name="means%d" % a, align_bytes=64) for a in range(2)]
+        ends = [keep.tile([P, 2 * HALF * PACK], BF16, name="ends%d" % a, align_bytes=64) for a in range(2)]
+        z_codes = [keep.tile([P, D * HALF], U32, name="z_codes%d" % a, align_bytes=64) for a in range(2)]
+        z_plane = [keep.tile([P, D * HALF], U8, name="z_plane%d" % a, align_bytes=64) for a in range(2)]
+
+        def lay_mean(b0, n):
+            j, b = divmod(b0, 2)
+            words = means[b0 // 4][:, b0 % 4 * P * PACK : (b0 % 4 + n) * P * PACK].bitcast(F32)
             nc.scalar.copy(
-                out=words.rearrange("p (b v u) -> p b v u", b=2, u=2),
-                in_=backs[j][:].rearrange("p b u v -> p b v u"),
+                out=words.rearrange("p (b v u) -> p b v u", b=n, u=2),
+                in_=backs[j][:, b : b + n].rearrange("p b u v -> p b v u"),
             )
 
         def compare(s, a):
             pair, op = (hi, ALU.max) if s == 1 else (lo, ALU.min)
             nc.vector.tensor_tensor(
-                z[s][a][:].rearrange("p (v u e) -> p v u e", u=2, e=2),
+                ends[a][:, (s - 1) * HALF * PACK : s * HALF * PACK].rearrange("p (v u e) -> p v u e", u=2, e=2),
                 pair[:].rearrange("p u v e -> p v u e")[:, a * HALF : (a + 1) * HALF],
-                rounded[:].rearrange("p u v e -> p v u e")[:, a * HALF : (a + 1) * HALF],
+                rounded[a][:].rearrange("p u v e -> p v u e"),
                 op,
             )
 
-        def finish(total, s, v0, n, first, last):
+        def quantise(s, v0, n):
             a, w0 = divmod(v0, HALF)
+            c0 = s * HALF + w0
+            values = means[a][:, w0 * PACK : (w0 + n) * PACK] if s == 0 else ends[a][:, (c0 - HALF) * PACK : (c0 - HALF + n) * PACK]
             nc.vector.quantize_mx(
-                out=z_codes[s][:, v0 : v0 + n].bitcast(FP8X4),
-                scales=z_plane[s][:, v0 : v0 + n],
-                in_=z[s][a][:, w0 * PACK : (w0 + n) * PACK],
+                out=z_codes[a][:, c0 : c0 + n].bitcast(FP8X4), scales=z_plane[a][:, c0 : c0 + n], in_=values
             )
-            for c0, width, acc in total:
-                if v0 <= c0 < v0 + n:
-                    nc.tensor.matmul_mx(
-                        out=acc[:],
-                        lhsT=w_codes[s][:].bitcast(FP4X4),
-                        lhsT_scale=w_plane[:, s * N : (s + 1) * N],
-                        rhs=z_codes[s][:, c0 : c0 + width].bitcast(FP8X4),
-                        rhs_scale=z_plane[s][:, c0 : c0 + width],
-                        start=first,
-                        stop=last,
-                    )
+
+        def multiply(acc, v0, n):
+            a, w0 = divmod(v0, HALF)
+            for s in (1, 2, 0):
+                c0 = s * HALF + w0
+                nc.tensor.matmul_mx(
+                    out=acc,
+                    lhsT=w_codes[s][:].bitcast(FP4X4),
+                    lhsT_scale=w_plane[:, s * N : (s + 1) * N],
+                    rhs=z_codes[a][:, c0 : c0 + n].bitcast(FP8X4),
+                    rhs_scale=z_plane[a][:, c0 : c0 + n],
+                    start=s == 1,
+                    stop=s == 0,
+                )
 
         result = keep.tile([P, T], F32, name="result", align_bytes=64)
-        turn(0, 0)
-        for a in range(2):
-            round_third(a)
-        for j in range(1, 4):
-            turn(0, j)
-        for j in range(4):
-            turn(1, j)
-        for j in range(4):
-            lay_mean(j)
-        z_codes = [
-            keep.tile([P, T], U32, name="z_codes", tag=tag, align_bytes=64) for tag in ("z_codes0", "turned13", "z_codes2")
-        ]
-        pieces = ((0, HALF), (HALF, CHUNK), (T - CHUNK, P), (T - P, P))
-        totals = [(c0, width, bank(4 + i, [P, width], "total")) for i, (c0, width) in enumerate(pieces)]
-        for a in range(2):
-            compare(1, a)
-            compare(2, a)
-        for a in range(2):
-            finish(totals, 1, a * HALF, HALF, True, False)
-            finish(totals, 2, a * HALF, HALF, False, False)
-        for v0, n, acc in totals:
-            finish(totals, 0, v0, n, False, True)
-            if v0 + n < T:
-                nc.scalar.copy(out=result[:, v0 : v0 + n], in_=acc[:])
-            else:
-                nc.vector.tensor_copy(out=result[:, v0 : v0 + n], in_=acc[:])
+        for u in range(2):
+            for j in range(4):
+                turn(u, j)
+        for b0, n in ((0, 2), (2, 2), (4, 2), (6, 1), (7, 1)):
+            lay_mean(b0, n)
+        compare(1, 0)
+        compare(2, 0)
+        quantise(1, 0, HALF)
+        round_third(1)
+        quantise(2, 0, HALF)
+        compare(1, 1)
+        compare(2, 1)
+        quantise(1, HALF, HALF)
+        quantise(2, HALF, HALF)
+        for v0, n, parts in ((0, HALF, ((4, HALF),)), (HALF, 3 * P, ((5, 2 * P), (6, P))), (T - P, P, ((7, P),))):
+            quantise(0, v0, n)
+            c0 = v0
+            for b, width in parts:
+                total = bank(b, [P, width], "total")
+                multiply(total[:], c0, width)
+                if v0 + n < T:
+                    nc.scalar.copy(out=result[:, c0 : c0 + width], in_=total[:])
+                else:
+                    nc.vector.tensor_copy(out=result[:, c0 : c0 + width], in_=total[:])
+                c0 = c0 + width
             nc.sync.dma_start(out=out[:, v0 : v0 + n], in_=result[:, v0 : v0 + n])

@@ -24,6 +24,7 @@ BANK = 512
 CHUNK = 256
 HALF = 512
 SPARE = 352
+HANDED = 256
 
 
 def tile_picked_wpna_silu_l_kernel(
@@ -134,7 +135,7 @@ def tile_picked_wpna_silu_l_kernel(
 
         def fetch(on_vector, d, t, v0, n):
             u, e = divmod(t, 2)
-            into = g[d, u][:, e, :] if n == T else late[v0 // HALF][:, t, :]
+            into = g[d, u][:, e, :] if n == T else late[v0 // HALF][:, t, v0 % HALF : v0 % HALF + n]
             picked = h[t][:].indirect(lists[d][:, v0 // 16 : (v0 + n) // 16])
             if on_vector:
                 nc.vector.tensor_copy(into, picked)
@@ -167,9 +168,11 @@ def tile_picked_wpna_silu_l_kernel(
             for d in range(2):
                 fetch(True, d, 2 * u, 0, T)
                 fetch(d + u == 0, d, 2 * u + 1, 0, T)
+        fetch(True, 2, PACK - 1, 0, HANDED)
         for a in range(2):
             for t in range(PACK):
-                fetch(False, 2, t, a * HALF, HALF)
+                v0 = HANDED if (a, t) == (0, PACK - 1) else a * HALF
+                fetch(False, 2, t, v0, (a + 1) * HALF - v0)
 
         def round_on_vector(into, pair):
             nc.vector.tensor_copy(
@@ -260,14 +263,15 @@ def tile_picked_wpna_silu_l_kernel(
         compare(1, 1)
         compare(2, 1)
         quantise(1, HALF, HALF)
-        quantise(2, HALF, HALF)
-        for v0, n, parts in ((0, HALF, ((4, HALF),)), (HALF, 3 * P, ((5, 2 * P), (6, P))), (T - P, P, ((7, P),))):
+        for v0, n, parts in ((0, HALF, ((5, HALF),)), (HALF, 3 * P, ((6, 2 * P), (7, P))), (T - P, P, ((4, P),))):
+            if v0 == HALF:
+                quantise(2, HALF, HALF)
             quantise(0, v0, n)
             c0 = v0
             for b, width in parts:
                 total = bank(b, [P, width], "total")
                 multiply(total[:], c0, width)
-                if v0 + n < T:
+                if width > P:
                     nc.scalar.copy(out=result[:, c0 : c0 + width], in_=total[:])
                 else:
                     nc.vector.tensor_copy(out=result[:, c0 : c0 + width], in_=total[:])

@@ -25,6 +25,7 @@ CHUNK = 256
 HALF = 512
 SPARE = 352
 HANDED = 256
+PIECES = ((0, HALF), (HALF, 3 * P), (T - P, P))
 
 
 def tile_picked_wpna_silu_l_kernel(
@@ -205,14 +206,15 @@ def tile_picked_wpna_silu_l_kernel(
                     round_third(0)
                 nc.vector.tensor_tensor(into[:, u], early[0, u][:], early[1, u][:], op)
 
-        means = [keep.tile([P, HALF * PACK], BF16, name="means%d" % a, align_bytes=64) for a in range(2)]
+        means = {v0: keep.tile([P, n * PACK], BF16, name="means%d" % v0, align_bytes=64) for v0, n in PIECES}
         ends = [keep.tile([P, 2 * HALF * PACK], BF16, name="ends%d" % a, align_bytes=64) for a in range(2)]
         z_codes = [keep.tile([P, D * HALF], U32, name="z_codes%d" % a, align_bytes=64) for a in range(2)]
         z_plane = [keep.tile([P, D * HALF], U8, name="z_plane%d" % a, align_bytes=64) for a in range(2)]
 
         def lay_mean(b0, n):
             j, b = divmod(b0, 2)
-            words = means[b0 // 4][:, b0 % 4 * P * PACK : (b0 % 4 + n) * P * PACK].bitcast(F32)
+            v0 = max(start for start, width in PIECES if start <= b0 * P)
+            words = means[v0][:, (b0 * P - v0) * PACK : ((b0 + n) * P - v0) * PACK].bitcast(F32)
             nc.scalar.copy(
                 out=words.rearrange("p (b v u) -> p b v u", b=n, u=2),
                 in_=backs[j][:, b : b + n].rearrange("p b u v -> p b v u"),
@@ -230,7 +232,7 @@ def tile_picked_wpna_silu_l_kernel(
         def quantise(s, v0, n):
             a, w0 = divmod(v0, HALF)
             c0 = s * HALF + w0
-            values = means[a][:, w0 * PACK : (w0 + n) * PACK] if s == 0 else ends[a][:, (c0 - HALF) * PACK : (c0 - HALF + n) * PACK]
+            values = means[v0][:] if s == 0 else ends[a][:, (c0 - HALF) * PACK : (c0 - HALF + n) * PACK]
             nc.vector.quantize_mx(
                 out=z_codes[a][:, c0 : c0 + n].bitcast(FP8X4), scales=z_plane[a][:, c0 : c0 + n], in_=values
             )
@@ -263,7 +265,7 @@ def tile_picked_wpna_silu_l_kernel(
         compare(1, 1)
         compare(2, 1)
         quantise(1, HALF, HALF)
-        for v0, n, parts in ((0, HALF, ((5, HALF),)), (HALF, 3 * P, ((6, 2 * P), (7, P))), (T - P, P, ((4, P),))):
+        for v0, n, parts in ((0, HALF, ((7, HALF),)), (HALF, 3 * P, ((5, 2 * P), (6, P))), (T - P, P, ((4, P),))):
             if v0 == HALF:
                 quantise(2, HALF, HALF)
             quantise(0, v0, n)

@@ -25,6 +25,7 @@ CHUNK = 256
 HALF = 512
 SPARE = 352
 HANDED = 256
+SUM_BANKS = (0, 1, 6, 7, 2, 3, 4, 5)
 PIECES = ((0, HALF), (HALF, 3 * P), (T - P, P))
 
 
@@ -75,7 +76,7 @@ def tile_picked_wpna_silu_l_kernel(
                 )
 
         def bank(b, shape, name):
-            return psum.tile(shape, F32, name=name, tag="bank%d" % b)
+            return psum.tile(shape, F32, name=name, tag="%s%d" % (name, b), offset=b * BANK * 4)
 
         h = [keep.tile([P, T + SPARE], F32, name="h%d" % t, align_bytes=64) for t in range(PACK)]
         for t in range(PACK):
@@ -99,53 +100,61 @@ def tile_picked_wpna_silu_l_kernel(
         )
         nc.scalar.copy(out=w1_mid[:], in_=dealt[:, :, :, 1])
         nc.vector.tensor_copy(out=w1_last[:].rearrange("p t m j -> p m j t"), in_=dealt[:, :, :, 2:4])
-        for t in range(PACK):
-            if t == 1:
-                rest_codes = keep.tile([P, (PACK - 1) * P], U32, name="rest_codes", tag="rest_codes", align_bytes=64)
-                mid = w1_mid[:].rearrange("p m j -> p (m j)")
-                for a, b, flat_in in ((0, 1, mid), (1, 3, w1_last[:].rearrange("p t m j -> p (t m j)"))):
-                    nc.vector.quantize_mx(
-                        out=rest_codes[:, a * P : b * P].bitcast(FP8X4),
-                        scales=w1_planes[:, (a + 1) * P : (b + 1) * P],
-                        in_=flat_in,
-                    )
-            w1_codes = first_codes[:] if t == 0 else rest_codes[:, (t - 1) * P : t * P]
-            w1_plane = w1_planes[:, t * P : (t + 1) * P]
-            width = 256 if t == 0 else BANK
-            for c0 in range(0, T, width) if t == 0 else range(T - width, -1, -width):
-                acc = bank(c0 // width if t == 0 else (3 + t if c0 else 2 + (t - 1) % 2), [P, width], "acc")
-                for c in range(c0 // CHUNK, (c0 + width) // CHUNK):
-                    nc.tensor.matmul_mx(
-                        out=acc[:, c * CHUNK - c0 : (c + 1) * CHUNK - c0],
-                        lhsT=w1_codes.bitcast(FP8X4),
-                        lhsT_scale=w1_plane,
-                        rhs=x_codes[c // 2][:, c % 2 * CHUNK : (c % 2 + 1) * CHUNK].bitcast(FP8X4),
-                        rhs_scale=x_plane[4 * c :, :],
-                        start=True,
-                        stop=True,
-                    )
-                nc.scalar.activation(h[t][:, c0 : c0 + width], acc[:], ACT.Silu)
+        rest_codes = keep.tile([P, (PACK - 1) * P], U32, name="rest_codes", align_bytes=64)
+        mid = w1_mid[:].rearrange("p m j -> p (m j)")
 
-        slots = {(1, 0): "x_codes0"}
+        def quantise_rest():
+            for a, b, flat_in in ((0, 1, mid), (1, 3, w1_last[:].rearrange("p t m j -> p (t m j)"))):
+                nc.vector.quantize_mx(
+                    out=rest_codes[:, a * P : b * P].bitcast(FP8X4),
+                    scales=w1_planes[:, (a + 1) * P : (b + 1) * P],
+                    in_=flat_in,
+                )
+
+        def project(t, acc, c0, width):
+            w1_codes = first_codes[:] if t == 0 else rest_codes[:, (t - 1) * P : t * P]
+            for c in range(c0 // CHUNK, (c0 + width) // CHUNK):
+                nc.tensor.matmul_mx(
+                    out=acc[:, c * CHUNK - c0 : (c + 1) * CHUNK - c0],
+                    lhsT=w1_codes.bitcast(FP8X4),
+                    lhsT_scale=w1_planes[:, t * P : (t + 1) * P],
+                    rhs=x_codes[c // 2][:, c % 2 * CHUNK : (c % 2 + 1) * CHUNK].bitcast(FP8X4),
+                    rhs_scale=x_plane[4 * c :, :],
+                    start=True,
+                    stop=True,
+                )
+
+        def activate(t, acc, c0, width):
+            nc.scalar.activation(h[t][:, c0 : c0 + width], acc, ACT.Silu)
+
         g = {}
-        for d, u in ((0, 0), (1, 0), (0, 1), (1, 1)):
-            g[d, u] = keep.tile([P, 2, T], F32, name="g", tag=slots.get((d, u), "g%d%d" % (d, u)), align_bytes=64)
-        late = [keep.tile([P, PACK, HALF], F32, name="late", tag=tag, align_bytes=64) for tag in ("rest_codes", "w1_planes")]
-        sums = [[bank(4 * u + j, [P, 2, 2, P], "sums") for j in range(4)] for u in range(2)]
+        for d, u in ((0, 0), (1, 0), (2, 0), (0, 1), (1, 1)):
+            g[d, u] = keep.tile([P, 2, T], F32, name="g", tag="g%d%d" % (d, u), align_bytes=64)
+        late = [keep.tile([P, 2, HALF], F32, name="late%d" % a, align_bytes=64) for a in range(2)]
+        sums = {}
         added = [0] * 8
 
-        def fetch(on_vector, d, t, v0, n):
+        def place(d, t, v0, n):
             u, e = divmod(t, 2)
-            into = g[d, u][:, e, :] if n == T else late[v0 // HALF][:, t, v0 % HALF : v0 % HALF + n]
+            return g[d, u][:, e, v0 : v0 + n] if (d, u) in g else late[v0 // HALF][:, e, :]
+
+        def gather(on_vector, d, t, v0, n):
+            into = place(d, t, v0, n)
             picked = h[t][:].indirect(lists[d][:, v0 // 16 : (v0 + n) // 16])
             if on_vector:
                 nc.vector.tensor_copy(into, picked)
             else:
                 nc.scalar.activation(into, picked, ACT.Copy)
+
+        def add_up(d, t, v0, n):
+            u, e = divmod(t, 2)
+            into = place(d, t, v0, n)
             for b in range(v0 // P, (v0 + n) // P):
                 j = 4 * u + b // 2
+                if j not in sums:
+                    sums[j] = bank(SUM_BANKS[j], [P, 2, 2, P], "sums")
                 nc.tensor.matmul(
-                    sums[u][b // 2][:, b % 2, e, :],
+                    sums[j][:, b % 2, e, :],
                     lhsT=into[:, b * P - v0 : (b + 1) * P - v0],
                     rhs=ident[:],
                     start=added[j] == 0,
@@ -154,26 +163,8 @@ def tile_picked_wpna_silu_l_kernel(
                 )
                 added[j] = added[j] + 1
 
-        def turn(u, j):
-            turned = keep.tile([P, 2, P, 2], BF16, name="turned", tag="turned%d%d" % (u, j), align_bytes=64)
-            summed = sums[u][j][:].rearrange("v b e p -> v b p e")
-            nc.scalar.activation(turned[:], summed, ACT.Copy, scale=1.0 / D)
-            pairs = turned[:].rearrange("v b p e -> v b (p e)").bitcast(F32)
-            if u == 0:
-                backs[j] = bank(j, [P, 2, 2, P], "back")
-            for b in range(2):
-                nc.tensor.transpose(backs[j][:, b, u, :], pairs[:, b, :], ident[:])
-
-        backs = {}
-        for u in range(2):
-            for d in range(2):
-                fetch(True, d, 2 * u, 0, T)
-                fetch(d + u == 0, d, 2 * u + 1, 0, T)
-        fetch(True, 2, PACK - 1, 0, HANDED)
-        for a in range(2):
-            for t in range(PACK):
-                v0 = HANDED if (a, t) == (0, PACK - 1) else a * HALF
-                fetch(False, 2, t, v0, (a + 1) * HALF - v0)
+        def round_on_gpsimd(into, pair):
+            nc.gpsimd.tensor_scalar(into, pair.rearrange("p e v -> p v e"), 1.0, 0.0, ALU.mult, ALU.add)
 
         def round_on_vector(into, pair):
             nc.vector.tensor_copy(
@@ -181,30 +172,84 @@ def tile_picked_wpna_silu_l_kernel(
             )
 
         early = {}
-        for u in range(2):
-            for d in range(2):
-                early[d, u] = keep.tile([P, T, 2], BF16, name="early", tag="early%d%d" % (d, u), align_bytes=64)
-                if d + u < 2:
-                    nc.gpsimd.tensor_scalar(
-                        early[d, u][:], g[d, u][:].rearrange("p e v -> p v e"), 1.0, 0.0, ALU.mult, ALU.add
-                    )
-                else:
-                    round_on_vector(early[d, u][:], g[d, u][:])
-        rounded = [keep.tile([P, 2, HALF, 2], BF16, name="rounded", tag=tag, align_bytes=64) for tag in ("g01", "early01")]
+        for d, u in ((0, 0), (1, 0), (1, 1)):
+            early[d, u] = keep.tile([P, T, 2], BF16, name="early%d%d" % (d, u), align_bytes=64)[:]
 
-        def round_third(a):
-            nc.vector.tensor_copy(
-                out=rounded[a][:].rearrange("p u (c i) e -> p u c e i", i=4),
-                in_=late[a][:].rearrange("p (u e) (c i) -> p u c e i", e=2, i=4),
-            )
+        for c, b in enumerate((0, 1, 2, 6)):
+            acc = bank(b, [P, CHUNK], "first")
+            project(0, acc[:], c * CHUNK, CHUNK)
+            activate(0, acc[:], c * CHUNK, CHUNK)
+        quantise_rest()
+        for a, b in ((1, 7), (0, 2)):
+            acc = bank(b, [P, BANK], "second")
+            project(1, acc[:], a * BANK, BANK)
+            activate(1, acc[:], a * BANK, BANK)
+        later = bank(2, [P, 2, 2, BANK], "later")
+        for t in (2, 3):
+            for a in range(2):
+                project(t, later[:, t - 2, a, :], a * BANK, BANK)
+        for d in range(2):
+            gather(True, d, 0, 0, T)
+            gather(False, d, 1, 0, T)
+            add_up(d, 0, 0, T)
+            add_up(d, 1, 0, T)
+            round_on_gpsimd(early[d, 0], g[d, 0][:])
+        gather(True, 2, 0, 0, T)
+        gather(True, 2, 1, 0, T)
+        add_up(2, 0, 0, T)
+        add_up(2, 1, 0, T)
+        shared = keep.tile([P, 2 * T + HALF, 2], BF16, name="shared", tag="g10", align_bytes=64)
+        third = shared[:, : 2 * T].rearrange("p (u v) e -> p u v e", u=2)
+        early[0, 1] = shared[:, T + HALF :]
+        round_on_gpsimd(third[:, 0], g[2, 0][:])
+        for t in (2, 3):
+            for a in range(2):
+                activate(t, later[:, t - 2, a, :], a * BANK, BANK)
+        gather(False, 0, 2, 0, T)
+        gather(True, 0, 3, 0, T)
+        gather(False, 1, 2, 0, T)
+        gather(True, 1, 3, 0, HANDED)
+        gather(False, 1, 3, HANDED, T - HANDED)
+        for a in range(2):
+            for t in (2, 3):
+                gather(False, 2, t, a * HALF, HALF)
+        for d in range(2):
+            for t in (2, 3):
+                add_up(d, t, 0, T)
+        for a in range(2):
+            for t in (2, 3):
+                add_up(2, t, a * HALF, HALF)
 
         hi = keep.tile([P, 2, T, 2], BF16, name="hi", align_bytes=64)
         lo = keep.tile([P, 2, T, 2], BF16, name="lo", align_bytes=64)
-        for u in range(2):
-            for into, op in ((hi, ALU.max), (lo, ALU.min)):
-                if u == 1 and op == ALU.min:
-                    round_third(0)
-                nc.vector.tensor_tensor(into[:, u], early[0, u][:], early[1, u][:], op)
+
+        def first_round(into, op, u, v0=0, n=T):
+            cols = slice(v0, v0 + n)
+            nc.vector.tensor_tensor(into[:, u, cols], early[0, u][:, cols], early[1, u][:, cols], op)
+
+        def round_third(a):
+            round_on_vector(third[:, 1, a * HALF : (a + 1) * HALF], late[a][:])
+
+        round_on_vector(early[0, 1], g[0, 1][:])
+        first_round(hi, ALU.max, 0)
+        first_round(lo, ALU.min, 0, 0, HALF)
+        round_on_vector(early[1, 1], g[1, 1][:])
+        first_round(lo, ALU.min, 0, HALF, HALF)
+        first_round(hi, ALU.max, 1)
+        round_third(0)
+        first_round(lo, ALU.min, 1)
+
+        backs = {}
+
+        def turn(u, j):
+            turned = keep.tile([P, 2, P, 2], BF16, name="turned", tag="turned%d%d" % (u, j), align_bytes=64)
+            summed = sums[4 * u + j][:].rearrange("v b e p -> v b p e")
+            nc.scalar.activation(turned[:], summed, ACT.Copy, scale=1.0 / D)
+            pairs = turned[:].rearrange("v b p e -> v b (p e)").bitcast(F32)
+            if u == 0:
+                backs[j] = bank(SUM_BANKS[j], [P, 2, 2, P], "back")
+            for b in range(2):
+                nc.tensor.transpose(backs[j][:, b, u, :], pairs[:, b, :], ident[:])
 
         means = {v0: keep.tile([P, n * PACK], BF16, name="means%d" % v0, align_bytes=64) for v0, n in PIECES}
         ends = [keep.tile([P, 2 * HALF * PACK], BF16, name="ends%d" % a, align_bytes=64) for a in range(2)]
@@ -225,7 +270,7 @@ def tile_picked_wpna_silu_l_kernel(
             nc.vector.tensor_tensor(
                 ends[a][:, (s - 1) * HALF * PACK : s * HALF * PACK].rearrange("p (v u e) -> p v u e", u=2, e=2),
                 pair[:].rearrange("p u v e -> p v u e")[:, a * HALF : (a + 1) * HALF],
-                rounded[a][:].rearrange("p u v e -> p v u e"),
+                third.rearrange("p u v e -> p v u e")[:, a * HALF : (a + 1) * HALF],
                 op,
             )
 
@@ -271,7 +316,7 @@ def tile_picked_wpna_silu_l_kernel(
             quantise(0, v0, n)
             c0 = v0
             for b, width in parts:
-                total = bank(b, [P, width], "total")
+                total = bank(SUM_BANKS[b], [P, width], "total")
                 multiply(total[:], c0, width)
                 if width > P:
                     nc.scalar.copy(out=result[:, c0 : c0 + width], in_=total[:])

@@ -184,10 +184,12 @@ def tile_picked_wpna_silu_l_kernel(
             acc = bank(b, [P, BANK], "second")
             project(1, acc[:], a * BANK, BANK)
             activate(1, acc[:], a * BANK, BANK)
-        later = bank(2, [P, 2, 2, BANK], "later")
-        for t in (2, 3):
-            for a in range(2):
-                project(t, later[:, t - 2, a, :], a * BANK, BANK)
+        filler = bank(1, [P, CHUNK], "filler")
+        project(2, filler[:], 0, CHUNK)
+        later = bank(2, [P, 4, BANK], "later")
+        parts = ((2, CHUNK, CHUNK), (2, BANK, BANK), (3, 0, BANK), (3, BANK, BANK))
+        for i, (t, c0, width) in enumerate(parts):
+            project(t, later[:, i, :width], c0, width)
         for d in range(2):
             gather(True, d, 0, 0, T)
             gather(False, d, 1, 0, T)
@@ -202,9 +204,9 @@ def tile_picked_wpna_silu_l_kernel(
         third = shared[:, : 2 * T].rearrange("p (u v) e -> p u v e", u=2)
         early[0, 1] = shared[:, T + HALF :]
         round_on_gpsimd(third[:, 0], g[2, 0][:])
-        for t in (2, 3):
-            for a in range(2):
-                activate(t, later[:, t - 2, a, :], a * BANK, BANK)
+        activate(2, filler[:], 0, CHUNK)
+        for i, (t, c0, width) in enumerate(parts):
+            activate(t, later[:, i, :width], c0, width)
         gather(False, 0, 2, 0, T)
         gather(True, 0, 3, 0, T)
         gather(False, 1, 2, 0, T)

from contextlib import ExitStack

import concourse.mybir as mybir
from concourse.masks import make_identity

K, T, H, N = 512, 1024, 512, 128
D = 3
FLOPS = 2 * K * H * T + D * 2 * H * N * T

F32 = mybir.dt.float32
BF16 = mybir.dt.bfloat16
I32 = mybir.dt.int32
U32 = mybir.dt.uint32
U16 = mybir.dt.uint16
U8 = mybir.dt.uint8
FP8X4 = mybir.dt.float8_e4m3fn_x4
FP4X4 = mybir.dt.float4_e2m1fn_x4
ACT = mybir.ActivationFunctionType
ALU = mybir.AluOpType

P = 128
PACK = 4
BANK = 512
CHUNK = 256
HALF = 512
SPARE = 352
HANDED = 256
SUM_BANKS = (0, 1, 6, 7, 2, 3, 4, 5)
PIECES = ((0, HALF), (HALF, 3 * P), (T - P, P))


def tile_picked_wpna_silu_l_kernel(
    tc, x_words, x_scales, w1, w2_words, w2_scales, w3_words, w3_scales, w4_words, w4_scales, pos1, pos2, pos3, out
):
    nc = tc.nc
    with ExitStack() as ctx:
        keep = ctx.enter_context(tc.tile_pool(name="keep", bufs=1))
        psum = ctx.enter_context(tc.psum_pool(name="psum", bufs=1))

        x_plane = keep.tile([P, CHUNK], U8, name="x_plane", align_bytes=64)
        w_plane = keep.tile([P, D * N], U8, name="w_plane", align_bytes=64)
        nc.vector.memset(x_plane[:].bitcast(I32), 0)
        nc.vector.memset(w_plane[:].bitcast(I32), 0)

        w1_rows = w1.rearrange("(p j) c -> p j c", j=PACK)
        w1_raw = keep.tile([P, PACK, H], F32, name="w1_raw")
        for j0, j1 in ((0, 3), (3, 4)):
            nc.sync.dma_start(out=w1_raw[:, j0:j1, :], in_=w1_rows[:, j0:j1, :])
        for q in range(4):
            nc.sync.dma_start(
                out=x_plane[32 * q : 32 * q + 16, :].bitcast(I32),
                in_=x_scales[0][4 * q : 4 * q + 4, :].bitcast(I32).rearrange("r (c n) -> c r n", c=T // CHUNK),
            )
        x_flat = x_words[0].rearrange("p n r -> p (n r)")
        x_codes = []
        for a in range(T // BANK):
            codes = keep.tile([P, BANK], U32, name="x_codes", tag="x_codes%d" % a, align_bytes=64)
            nc.sync.dma_start(
                out=codes[:].bitcast(I32), in_=x_flat[:, PACK * BANK * a : PACK * BANK * (a + 1)].bitcast(I32)
            )
            x_codes.append(codes)
        lists = []
        for d, pos in enumerate((pos1, pos2, pos3)):
            offsets = keep.tile([P, T // 16], U16, name="offsets%d" % d)
            nc.sync.dma_start(offsets[:], pos)
            lists.append(offsets)
        w_codes = []
        for s, (words, scales) in enumerate(((w2_words, w2_scales), (w3_words, w3_scales), (w4_words, w4_scales))):
            codes = keep.tile([P, 2 * N], U8, name="w_codes%d" % s, align_bytes=64)
            nc.sync.dma_start(out=codes[:].bitcast(I32), in_=words[0].bitcast(I32))
            w_codes.append(codes)
            for q in range(4):
                nc.sync.dma_start(
                    out=w_plane[32 * q : 32 * q + 4, s * N : (s + 1) * N].bitcast(I32),
                    in_=scales[0][4 * q : 4 * q + 4, :].bitcast(I32),
                )

        def bank(b, shape, name):
            return psum.tile(shape, F32, name=name, tag="%s%d" % (name, b), offset=b * BANK * 4)

        h = [keep.tile([P, T + SPARE], F32, name="h%d" % t, align_bytes=64) for t in range(PACK)]
        for t in range(PACK):
            nc.gpsimd.memset(h[t][:, T:], 0.0)

        ident = keep.tile([P, P], F32, name="ident")
        make_identity(nc, ident[:])

        warm = keep.tile([P, 1], F32, name="warm")
        nc.scalar.activation(warm[:], h[0][:, T : T + 1], ACT.Silu)
        w1_first = keep.tile([P, P, PACK], BF16, name="w1_first", tag="w1_bf", align_bytes=64)
        w1_mid = keep.tile([P, P, PACK], BF16, name="w1_mid", align_bytes=64)
        w1_last = keep.tile([P, 2, P, PACK], BF16, name="w1_last", tag="w1_bf", align_bytes=64)
        dealt = w1_raw[:].rearrange("p j (m t) -> p m j t", t=PACK)
        for j0, j1 in ((0, 3), (3, 4)):
            nc.vector.tensor_copy(out=w1_first[:, :, j0:j1], in_=dealt[:, :, j0:j1, 0])
        first_codes = keep.tile([P, P], U32, name="first_codes", align_bytes=64)
        w1_planes = keep.tile([P, PACK * P], U8, name="w1_planes", tag="w1_planes", align_bytes=64)
        nc.vector.quantize_mx(
            out=first_codes[:].bitcast(FP8X4), scales=w1_planes[:, :P], in_=w1_first[:].rearrange("p m j -> p (m j)")
        )
        nc.scalar.copy(out=w1_mid[:], in_=dealt[:, :, :, 1])
        nc.vector.tensor_copy(out=w1_last[:].rearrange("p t m j -> p m j t"), in_=dealt[:, :, :, 2:4])
        rest_codes = keep.tile([P, (PACK - 1) * P], U32, name="rest_codes", align_bytes=64)
        mid = w1_mid[:].rearrange("p m j -> p (m j)")

        def quantise_rest():
            for a, b, flat_in in ((0, 1, mid), (1, 3, w1_last[:].rearrange("p t m j -> p (t m j)"))):
                nc.vector.quantize_mx(
                    out=rest_codes[:, a * P : b * P].bitcast(FP8X4),
                    scales=w1_planes[:, (a + 1) * P : (b + 1) * P],
                    in_=flat_in,
                )

        def project(t, acc, c0, width):
            w1_codes = first_codes[:] if t == 0 else rest_codes[:, (t - 1) * P : t * P]
            for c in range(c0 // CHUNK, (c0 + width) // CHUNK):
                nc.tensor.matmul_mx(
                    out=acc[:, c * CHUNK - c0 : (c + 1) * CHUNK - c0],
                    lhsT=w1_codes.bitcast(FP8X4),
                    lhsT_scale=w1_planes[:, t * P : (t + 1) * P],
                    rhs=x_codes[c // 2][:, c % 2 * CHUNK : (c % 2 + 1) * CHUNK].bitcast(FP8X4),
                    rhs_scale=x_plane[4 * c :, :],
                    start=True,
                    stop=True,
                )

        def activate(t, acc, c0, width):
            nc.scalar.activation(h[t][:, c0 : c0 + width], acc, ACT.Silu)

        g = {}
        for d, u in ((0, 0), (1, 0), (2, 0), (0, 1), (1, 1)):
            g[d, u] = keep.tile([P, 2, T], F32, name="g", tag="g%d%d" % (d, u), align_bytes=64)
        late = [keep.tile([P, 2, HALF], F32, name="late%d" % a, align_bytes=64) for a in range(2)]
        sums = {}
        added = [0] * 8

        def place(d, t, v0, n):
            u, e = divmod(t, 2)
            return g[d, u][:, e, v0 : v0 + n] if (d, u) in g else late[v0 // HALF][:, e, :]

        def gather(on_vector, d, t, v0, n):
            into = place(d, t, v0, n)
            picked = h[t][:].indirect(lists[d][:, v0 // 16 : (v0 + n) // 16])
            if on_vector:
                nc.vector.tensor_copy(into, picked)
            else:
                nc.scalar.activation(into, picked, ACT.Copy)

        def add_up(d, t, v0, n):
            u, e = divmod(t, 2)
            into = place(d, t, v0, n)
            for b in range(v0 // P, (v0 + n) // P):
                j = 4 * u + b // 2
                if j not in sums:
                    sums[j] = bank(SUM_BANKS[j], [P, 2, 2, P], "sums")
                nc.tensor.matmul(
                    sums[j][:, b % 2, e, :],
                    lhsT=into[:, b * P - v0 : (b + 1) * P - v0],
                    rhs=ident[:],
                    start=added[j] == 0,
                    stop=added[j] == 4 * D - 1,
                    is_transpose=True,
                )
                added[j] = added[j] + 1

        def round_on_gpsimd(into, pair):
            nc.gpsimd.tensor_scalar(into, pair.rearrange("p e v -> p v e"), 1.0, 0.0, ALU.mult, ALU.add)

        def round_on_vector(into, pair):
            nc.vector.tensor_copy(
                out=into.rearrange("p (c i) e -> p c e i", i=4), in_=pair.rearrange("p e (c i) -> p c e i", i=4)
            )

        early = {}
        for d, u in ((0, 0), (1, 0), (1, 1)):
            early[d, u] = keep.tile([P, T, 2], BF16, name="early%d%d" % (d, u), align_bytes=64)[:]

        for c, b in enumerate((0, 1, 2, 6)):
            acc = bank(b, [P, CHUNK], "first")
            project(0, acc[:], c * CHUNK, CHUNK)
            activate(0, acc[:], c * CHUNK, CHUNK)
        quantise_rest()
        for a, b in ((1, 7), (0, 2)):
            acc = bank(b, [P, BANK], "second")
            project(1, acc[:], a * BANK, BANK)
            activate(1, acc[:], a * BANK, BANK)
        filler = bank(1, [P, CHUNK], "filler")
        project(2, filler[:], 0, CHUNK)
        later = bank(2, [P, 4, BANK], "later")
        parts = ((2, CHUNK, CHUNK), (2, BANK, BANK), (3, 0, BANK), (3, BANK, BANK))
        for i, (t, c0, width) in enumerate(parts):
            project(t, later[:, i, :width], c0, width)
        for d in range(2):
            gather(True, d, 0, 0, T)
            gather(False, d, 1, 0, T)
            add_up(d, 0, 0, T)
            add_up(d, 1, 0, T)
            round_on_gpsimd(early[d, 0], g[d, 0][:])
        gather(True, 2, 0, 0, T)
        gather(True, 2, 1, 0, T)
        add_up(2, 0, 0, T)
        add_up(2, 1, 0, T)
        shared = keep.tile([P, 2 * T + HALF, 2], BF16, name="shared", tag="g10", align_bytes=64)
        third = shared[:, : 2 * T].rearrange("p (u v) e -> p u v e", u=2)
        early[0, 1] = shared[:, T + HALF :]
        round_on_gpsimd(third[:, 0], g[2, 0][:])
        activate(2, filler[:], 0, CHUNK)
        for i, (t, c0, width) in enumerate(parts):
            activate(t, later[:, i, :width], c0, width)
        gather(False, 0, 2, 0, T)
        gather(True, 0, 3, 0, T)
        gather(False, 1, 2, 0, T)
        gather(True, 1, 3, 0, HANDED)
        gather(False, 1, 3, HANDED, T - HANDED)
        for a in range(2):
            for t in (2, 3):
                gather(False, 2, t, a * HALF, HALF)
        for d in range(2):
            for t in (2, 3):
                add_up(d, t, 0, T)
        for a in range(2):
            for t in (2, 3):
                add_up(2, t, a * HALF, HALF)

        hi = keep.tile([P, 2, T, 2], BF16, name="hi", align_bytes=64)
        lo = keep.tile([P, 2, T, 2], BF16, name="lo", align_bytes=64)

        def first_round(into, op, u, v0=0, n=T):
            cols = slice(v0, v0 + n)
            nc.vector.tensor_tensor(into[:, u, cols], early[0, u][:, cols], early[1, u][:, cols], op)

        def round_third(a):
            round_on_vector(third[:, 1, a * HALF : (a + 1) * HALF], late[a][:])

        round_on_vector(early[0, 1], g[0, 1][:])
        first_round(hi, ALU.max, 0)
        first_round(lo, ALU.min, 0, 0, HALF)
        round_on_vector(early[1, 1], g[1, 1][:])
        first_round(lo, ALU.min, 0, HALF, HALF)
        first_round(hi, ALU.max, 1)
        round_third(0)
        first_round(lo, ALU.min, 1)

        backs = {}

        def turn(u, j):
            turned = keep.tile([P, 2, P, 2], BF16, name="turned", tag="turned%d%d" % (u, j), align_bytes=64)
            summed = sums[4 * u + j][:].rearrange("v b e p -> v b p e")
            nc.scalar.activation(turned[:], summed, ACT.Copy, scale=1.0 / D)
            pairs = turned[:].rearrange("v b p e -> v b (p e)").bitcast(F32)
            if u == 0:
                backs[j] = bank(SUM_BANKS[j], [P, 2, 2, P], "back")
            for b in range(2):
                nc.tensor.transpose(backs[j][:, b, u, :], pairs[:, b, :], ident[:])

        means = {v0: keep.tile([P, n * PACK], BF16, name="means%d" % v0, align_bytes=64) for v0, n in PIECES}
        ends = [keep.tile([P, 2 * HALF * PACK], BF16, name="ends%d" % a, align_bytes=64) for a in range(2)]
        z_codes = [keep.tile([P, D * HALF], U32, name="z_codes%d" % a, align_bytes=64) for a in range(2)]
        z_plane = [keep.tile([P, D * HALF], U8, name="z_plane%d" % a, align_bytes=64) for a in range(2)]

        def lay_mean(b0, n):
            j, b = divmod(b0, 2)
            v0 = max(start for start, width in PIECES if start <= b0 * P)
            words = means[v0][:, (b0 * P - v0) * PACK : ((b0 + n) * P - v0) * PACK].bitcast(F32)
            nc.scalar.copy(
                out=words.rearrange("p (b v u) -> p b v u", b=n, u=2),
                in_=backs[j][:, b : b + n].rearrange("p b u v -> p b v u"),
            )

        def compare(s, a):
            pair, op = (hi, ALU.max) if s == 1 else (lo, ALU.min)
            nc.vector.tensor_tensor(
                ends[a][:, (s - 1) * HALF * PACK : s * HALF * PACK].rearrange("p (v u e) -> p v u e", u=2, e=2),
                pair[:].rearrange("p u v e -> p v u e")[:, a * HALF : (a + 1) * HALF],
                third.rearrange("p u v e -> p v u e")[:, a * HALF : (a + 1) * HALF],
                op,
            )

        def quantise(s, v0, n):
            a, w0 = divmod(v0, HALF)
            c0 = s * HALF + w0
            values = means[v0][:] if s == 0 else ends[a][:, (c0 - HALF) * PACK : (c0 - HALF + n) * PACK]
            nc.vector.quantize_mx(
                out=z_codes[a][:, c0 : c0 + n].bitcast(FP8X4), scales=z_plane[a][:, c0 : c0 + n], in_=values
            )

        def multiply(acc, v0, n):
            a, w0 = divmod(v0, HALF)
            for s in (1, 2, 0):
                c0 = s * HALF + w0
                nc.tensor.matmul_mx(
                    out=acc,
                    lhsT=w_codes[s][:].bitcast(FP4X4),
                    lhsT_scale=w_plane[:, s * N : (s + 1) * N],
                    rhs=z_codes[a][:, c0 : c0 + n].bitcast(FP8X4),
                    rhs_scale=z_plane[a][:, c0 : c0 + n],
                    start=s == 1,
                    stop=s == 0,
                )

        result = keep.tile([P, T], F32, name="result", align_bytes=64)
        for u in range(2):
            for j in range(4):
                turn(u, j)
        for b0, n in ((0, 2), (2, 2), (4, 2), (6, 1), (7, 1)):
            lay_mean(b0, n)
        compare(1, 0)
        compare(2, 0)
        quantise(1, 0, HALF)
        round_third(1)
        quantise(2, 0, HALF)
        compare(1, 1)
        compare(2, 1)
        quantise(1, HALF, HALF)
        for v0, n, parts in ((0, HALF, ((7, HALF),)), (HALF, 3 * P, ((5, 2 * P), (6, P))), (T - P, P, ((4, P),))):
            if v0 == HALF:
                quantise(2, HALF, HALF)
            quantise(0, v0, n)
            c0 = v0
            for b, width in parts:
                total = bank(SUM_BANKS[b], [P, width], "total")
                multiply(total[:], c0, width)
                if width > P:
                    nc.scalar.copy(out=result[:, c0 : c0 + width], in_=total[:])
                else:
                    nc.vector.tensor_copy(out=result[:, c0 : c0 + width], in_=total[:])
                c0 = c0 + width
            nc.sync.dma_start(out=out[:, v0 : v0 + n], in_=result[:, v0 : v0 + n])
